import numpy as np, ml_dtypes
CORES = [78,86,94,102,110,118]
N = 6
BF = ml_dtypes.bfloat16
def gentries(a):
    return np.ascontiguousarray(a.reshape(8, 16, -1).transpose(0, 2, 1)).reshape(8, -1)
def gtable(e):
    e = np.asarray(e); return np.ascontiguousarray(e.reshape(8, -1, 16).transpose(0, 2, 1)).reshape(128, -1).astype(np.int32)
V, K, CAP, S, RO, TH = 3072, 1024, 384, 3, 3, 10
def trees(rng, x, span):
    n = N * 8; v = np.arange(V); back = 1 + (span[..., None] * rng.random((N, 8, V)) ** 2).astype(np.int64)
    p = np.where((rng.random((N, 8, V)) < 0.003) | (v == 0), v, np.maximum(v - back, 0))
    ids = np.argsort(rng.random((N, 8, V)), axis=-1); inv = np.argsort(ids, axis=-1)
    xo = np.ascontiguousarray(np.take_along_axis(x, ids[:, :, None, :], 3).reshape(n, 16, V).transpose(2, 0, 1)).astype(np.int16)
    po = np.ascontiguousarray(p.reshape(n, V).T); a = np.arange(n)
    jo = np.zeros((V, n), np.int64); lo = np.zeros((V, n), np.int64); mo = np.zeros((V, n, 16), np.int16)
    for i in range(V):
        pi = po[i]; top = pi == i; ji = jo[pi, a]; lp = lo[pi, a]; lj = lo[ji, a]; same = lp == lj
        jo[i] = np.where(top, i, np.where(same, jo[ji, a], pi)); lo[i] = np.where(top, 0, np.where(same, lp + lj + 1, 1))
        mo[i] = np.where(top[:, None], 0, np.where(same[:, None], np.maximum(xo[i], np.maximum(mo[pi, a], mo[ji, a])), xo[i]))
    j = jo.T.reshape(N, 8, V); l = lo.T.reshape(N, 8, V); m = mo.transpose(1, 2, 0).reshape(N, 8, 16, V)
    go = lambda e: np.take_along_axis(e, inv, 2)
    return np.take_along_axis(m, inv[:, :, None, :], 3).astype(np.int64), np.take_along_axis(ids, go(p), 2), np.take_along_axis(ids, go(j), 2), go(l)
def spans(rng):
    return np.stack([rng.permutation(np.array([0, 3, 8, 30, 100, 400, 1500, V])) for _ in range(N)])
def asks(rng, top):
    a = (top[..., None] * rng.random((N, 8, K)))[:, :, None, :]
    return np.minimum((256 * (a + (1 - a) * rng.random((N, 8, 16, K)))).astype(np.int64), 255)
def tops(rng):
    return np.stack([rng.permutation(np.array([0.3, 0.5, 0.6, 0.7, 0.8, 0.9, 0.95, 0.99])) for _ in range(N)])
def pack(x, m, par, jump, ln, q, u, w):
    b = lambda e: np.ascontiguousarray(e.reshape(N, 128, -1)).astype(np.float32).astype(BF)
    return {"x": b(x), "m": b(m), "par": par.astype(np.int32), "jump": jump.astype(np.int32), "ln": ln.astype(np.int32), "q": b(q),
            "u0": np.stack([gtable(e) for e in u]), "w": np.ascontiguousarray(w.reshape(N, 128, 1)).astype(np.int32)}
def setup_inputs(rng):
    x = rng.integers(0, 256, (N, 8, 16, V)); m, par, jump, ln = trees(rng, x, spans(rng))
    return pack(x, m, par, jump, ln, asks(rng, tops(rng)), rng.integers(0, V, (N, 8, K)), rng.integers(0, 256, (N, 8, 16)))
def setup_inputs_room(rng):
    x = rng.integers(0, 255, (N, 8, 16, V)); m, par, jump, ln = trees(rng, x, spans(rng))
    n = rng.choice(np.array([0, 1, CAP - 1, CAP, CAP + 1, K]), (N, 8))
    n[0] = (CAP, CAP + 1, K, CAP - 1, 1, 0, CAP, CAP + 1); n[1] = (CAP, K, CAP - 1, K, K, CAP, 1, 0)
    fail = np.argsort(rng.random((N, 8, K)), axis=-1) < n[..., None]
    place = np.argsort(rng.random((N, 8, 16, K)), axis=2)
    q = np.where(place < np.where(fail, TH - 1, TH)[:, :, None, :], 0, 255)
    return pack(x, m, par, jump, ln, q, rng.integers(0, V, (N, 8, K)), rng.integers(0, 256, (N, 8, 16)))
def setup_inputs_votes(rng):
    v = np.stack([rng.permutation(np.array([0, 1, 63, 100, 127, 128, 200, 254])) for _ in range(N)])[:, :, None, None]
    x = v + rng.integers(0, 2, (N, 8, 16, V)); m, par, jump, ln = trees(rng, x, spans(rng))
    z = rng.random((N, 8, 16, K)); q = np.minimum(v + (z > 0.3) + (z > 0.8), 255)
    w = np.where(v[..., 0] == 254, rng.integers(250, 256, (N, 8, 16)), rng.integers(0, 256, (N, 8, 16)))
    return pack(x, m, par, jump, ln, q, rng.integers(0, V, (N, 8, K)), w)
def setup_inputs_free(rng):
    x = rng.integers(0, 256, (N, 8, 16, V)); m = (rng.integers(0, 256, (N, 8, 16, V)) * rng.random((N, 8, 1, V))).astype(np.int64)
    m[:, ::2] = rng.integers(0, 256, (N, 4, 16, V)); v = np.arange(V)
    par = rng.integers(0, V, (N, 8, V)); jump = rng.integers(0, V, (N, 8, V)); ln = rng.choice(np.array([0, 1, 2, V - 1]), (N, 8, V))
    par[:, 1] = rng.choice(np.array([0, V - 1]), (N, V)); jump[:, 1] = rng.choice(np.array([0, V - 1]), (N, V))
    par[:, 2] = v; ln[:, 3] = V - 1; jump[:, 4] = par[:, 4]; jump[:, 5] = v; par[:, 6] = (v + 1) % V
    ln[:, 6] = V - 1 - rng.integers(0, 4, (N, V)); ln[:, 7] = 1000 + rng.integers(0, 4, (N, V))
    ln[:, 0] = rng.integers(0, 256, (N, 1)) + rng.choice(np.array([0, 256, 512, 1024, 2048]), (N, V))
    l = rng.integers(1024, V // 2, (N, 1)); l[0] = V // 2 - 1; l[1] = 300 + rng.integers(0, 8); l[2] = 1024
    ln[:, 4] = np.where(rng.random((N, V)) < 0.5, l, 2 * l + 1)
    return pack(x, m, par, jump, ln, asks(rng, tops(rng)), rng.integers(0, V, (N, 8, K)), rng.integers(0, 256, (N, 8, 16)))
def setup_inputs_alike(rng):
    x = rng.integers(0, 256, (N, 8, 16, V)); s = spans(rng); s[:, 2] = 0; m, par, jump, ln = trees(rng, x, s)
    par[:, 3] = np.arange(V); jump[:, 3] = np.arange(V); ln[:, 3] = 0; m[:, 3] = 0
    c = rng.integers(0, V, (N, 8, 4)); c[:, 0] = (0, V - 1, 0, V - 1); w = rng.integers(0, 256, (N, 8, 16)); w[:, 1] = 0
    u = np.take_along_axis(c, rng.integers(0, 4, (N, 8, K)), 2)
    q = np.take_along_axis(asks(rng, tops(rng)), rng.integers(0, 4, (N, 8, 1, K)), 3)
    return pack(x, m, par, jump, ln, q, u, w)
def setup_inputs_spread(rng):
    x = (np.exp2(8 * rng.random((N, 8, 1, V))) * rng.random((N, 8, 16, V))).astype(np.int64); m, par, jump, ln = trees(rng, x, spans(rng))
    q = (np.exp2(8 * rng.random((N, 8, 1, K))) * rng.random((N, 8, 16, K))).astype(np.int64)
    u = (V * rng.random((N, 8, K)) ** 3).astype(np.int64); w = np.exp2(8 * rng.random((N, 8, 16))).astype(np.int64)
    return pack(x, m, par, jump, ln, q, np.minimum(u, V - 1), np.minimum(w, 255))
def check_inputs(d):
    bad = []
    for k in ("x", "m", "q"):
        a = np.asarray(d[k]).astype(np.float32)
        if not np.all((a >= 0) & (a <= 255) & (a == np.floor(a))): bad.append("whole numbers from 0 to 255 in " + k)
    for k, hi in (("par", V - 1), ("jump", V - 1), ("ln", V - 1), ("u0", V - 1), ("w", 255)):
        if np.min(d[k]) < 0 or np.max(d[k]) > hi: bad.append("range of " + k)
    return bad
def wpick(e, i):
    return np.take_along_axis(e, i[:, :, None, :], 3)
def npick(e, i):
    return np.take_along_axis(e, i, 2)
def votes(e, ask):
    return np.sum((e >= ask).astype(np.int64), axis=2)
def reference(x, m, par, jump, ln, q, u0, w):
    W = V + RO * K
    X = np.zeros((N, 8, 16, W), np.int64); Y = np.zeros((N, 8, 16, W), np.int64); P = np.zeros((N, 8, W), np.int64); J = np.zeros((N, 8, W), np.int64); L = np.zeros((N, 8, W), np.int64)
    X[..., :V] = x.astype(np.float32).reshape(N, 8, 16, V); Y[..., :V] = m.astype(np.float32).reshape(N, 8, 16, V)
    P[..., :V] = par; J[..., :V] = jump; L[..., :V] = ln
    ask = q.astype(np.float32).astype(np.int64).reshape(N, 8, 16, K); wt = w.astype(np.int64).reshape(N, 8, 16, 1)
    u = np.stack([gentries(a) for a in u0]).astype(np.int64)
    for t in range(RO):
        for s in range(S):
            rest = votes(wpick(X, u), ask) >= TH; far = votes(wpick(Y, u), ask) < TH
            u = np.where(rest, u, np.where(far, npick(J, u), npick(P, u)))
        j = npick(J, u); lp = npick(L, u); lj = npick(L, j); same = lp == lj; o = V + K * t
        X[..., o:o + K] = ask; P[..., o:o + K] = u
        J[..., o:o + K] = np.where(same, npick(J, j), u); L[..., o:o + K] = np.where(same, lp + lj + 1, 1)
        Y[..., o:o + K] = np.where(same[:, :, None, :], np.maximum(ask, np.maximum(wpick(Y, u), wpick(Y, j))), ask)
        if t < RO - 1:
            xu = wpick(X, u); fail = votes(xu, ask) < TH
            before = np.add.accumulate(fail.astype(np.int64), axis=2) - fail
            come = np.zeros((N, 8, 16, CAP), np.int64); got = np.zeros((N, 8, 1), np.int64)
            for r in range(N):
                for g in range(8):
                    c = np.flatnonzero(fail[r, g])[:CAP]; d = (r + 1) % N
                    come[d, g, :, :c.size] = ask[r, g][:, c]; got[d, g, 0] = c.size
            hit = fail & (before < got)
            ask = np.where(hit[:, :, None, :], wpick(come, np.minimum(before, CAP - 1)), (ask + xu + t) & 255)
            u = o + (np.sum(wt * ask, axis=2) & (K - 1))
    return {"ypar": P[..., V:].astype(np.float32), "yjump": J[..., V:].astype(np.float32), "ym": np.ascontiguousarray(Y[..., V:]).reshape(N, 128, RO * K).astype(np.float32).astype(BF)}

@@ -1,0 +1,448 @@
+from concourse.mybir import AluOpType as A, ActivationFunctionType as F
+
+V0, K, CAP, RO = 3072, 1024, 384, 3
+Z = 16
+CS = 16
+BIG = 8192.0
+BW = 144
+B_ONE, B_DH, B_SH, B_SI, B_J, B_LP, B_LN, B_W = range(8)
+W_I, W_NI, W_N128, W_ONE, W_NU, W_P, W_J, W_ID0, W_ID1 = range(9)
+
+bf, f32, i32, u16 = "bfloat16", "float32", "int32", "uint16"
+SCRATCH = {
+    "X": ("sbuf", [128, V0 + RO * K], bf), "M": ("sbuf", [128, Z + V0 + RO * K], bf), "PT": ("sbuf", [128, Z + V0 + RO * K], bf),
+    "Ci": ("sbuf", [128, 576], i32), "Cj": ("sbuf", [128, 1152], i32), "Cb": ("sbuf", [128, 1728], bf), "idt": ("sbuf", [128, 192], bf),
+    "u0i": ("sbuf", [128, 64], i32), "wi": ("sbuf", [128, 1], i32), "wf": ("sbuf", [128, 1], f32),
+    "pi": ("sbuf", [128, 1], i32), "pj": ("sbuf", [128, 1], i32), "pm": ("sbuf", [128, 1], f32), "pm192": ("sbuf", [128, 1], f32),
+    "Ct": ("sbuf", [128, 64], f32), "Cf": ("sbuf", [128, 64], f32),
+    "ou0": ("sbuf", [128, 64], u16), "ou1": ("sbuf", [128, 64], u16), "ou2": ("sbuf", [128, 64], u16), "op": ("sbuf", [128, 64], u16),
+    "oj": ("sbuf", [128, 64], u16), "opj": ("sbuf", [128, 128], u16), "opos": ("sbuf", [128, 64], u16), "oidx": ("sbuf", [128, 64], u16),
+    "cm": ("sbuf", [128, K], bf), "cx0": ("sbuf", [128, K], bf), "cx1": ("sbuf", [128, K], bf), "gx": ("sbuf", [128, K], bf),
+    "pg0": ("sbuf", [128, K], bf), "pg1": ("sbuf", [128, K], bf), "pgp": ("sbuf", [128, K], bf), "pgj": ("sbuf", [128, K], bf),
+    "pgz": ("sbuf", [128, K], bf), "ge": ("sbuf", [128, K], bf), "tm": ("sbuf", [128, K], bf),
+    "u0f": ("sbuf", [128, 64], f32), "su1": ("sbuf", [128, 128], f32), "su2": ("sbuf", [128, 128], f32), "sp": ("sbuf", [128, 320], f32),
+    "spos": ("sbuf", [128, 128], f32), "sidx": ("sbuf", [128, 128], f32),
+    "d0s": ("sbuf", [128, 128], bf), "d0f": ("sbuf", [128, 320], bf), "fb": ("sbuf", [128, 128], bf), "hb": ("sbuf", [128, 128], bf),
+    "one64": ("sbuf", [128, 64], bf), "na": ("sbuf", [128, 64], f32), "ad": ("sbuf", [128, 128], f32), "yy": ("sbuf", [128, 128], f32),
+    "h0": ("sbuf", [128, 64], i32), "h1": ("sbuf", [128, 64], i32), "Sc": ("sbuf", [128, 64], bf),
+    "send": ("sbuf", [128, 16 + 2 * K], bf), "tab0": ("sbuf", [128, 16 + 2 * K], bf), "tab1": ("sbuf", [128, 16 + 2 * K], bf),
+    "Bm": ("sbuf", [128, 8 * BW], bf), "Wm": ("sbuf", [128, 9 * 128 + 16], bf), "If": ("sbuf", [128, 256], f32),
+    "yo": ("sbuf", [128, K], f32),
+    "pw0": ("psum", [128, 1024], f32), "pw1": ("psum", [128, 1024], f32),
+    "pa": ("psum", [128, 512], f32), "pb": ("psum", [128, 512], f32), "pc": ("psum", [128, 512], f32), "pd": ("psum", [128, 512], f32),
+}
+NDMA = 40
+SEMAPHORES = ["sV", "sS", "sP", "sG", "arr0", "arr1", "sent0", "sent1"] + ["d%d" % k for k in range(NDMA)]
+BANKS = ("pw0a", "pw0b", "pw1a", "pw1b", "pa", "pb", "pc", "pd")
+
+
+def rank_program(g, core, T, topo):
+    rank = T.rank_of(core)
+    if rank is None:
+        return
+    nxt = T.cores[(rank + 1) % len(T.cores)]
+    Q = {"V": g.vector, "S": g.scalar, "P": g.tensor, "G": g, "Y": g.sync}
+    total = {}
+    known = {q: {} for q in Q}
+    clock = {}
+    lastw, readers = {}, {}
+    ndma = [0]
+
+    def need(q, ev):
+        s, c = ev[1], ev[2]
+        if known[q].get(s, 0) >= c:
+            return
+        Q[q].wait_ge(T.sem[s], c)
+        known[q][s] = c
+        for s2, c2 in clock.get((s, c), {}).items():
+            if known[q].get(s2, 0) < c2:
+                known[q][s2] = c2
+
+    def order(q, eng, r, w):
+        evs = []
+        for x in r:
+            if x in lastw:
+                evs.append(lastw[x])
+            if x in BANKS:
+                evs += [e for e in readers.get(x, []) if e[0] != eng]
+        for x in w:
+            if x in lastw and not (eng == "P" and lastw[x][0] == "P"):
+                evs.append(lastw[x])
+            evs += readers.get(x, [])
+        best = {}
+        for e in evs:
+            if best.get(e[1], (0, 0, 0))[2] < e[2]:
+                best[e[1]] = e
+        for e in sorted(best.values(), key=lambda e: -len(clock.get((e[1], e[2]), {}))):
+            need(q, e)
+
+    def note(ev, q, r, w):
+        clock[(ev[1], ev[2])] = dict(known[q])
+        for x in r:
+            readers.setdefault(x, []).append(ev)
+        for x in w:
+            lastw[x] = ev
+            readers[x] = []
+
+    def op(q, fn, r, w):
+        order(q, q, r, w)
+        s = "s" + q
+        total[s] = total.get(s, 0) + 1
+        fn().then_inc(T.sem[s], 1)
+        note((q, s, total[s]), q, r, w)
+
+    def dma(q, out, in_, r, w):
+        order(q, "D", r, w)
+        s = "d%d" % ndma[0]
+        ndma[0] += 1
+        total[s] = 16
+        Q[q].dma_start(out, in_).then_inc(T.sem[s], 16)
+        note(("D", s, 16), q, r, w)
+
+    vec, act, pe = g.vector, g.scalar, g.tensor
+
+    def Bi(k, i):
+        return T.Bm[:, k * BW + 15 - i:k * BW + 143 - i]
+
+    def Wk(k):
+        return T.Wm[:, k * 128:(k + 1) * 128]
+
+    def extract(out, k, src, r, w, start=True, stop=True, c0=0):
+        def fn():
+            for i in range(16):
+                ins = pe.matmul(out, Bi(k, i), src[:, c0 + i:c0 + K:16], start and i == 0, stop and i == 15)
+            return ins
+        op("P", fn, r + ["B%d" % k], w)
+
+    def mm(out, lhsT, rhs, start, stop, r, w):
+        op("P", lambda: pe.matmul(out, lhsT, rhs, start, stop), r, w)
+
+    def gS(out, win, off, r, w):
+        op("S", lambda: act.activation(out, win.indirect(off), F.Identity), r, w)
+
+    def gV(out, win, off, r, w):
+        op("V", lambda: vec.tensor_copy(out, win.indirect(off)), r, w)
+
+    def gT(out, win, off, in1, alu, r, w):
+        op("V", lambda: vec.tensor_tensor(out, win.indirect(off), in1, alu), r, w)
+
+    def sel(ap, pattern, cmp, fill, base, name):
+        op("G", lambda: g.affine_select(ap, ap, pattern, cmp, fill, base, 1), [name], [name])
+
+    for k, src in enumerate((T.par, T.jump, T.ln)):
+        dma("Y", T.Ci[:, 192 * k:192 * k + 192], src[:], [], ["Ci%d" % k])
+    dma("S", T.X[:, V0:V0 + K], T.q[:], [], ["X1"])
+    dma("S", T.M[:, Z:Z + V0], T.m[:], [], ["M0"])
+    dma("Y", T.u0i[:], T.u0[:], [], ["u0i"])
+    dma("Y", T.wi[:], T.w[:], [], ["wi"])
+    dma("S", T.X[:, 0:V0], T.x[:], [], ["X0"])
+
+    op("G", lambda: g.iota(T.pi[:], [[0, 1]], 0, 1), [], ["pi"])
+    op("G", lambda: g.iota(T.idt[:], [[64, 3], [0, 64]], 0, 0, allow_small_or_imprecise_dtypes=True), [], ["idt"])
+    op("G", lambda: g.iota(T.Cb[:, 1344:1536], [[0, 3], [1, 64]], 0, 0, allow_small_or_imprecise_dtypes=True), [], ["Cb7"])
+    op("G", lambda: g.iota(T.Cb[:, 1536:1728], [[0, 192]], 1, 0, allow_small_or_imprecise_dtypes=True), [], ["Cb8"])
+    ball = ["B%d" % k for k in range(8)]
+    wall = ["W%d" % k for k in range(10)]
+    op("V", lambda: vec.memset(T.Bm[:], 0.0), [], ball)
+    op("V", lambda: vec.tensor_scalar(T.pj[:], T.pi[:], 15, None, A.bitwise_and), ["pi"], ["pj"])
+    prow = ["PT0_%d" % f for f in range(11)]
+    op("V", lambda: vec.memset(T.PT[:, 0:Z + V0], 0.0), [], prow)
+    op("V", lambda: vec.tensor_scalar(T.pm192[:], T.pj[:], 192.0, None, A.mult), ["pj"], ["pm192"])
+    op("V", lambda: vec.memset(T.Wm[:], 0.0), [], wall)
+    op("V", lambda: vec.tensor_scalar(T.Cb[:, 1152:1344], T.idt[:], T.pm192[:], None, A.add), ["idt", "pm192"], ["Cb6"])
+
+    def row(q, f, blk):
+        dma(q, T.PT[f::16, Z:Z + V0], T.Cb[:, 192 * blk:192 * blk + 192], ["Cb%d" % blk], ["PT0_%d" % f])
+    row("Y", 10, 8)
+    row("Y", 7, 7)
+    row("Y", 6, 6)
+    for k, f in enumerate((0, 2, 8)):
+        ci = T.Ci[:, 192 * k:192 * k + 192]
+        op("V", lambda: vec.tensor_scalar(T.Cj[:, 384 * k:384 * k + 192], ci, 0xFFC0, None, A.bitwise_and), ["Ci%d" % k], ["Cja%d" % k])
+        op("V", lambda: vec.tensor_scalar(T.Cj[:, 384 * k + 192:384 * k + 384], ci, 63, None, A.bitwise_and), ["Ci%d" % k], ["Cjb%d" % k])
+        if k == 0:
+            op("V", lambda: vec.tensor_copy(T.ou0[:], T.u0i[:]), ["u0i"], ["ou0"])
+        op("V", lambda: vec.tensor_copy(T.Cb[:, 384 * k:384 * k + 384], T.Cj[:, 384 * k:384 * k + 384]),
+           ["Cja%d" % k, "Cjb%d" % k], ["Cb%d" % (2 * k), "Cb%d" % (2 * k + 1)])
+        row("Y", f, 2 * k)
+        row("S", f + 1, 2 * k + 1)
+    op("V", lambda: vec.memset(T.If[:], 0.0), [], ["If0", "If1"])
+    op("V", lambda: vec.memset(T.d0s[:], 0.0), [], ["d0s"])
+    op("V", lambda: vec.memset(T.d0f[:], 0.0), [], ["d0f1", "d0f2", "d0f3", "d0f4"])
+    op("V", lambda: vec.memset(T.fb[:], 0.0), [], ["fb"])
+    op("V", lambda: vec.memset(T.hb[:], 0.0), [], ["hb"])
+    op("V", lambda: vec.memset(T.one64[:], 1.0), [], ["one64"])
+    op("V", lambda: vec.memset(T.M[:, 0:Z], 0.0), [], ["Mz"])
+    op("V", lambda: vec.memset(T.send[:, 0:16 + CAP], 0.0), [], ["sendh", "sendw"])
+    op("V", lambda: vec.memset(T.tab0[:, 16 + CAP:16 + K], 0.0), [], ["gap0"])
+    op("V", lambda: vec.memset(T.tab1[:, 16 + CAP:16 + K], 0.0), [], ["gap1"])
+    op("V", lambda: vec.tensor_copy(T.u0f[:], T.u0i[:]), ["u0i"], ["u0f"])
+    op("V", lambda: vec.tensor_copy(T.pm[:], T.pj[:]), ["pj"], ["pm"])
+    op("V", lambda: vec.tensor_copy(T.wf[:], T.wi[:]), ["wi"], ["wf"])
+
+    fills = {B_ONE: [(16, 1.0), (0, 0.0)], B_DH: [(6, -0.5), (2, 0.5), (0, 0.0)], B_SH: [(6, 0.5), (0, 0.0)],
+             B_SI: [(8, -1.0), (6, 0.5), (0, 0.0)], B_J: [(6, 1.0), (2, 0.0)], B_LP: [(10, BIG), (8, 0.0)], B_LN: [(10, -BIG), (8, 0.0)]}
+
+    def bfill(ks):
+        for lvl in range(3):
+            for k in ks:
+                if lvl < len(fills[k]):
+                    top, val = fills[k][lvl]
+                    sel(T.Bm[:, k * BW + 15:k * BW + 143:16], [[-16, 8]], A.is_ge, val, -top, "B%d" % k)
+    bfill([B_ONE, B_DH, B_SH])
+    sel(Wk(W_I), [[-1, 128]], A.not_equal, 1.0, 0, "W%d" % W_I)
+    sel(Wk(W_NI), [[-1, 128]], A.not_equal, -1.0, 0, "W%d" % W_NI)
+    sel(T.If[:, 0:128], [[-1, 128]], A.not_equal, 1.0, 0, "If0")
+    sel(T.If[:, 128:256], [[-1, 128]], A.not_equal, -1.0, 0, "If1")
+    op("G", lambda: g.iota(T.Ct[:], [[16, 64]], K, 0, allow_small_or_imprecise_dtypes=True), [], ["Ct"])
+    bfill([B_SI, B_J, B_LP, B_LN])
+    sel(Wk(W_ONE), [[-16, 8], [0, 16]], A.is_ge, 1.0, -16, "W%d" % W_ONE)
+    sel(Wk(W_NU), [[-16, 8], [0, 16]], A.is_ge, -1.0, -16, "W%d" % W_NU)
+    sel(Wk(W_N128), [[-1, 128]], A.not_equal, -128.0, 0, "W%d" % W_N128)
+    sel(Wk(W_ONE), [[-16, 8], [0, 16]], A.is_ge, 0.0, 0, "W%d" % W_ONE)
+    sel(Wk(W_NU), [[-1, 128]], A.is_ge, 0.0, 0, "W%d" % W_NU)
+    ents = {W_P: [(6, 0, 1.0), (7, 1, 1.0), (6, 4, 1.0), (7, 5, 1.0), (10, 9, 1.0), (10, 10, 1.0)],
+            W_J: [(2, 2, 1.0), (3, 3, 1.0), (4, 2, 1.0), (5, 3, 1.0), (8, 8, 2.0), (9, 9, 2.0), (10, 4, -BIG), (10, 5, -BIG)],
+            W_ID0: [(6, 6, 1.0), (7, 7, 1.0), (10, 6, float(V0))], W_ID1: [(6, 6, 1.0), (7, 7, 1.0), (10, 6, float(V0 + K))]}
+    for lvl in range(8):
+        for k in ents:
+            if lvl < len(ents[k]):
+                f, f2, val = ents[k][lvl]
+                sel(T.Wm[:, k * 128 + f2:(k + 1) * 128:16], [[-16, 8]], A.not_equal, val, -f, "W%d" % k)
+    Wo = T.Wm[:, 1152:1168]
+    sel(T.Wm[:, 1152:1160], [[-16, 8]], A.is_ge, 1.0, -2, "W9")
+    sel(T.Wm[:, 1160:1168], [[-16, 8]], A.is_ge, 1.0, -6, "W9")
+    sel(T.Wm[:, 1152:1160], [[-16, 8]], A.is_ge, 0.0, 0, "W9")
+    sel(T.Wm[:, 1160:1168], [[-16, 8]], A.is_ge, 0.0, -2, "W9")
+    Ip, In = T.If[:, 0:128], T.If[:, 128:256]
+
+    def late_constants():
+        op("V", lambda: vec.tensor_scalar(T.Bm[:, B_W * BW + 15:B_W * BW + 143:16], T.Bm[:, 15:143:16], T.wf[:], None, A.mult),
+           ["B0", "wf"], ["B%d" % B_W])
+        op("V", lambda: vec.tensor_scalar(T.Cf[:], T.Ct[:], T.pm[:], None, A.add), ["Ct", "pm"], ["Cf"])
+
+    def emit_out_mm(t, h):
+        o = V0 + K * t
+        mm(T.pw1[0:16, 512 * h:512 * h + 512], Wo, T.PT[:, Z + o + 512 * h:Z + o + 512 * h + 512], True, True,
+           ["W9", "PT%d_%d" % (t + 1, h)], ["pw1" + "ab"[h]])
+
+    def emit_out_copy(t, hs):
+        a, b = 512 * hs[0], 512 * hs[-1] + 512
+        op("S", lambda: act.activation(T.yo[0:16, a:b], T.pw1[0:16, a:b], F.Identity), ["pw1" + "ab"[h] for h in hs], ["yo%d" % h for h in hs])
+
+    def emit_out_dma(t, q2="Y"):
+        dma("Y", T.ypar[:, K * t:K * t + K], T.yo[0:8, :], ["yo0", "yo1"], [])
+        dma(q2, T.yjump[:, K * t:K * t + K], T.yo[8:16, :], ["yo0", "yo1"], [])
+
+    CV = 64 - CS
+    LV = 16 * CV
+    rid, pid, _ = topo.addr(nxt)
+    mask = topo.mask(core, nxt)
+    neng = len(topo.engines(core, nxt))
+
+    for t in range(RO):
+        o = V0 + K * t
+        last = t == RO - 1
+        rX = ["X%d" % k for k in range(t + 1)]
+        rM = ["M0"] + ["M%d_%d" % (k, h) for k in range(1, t + 1) for h in (0, 1)]
+        rP = prow + ["PT%d_%d" % (k, h) for k in range(1, t + 1) for h in (0, 1)]
+        rq = ["X%d" % (t + 1)]
+        if t > 0:
+            rX = rX + ["X%db" % k for k in range(2, t + 1)]
+            rq = rq + ["X%db" % (t + 1)]
+        ask = T.X[:, o:o + K]
+        offs = [T.ou0, T.ou1, T.ou2]
+        scans = [T.su1, T.su2]
+        cx = [T.cx0, T.cx1]
+        pg = [T.pg0, T.pg1]
+
+        def wins(s):
+            a = o - K if (s == 0 and t > 0) else 0
+            return T.X[:, a:o], T.M[:, Z + a:Z + o], T.PT[:, Z + a:Z + o]
+
+        def votes_x(s, bank, bn):
+            extract(bank[:, 0:64], B_ONE, cx[s % 2], ["cx%da" % (s % 2), "cx%db" % (s % 2)], [bn])
+
+        def stays(s, bank, bn, split):
+            if split:
+                op("S", lambda: act.activation(T.na[:, 0:CV], bank[:, 0:CV], F.Relu, bias=-9.0), [bn], ["naa"])
+                op("S", lambda: act.activation(T.na[:, CV:64], bank[:, CV:64], F.Relu, bias=-2.0), [bn], ["nab"])
+            else:
+                op("S", lambda: act.activation(T.na[:], bank[:, 0:64], F.Relu, bias=-9.0), [bn], ["naa", "nab"])
+            op("S", lambda: act.activation(T.d0f[:, 4 - s::5], T.na[:], F.Relu, bias=1.0, scale=-1.0), ["naa", "nab"], ["d0f%d" % (4 - s)])
+
+        for s in (0, 1):
+            wx, wm, wp = wins(s)
+            on = "ou%d" % s
+            gS(pg[s][:], wp, offs[s][:], rP + [on], ["pg%d" % s])
+            gT(T.cm[:], wm, offs[s][:], ask, A.is_ge, rM + rq + [on], ["cm"])
+            if s == 1:
+                votes_x(0, T.pc, "pc")
+            if CS:
+                gS(T.gx[:, 0:K - LV], wx, offs[s][:, CV:64], rX + [on], ["gx"])
+            gT(cx[s][:, 0:LV], wx, offs[s][:, 0:CV], T.X[:, o:o + LV], A.is_ge, rX + rq + [on],
+               ["cx%da" % s] if CS else ["cx%da" % s, "cx%db" % s])
+            if s == 0 and t > 0:
+                op("V", lambda: vec.tensor_scalar(T.u0f[:], T.h1[:], float(o - K), None, A.add), ["h1"], ["u0f"])
+            if s == 0 and t == 0:
+                late_constants()
+            extract(T.pb[:, 0:64], B_ONE, T.cm, ["cm"], ["pb"])
+            op("S", lambda: act.activation(T.d0s[:, 1::2], T.pb[:, 0:64], F.Sign, bias=-9.5), ["pb"], ["d0s"])
+            extract(T.pa[:, 0:128:2], B_DH, pg[s], ["pg%d" % s], ["pa"])
+            extract(T.pa[:, 1:128:2], B_SH, pg[s], ["pg%d" % s], ["pa"])
+            if CS:
+                mm(T.pw0[:, 0:K - LV], Wk(W_I), T.gx[:, 0:K - LV], True, False, ["gx", "W%d" % W_I], ["pw0a"])
+                mm(T.pw0[:, 0:K - LV], Wk(W_NI), T.X[:, o + LV:o + K], False, True, rq + ["W%d" % W_NI], ["pw0a"])
+            if s == 1:
+                stays(0, T.pc, "pc", CS > 0)
+            if CS:
+                op("S", lambda: act.activation(cx[s][:, LV:K], T.pw0[:, 0:K - LV], F.Sign, bias=0.5), ["pw0a"], ["cx%db" % s])
+            sn = "su%d" % (s + 1)
+            op("V", lambda: vec.tensor_tensor_scan(scans[s][:], T.d0s[:], T.pa[:, 0:128], 0.0, A.mult, A.add), ["d0s", "pa"], [sn])
+            op("V", lambda: vec.tensor_copy(offs[s + 1][:], scans[s][:, 1::2]), [sn], ["ou%d" % (s + 1)])
+
+        wx, wm, wp = wins(2)
+        u1, u2 = T.su1[:, 1::2], T.su2[:, 1::2]
+        gS(pg[0][:], wp, T.ou2[:], rP + ["ou2"], ["pg0"])
+        gT(cx[0][:], wx, T.ou2[:], ask, A.is_ge, rX + rq + ["ou2"], ["cx0a", "cx0b"])
+        gT(T.cm[:], wm, T.ou2[:], ask, A.is_ge, rM + rq + ["ou2"], ["cm"])
+        votes_x(1, T.pc, "pc")
+        mm(T.pa[:, 2:320:5], Ip, u2, True, False, ["If0", "su2"], ["pa"])
+        mm(T.pa[:, 2:320:5], In, u1, False, True, ["If1", "su1"], ["pa"])
+        mm(T.pa[:, 3:320:5], Ip, u1, True, False, ["If0", "su1"], ["pa"])
+        mm(T.pa[:, 3:320:5], In, T.u0f[:], False, True, ["If1", "u0f"], ["pa"])
+        mm(T.pa[:, 4:320:5], Ip, T.u0f[:], True, True, ["If0", "u0f"], ["pa"])
+        if t > 0:
+            emit_out_mm(t - 1, 0)
+            emit_out_mm(t - 1, 1)
+        stays(1, T.pc, "pc", CS > 0)
+        votes_x(2, T.pd, "pd")
+        stays(2, T.pd, "pd", False)
+        extract(T.pa[:, 0:320:5], B_DH, pg[0], ["pg0"], ["pa"])
+        extract(T.pa[:, 1:320:5], B_SI, pg[0], ["pg0"], ["pa"])
+        if t > 0:
+            emit_out_copy(t - 1, (0, 1))
+            emit_out_dma(t - 1)
+        extract(T.pb[:, 0:64], B_ONE, T.cm, ["cm"], ["pb"])
+        op("S", lambda: act.activation(T.d0f[:, 1::5], T.pb[:, 0:64], F.Sign, bias=-9.5), ["pb"], ["d0f1"])
+        op("V", lambda: vec.tensor_tensor_scan(T.sp[:], T.d0f[:], T.pa[:, 0:320], 0.0, A.mult, A.add),
+           ["d0f1", "d0f2", "d0f3", "d0f4", "pa"], ["sp"])
+        op("V", lambda: vec.tensor_copy(T.op[:], T.sp[:, 4::5]), ["sp"], ["op"])
+        pf = T.sp[:, 4::5]
+        wz_m, wz_p = T.M[:, 0:Z + o], T.PT[:, 0:Z + o]
+
+        def pick_zero():
+            op("S", lambda: act.activation(T.ad[:, 0:64], T.pb[:, 0:64], F.Abs), ["pb"], ["ada"])
+            op("S", lambda: act.activation(T.ad[:, 64:128], T.pb[:, 0:64], F.Abs), ["pb"], ["adb"])
+
+        def pick_zero_v():
+            op("V", lambda: vec.tensor_tensor(T.yy[:], T.pa[:, 0:128], T.ad[:], A.subtract), ["pa", "ada", "adb"], ["yy"])
+            op("V", lambda: vec.tensor_scalar(T.opj[:], T.yy[:], float(Z), None, A.add), ["yy"], ["opj"])
+
+        if not last:
+            tab = T["tab%d" % t]
+            gT(cx[0][:], wx, T.op[:], ask, A.is_ge, rX + rq + ["op"], ["cx0a", "cx0b"])
+            gS(T.pgp[:], wp, T.op[:], rP + ["op"], ["pgp0", "pgp1"])
+            mm(T.pd[:, 1:128:2], Ip, T.Cf[:], True, True, ["If0", "Cf"], ["pd"])
+            mm(T.pd[:, 0:128:2], In, T.Cf[:], True, False, ["If1", "Cf"], ["pd"])
+            mm(T.pa[:, 0:64], Ip, pf, True, True, ["If0", "sp"], ["pa"])
+            for h in (0, 1):
+                mm(T.pw1[:, 512 * h:512 * h + 512], Wk(W_ID0 + t), T.PT[:, Z + 512 * h:Z + 512 * h + 512], True, False,
+                   prow + ["W%d" % (W_ID0 + t)], ["pw1" + "ab"[h]])
+            votes_x(0, T.pc, "pc")
+            op("V", lambda: vec.tensor_scalar(T.fb[:, 1::2], T.pc[:, 0:64], 9.5, None, A.is_lt), ["pc"], ["fb"])
+            extract(T.pa[:, 64:128], B_J, T.pgp, ["pgp0", "pgp1"], ["pa"])
+            gS(T.gx[:], wx, T.op[:], rX + ["op"], ["gx"])
+            op("V", lambda: vec.tensor_tensor_scan(T.Sc[:], T.one64[:], T.fb[:, 1::2], 0.0, A.mult, A.add), ["one64", "fb"], ["Sc"])
+            mm(T.pd[:, 0:128:2], Wk(W_ONE), T.Sc[:], False, False, ["Sc", "W%d" % W_ONE], ["pd"])
+            mm(T.pd[:, 0:128:2], Wk(W_NU), T.fb[:, 1::2], False, True, ["fb", "W%d" % W_NU], ["pd"])
+            mm(T.pc[:, 64:65], Wk(W_ONE), T.Sc[:, 63:64], True, True, ["Sc", "W%d" % W_ONE], ["pc"])
+            op("V", lambda: vec.tensor_copy(T.oj[:], T.pa[:, 64:128]), ["pa"], ["oj"])
+            op("V", lambda: vec.tensor_tensor_scan(T.spos[:], T.fb[:], T.pd[:, 0:128], 0.0, A.mult, A.add), ["fb", "pd"], ["spos"])
+            op("V", lambda: vec.tensor_scalar(T.send[:, 15:16], T.pc[:, 64:65], float(CAP), 192.0, A.min, A.subtract), ["pc"], ["sendh"])
+            op("V", lambda: vec.tensor_copy(T.opos[:], T.spos[:, 1::2]), ["spos"], ["opos"])
+            op("V", lambda: vec.tensor_copy(T.send[:, 16:16 + 2 * K].indirect(T.opos[:]), ask), rq + ["opos"], ["sendw"])
+            order("G", "D", ["sendh", "sendw"], [])
+            g.remote_dma(tab[:, 0:16 + CAP], T.send[:, 0:16 + CAP], T.sem["arr%d" % t], T.sem["sent%d" % t], pid, rid, mask)
+            total["sent%d" % t] = neng
+            total["arr%d" % t] = neng
+            note(("D", "sent%d" % t, neng), "G", ["sendh", "sendw"], [])
+            lastw["land%d" % t] = ("D", "arr%d" % t, neng)
+            extract(T.pb[:, 0:64], B_LP, T.pgp, ["pgp0", "pgp1"], ["pb"], stop=False)
+            gS(T.pgj[:], wp, T.oj[:], rP + ["oj"], ["pgj0", "pgj1"])
+            for h in (0, 1):
+                mm(T.pw1[:, 512 * h:512 * h + 512], Wk(W_P), T.pgp[:, 512 * h:512 * h + 512], False, False,
+                   ["pgp0", "pgp1", "W%d" % W_P], ["pw1" + "ab"[h]])
+            for h in (0, 1):
+                c = slice(512 * h, 512 * h + 512)
+                mm(T.pw0[:, c], Wk(W_I), T.gx[:, c], True, False, ["gx", "W%d" % W_I], ["pw0" + "ab"[h]])
+                mm(T.pw0[:, c], Wk(W_I), T.X[:, o + 512 * h:o + 512 * h + 512], False, True, rq, ["pw0" + "ab"[h]])
+            extract(T.pb[:, 0:64], B_LN, T.pgj, ["pgj0", "pgj1"], ["pb"], start=False)
+            op("S", lambda: act.activation(T.ge[:], T.pw0[:], F.Sign, bias=t - 255.5), ["pw0a", "pw0b"], ["ge"])
+            pick_zero()
+            for h in (0, 1):
+                c = slice(512 * h, 512 * h + 512)
+                mm(T.pw0[:, c], Wk(W_I), T.gx[:, c], True, False, ["gx"], ["pw0" + "ab"[h]])
+                mm(T.pw0[:, c], Wk(W_I), T.X[:, o + 512 * h:o + 512 * h + 512], False, False, rq, ["pw0" + "ab"[h]])
+                mm(T.pw0[:, c], Wk(W_N128), T.ge[:, c], False, True, ["ge", "W%d" % W_N128], ["pw0" + "ab"[h]])
+            op("S", lambda: act.activation(tab[:, 16 + K:16 + 2 * K], T.pw0[:], F.Identity, bias=t - 128.0), ["pw0a", "pw0b"], ["tabc%d" % t])
+            pick_zero_v()
+            gS(T.pgz[:], wz_p, T.opj[:, 64:128], rP + ["opj"], ["pgz0", "pgz1"])
+            gT(T.tm[:], wz_m, T.opj[:, 0:64], ask, A.max, rM + rq + ["Mz", "opj"], ["tm0", "tm1"])
+            gT(T.M[:, Z + o:Z + o + K], wz_m, T.opj[:, 64:128], T.tm[:], A.max, rM + ["Mz", "opj", "tm0", "tm1"],
+               ["M%d_0" % (t + 1), "M%d_1" % (t + 1)])
+            for h in (0, 1):
+                mm(T.pw1[:, 512 * h:512 * h + 512], Wk(W_J), T.pgz[:, 512 * h:512 * h + 512], False, True,
+                   ["pgz0", "pgz1", "W%d" % W_J], ["pw1" + "ab"[h]])
+            op("S", lambda: act.activation(T.PT[:, Z + o:Z + o + K], T.pw1[:], F.Relu), ["pw1a", "pw1b"], ["PT%d_0" % (t + 1), "PT%d_1" % (t + 1)])
+            dma("Y", T.ym[:, K * t:K * t + K], T.M[:, Z + o:Z + o + K], ["M%d_0" % (t + 1), "M%d_1" % (t + 1)], [])
+            op("V", lambda: vec.tensor_scalar(T.hb[:, 1::2], T.spos[:, 1::2], 192.0, tab[:, 15:16], A.subtract, A.is_lt),
+               ["spos", "land%d" % t], ["hb"])
+            op("V", lambda: vec.tensor_tensor_scan(T.sidx[:], T.hb[:], T.pd[:, 0:128], 0.0, A.mult, A.add), ["hb", "pd"], ["sidx"])
+            op("V", lambda: vec.tensor_copy(T.oidx[:], T.sidx[:, 1::2]), ["sidx"], ["oidx"])
+            rt = ["land%d" % t, "gap%d" % t, "tabc%d" % t, "oidx"]
+            gV(T.X[:, o + K:o + K + 512], tab[:, 16:16 + 2 * K], T.oidx[:, 0:32], rt, ["X%d" % (t + 2)])
+            gS(T.X[:, o + K + 512:o + 2 * K], tab[:, 16:16 + 2 * K], T.oidx[:, 32:64], rt, ["X%db" % (t + 2)])
+            extract(T.pc[:, 0:64], B_W, T.X, ["X%d" % (t + 2), "X%db" % (t + 2)], ["pc"], c0=o + K)
+            op("V", lambda: vec.tensor_copy(T.h0[:], T.pc[:, 0:64]), ["pc"], ["h0"])
+            op("V", lambda: vec.tensor_scalar(T.h1[:], T.h0[:], K - 1, None, A.bitwise_and), ["h0"], ["h1"])
+            op("V", lambda: vec.tensor_copy(T.ou0[:], T.h1[:]), ["h1"], ["ou0"])
+        else:
+            gS(T.pgp[:, 512:K], wp, T.op[:, 32:64], rP + ["op"], ["pgp1"])
+            gV(T.pgp[:, 0:512], wp, T.op[:, 0:32], rP + ["op"], ["pgp0"])
+            mm(T.pa[:, 0:64], Ip, pf, True, True, ["If0", "sp"], ["pa"])
+            extract(T.pa[:, 64:128], B_J, T.pgp, ["pgp0", "pgp1"], ["pa"])
+            op("V", lambda: vec.tensor_copy(T.oj[:], T.pa[:, 64:128]), ["pa"], ["oj"])
+            extract(T.pb[:, 0:64], B_LP, T.pgp, ["pgp0", "pgp1"], ["pb"], stop=False)
+            gS(T.pgj[:, 512:K], wp, T.oj[:, 32:64], rP + ["oj"], ["pgj1"])
+            gV(T.pgj[:, 0:512], wp, T.oj[:, 0:32], rP + ["oj"], ["pgj0"])
+            for h in (0, 1):
+                mm(T.pw0[:, 512 * h:512 * h + 512], Wk(W_P), T.pgp[:, 512 * h:512 * h + 512], True, False,
+                   ["pgp0", "pgp1", "W%d" % W_P], ["pw0" + "ab"[h]])
+            extract(T.pb[:, 0:64], B_LN, T.pgj, ["pgj0", "pgj1"], ["pb"], start=False)
+            pick_zero()
+            pick_zero_v()
+            for h in (0, 1):
+                c = slice(512 * h, 512 * h + 512)
+                gS(T.pgz[:, c], wz_p, T.opj[:, 64 + 32 * h:96 + 32 * h], rP + ["opj"], ["pgz%d" % h])
+                mm(T.pw0[:, c], Wk(W_J), T.pgz[:, c], False, True, ["pgz%d" % h, "W%d" % W_J], ["pw0" + "ab"[h]])
+            for h in (0, 1):
+                c = slice(512 * h, 512 * h + 512)
+                a = Z + o + 512 * h
+                gT(T.tm[:, c], wz_m, T.opj[:, 32 * h:32 * h + 32], T.X[:, o + 512 * h:o + 512 * h + 512], A.max,
+                   rM + rq + ["Mz", "opj"], ["tm%d" % h])
+                gT(T.M[:, a:a + 512], wz_m, T.opj[:, 64 + 32 * h:96 + 32 * h], T.tm[:, c], A.max,
+                   rM + ["Mz", "opj", "tm%d" % h], ["M%d_%d" % (t + 1, h)])
+                dma("Y", T.ym[:, K * t + 512 * h:K * t + 512 * h + 512], T.M[:, a:a + 512], ["M%d_%d" % (t + 1, h)], [])
+            for h in (0, 1):
+                a = Z + o + 512 * h
+                op("S", lambda: act.activation(T.PT[:, a:a + 512], T.pw0[:, 512 * h:512 * h + 512], F.Relu),
+                   ["pw0" + "ab"[h]], ["PT%d_%d" % (t + 1, h)])
+                emit_out_mm(t, h)
+            emit_out_copy(t, (0,))
+            emit_out_copy(t, (1,))
+            dma("S", T.ypar[:, K * t:K * t + K], T.yo[0:8, :], ["yo0", "yo1"], [])
+            dma("S", T.yjump[:, K * t:K * t + K], T.yo[8:16, :], ["yo0", "yo1"], [])
+
+    for s in total:
+        g.wait_ge(T.sem[s], total[s])

@@ -3,6 +3,7 @@ from concourse.mybir import AluOpType as A, ActivationFunctionType as F
 V0, K, CAP, RO = 3072, 1024, 384, 3
 Z = 16
 CS = 16
+SC0 = 16
 BIG = 8192.0
 BW = 144
 B_ONE, B_DH, B_SH, B_SI, B_J, B_LP, B_LN, B_W = range(8)
@@ -11,18 +12,22 @@ W_I, W_NI, W_N128, W_ONE, W_NU, W_P, W_J, W_ID0, W_ID1 = range(9)
 bf, f32, i32, u16 = "bfloat16", "float32", "int32", "uint16"
 SCRATCH = {
     "X": ("sbuf", [128, V0 + RO * K], bf), "M": ("sbuf", [128, Z + V0 + RO * K], bf), "PT": ("sbuf", [128, Z + V0 + RO * K], bf),
-    "Ci": ("sbuf", [128, 576], i32), "Cj": ("sbuf", [128, 1152], i32), "Cb": ("sbuf", [128, 1728], bf), "idt": ("sbuf", [128, 192], bf),
+    "PA": ("sbuf", [128, V0], bf),
+    "Ci": ("sbuf", [128, 576], i32), "Cb": ("sbuf", [128, 1728], bf), "idt": ("sbuf", [128, 192], bf),
     "u0i": ("sbuf", [128, 64], i32), "wi": ("sbuf", [128, 1], i32), "wf": ("sbuf", [128, 1], f32),
     "pi": ("sbuf", [128, 1], i32), "pj": ("sbuf", [128, 1], i32), "pm": ("sbuf", [128, 1], f32), "pm192": ("sbuf", [128, 1], f32),
     "Ct": ("sbuf", [128, 64], f32), "Cf": ("sbuf", [128, 64], f32),
-    "ou0": ("sbuf", [128, 64], u16), "ou1": ("sbuf", [128, 64], u16), "ou2": ("sbuf", [128, 64], u16), "op": ("sbuf", [128, 64], u16),
+    "ou0": ("sbuf", [128, 64], u16), "ou1": ("sbuf", [128, 64], u16), "ou2": ("sbuf", [128, 64], u16), "ou3": ("sbuf", [128, 64], u16),
+    "op": ("sbuf", [128, 64], u16),
     "oj": ("sbuf", [128, 64], u16), "opj": ("sbuf", [128, 128], u16), "opos": ("sbuf", [128, 64], u16), "oidx": ("sbuf", [128, 64], u16),
     "cm": ("sbuf", [128, K], bf), "cx0": ("sbuf", [128, K], bf), "cx1": ("sbuf", [128, K], bf), "gx": ("sbuf", [128, K], bf),
+    "gy": ("sbuf", [128, 16 * CS], bf),
     "pg0": ("sbuf", [128, K], bf), "pg1": ("sbuf", [128, K], bf), "pgp": ("sbuf", [128, K], bf), "pgj": ("sbuf", [128, K], bf),
     "pgz": ("sbuf", [128, K], bf), "ge": ("sbuf", [128, K], bf), "tm": ("sbuf", [128, K], bf),
-    "u0f": ("sbuf", [128, 64], f32), "su1": ("sbuf", [128, 128], f32), "su2": ("sbuf", [128, 128], f32), "sp": ("sbuf", [128, 320], f32),
-    "spos": ("sbuf", [128, 128], f32), "sidx": ("sbuf", [128, 128], f32),
-    "d0s": ("sbuf", [128, 128], bf), "d0f": ("sbuf", [128, 320], bf), "fb": ("sbuf", [128, 128], bf), "hb": ("sbuf", [128, 128], bf),
+    "u0f": ("sbuf", [128, 64], f32), "su1": ("sbuf", [128, 128], f32), "su2": ("sbuf", [128, 128], f32), "su3": ("sbuf", [128, 128], f32),
+    "sp": ("sbuf", [128, 320], f32), "spos": ("sbuf", [128, 128], f32), "sidx": ("sbuf", [128, 128], f32),
+    "d0s": ("sbuf", [128, 128], bf), "d0f": ("sbuf", [128, 320], bf), "d0g": ("sbuf", [128, 256], bf),
+    "fb": ("sbuf", [128, 128], bf), "hb": ("sbuf", [128, 128], bf),
     "one64": ("sbuf", [128, 64], bf), "na": ("sbuf", [128, 64], f32), "ad": ("sbuf", [128, 128], f32), "yy": ("sbuf", [128, 128], f32),
     "h0": ("sbuf", [128, 64], i32), "h1": ("sbuf", [128, 64], i32), "Sc": ("sbuf", [128, 64], bf),
     "send": ("sbuf", [128, 16 + 2 * K], bf), "tab0": ("sbuf", [128, 16 + 2 * K], bf), "tab1": ("sbuf", [128, 16 + 2 * K], bf),
@@ -31,8 +36,9 @@ SCRATCH = {
     "pw0": ("psum", [128, 1024], f32), "pw1": ("psum", [128, 1024], f32),
     "pa": ("psum", [128, 512], f32), "pb": ("psum", [128, 512], f32), "pc": ("psum", [128, 512], f32), "pd": ("psum", [128, 512], f32),
 }
-NDMA = 40
-SEMAPHORES = ["sV", "sS", "sP", "sG", "arr0", "arr1", "sent0", "sent1"] + ["d%d" % k for k in range(NDMA)]
+NDMA = 44
+SEMAPHORES = (["sV", "sS", "sP", "sG"] + [a + b + c for a in ("arr", "sent") for b in "hd" for c in "01"]
+              + ["d%d" % k for k in range(NDMA)])
 BANKS = ("pw0a", "pw0b", "pw1a", "pw1b", "pa", "pb", "pc", "pd")
 
 
@@ -99,6 +105,18 @@ def rank_program(g, core, T, topo):
         Q[q].dma_start(out, in_).then_inc(T.sem[s], 16)
         note(("D", s, 16), q, r, w)
 
+    rid, pid, _ = topo.addr(nxt)
+    mask = topo.mask(core, nxt)
+    neng = len(topo.engines(core, nxt))
+
+    def remote(out, in_, tag, r, land):
+        order("G", "D", r, [])
+        g.remote_dma(out, in_, T.sem["arr" + tag], T.sem["sent" + tag], pid, rid, mask)
+        total["sent" + tag] = neng
+        total["arr" + tag] = neng
+        note(("D", "sent" + tag, neng), "G", r, [])
+        lastw[land] = ("D", "arr" + tag, neng)
+
     vec, act, pe = g.vector, g.scalar, g.tensor
 
     def Bi(k, i):
@@ -129,56 +147,47 @@ def rank_program(g, core, T, topo):
     def sel(ap, pattern, cmp, fill, base, name):
         op("G", lambda: g.affine_select(ap, ap, pattern, cmp, fill, base, 1), [name], [name])
 
-    for k, src in enumerate((T.par, T.jump, T.ln)):
-        dma("Y", T.Ci[:, 192 * k:192 * k + 192], src[:], [], ["Ci%d" % k])
-    dma("S", T.X[:, V0:V0 + K], T.q[:], [], ["X1"])
-    dma("S", T.M[:, Z:Z + V0], T.m[:], [], ["M0"])
+    def fill(ap, val, names):
+        op("V", lambda: vec.memset(ap, val), [], names)
+
+    dma("Y", T.Ci[:, 0:192], T.par[:], [], ["Ci0"])
+    dma("S", T.Ci[:, 192:384], T.jump[:], [], ["Ci1"])
     dma("Y", T.u0i[:], T.u0[:], [], ["u0i"])
-    dma("Y", T.wi[:], T.w[:], [], ["wi"])
-    dma("S", T.X[:, 0:V0], T.x[:], [], ["X0"])
+    dma("S", T.X[:, V0:V0 + K], T.q[:], [], ["X1"])
+    dma("Y", T.M[:, Z:Z + V0], T.m[:], [], ["M0"])
 
     op("G", lambda: g.iota(T.pi[:], [[0, 1]], 0, 1), [], ["pi"])
-    op("G", lambda: g.iota(T.idt[:], [[64, 3], [0, 64]], 0, 0, allow_small_or_imprecise_dtypes=True), [], ["idt"])
-    op("G", lambda: g.iota(T.Cb[:, 1344:1536], [[0, 3], [1, 64]], 0, 0, allow_small_or_imprecise_dtypes=True), [], ["Cb7"])
-    op("G", lambda: g.iota(T.Cb[:, 1536:1728], [[0, 192]], 1, 0, allow_small_or_imprecise_dtypes=True), [], ["Cb8"])
     ball = ["B%d" % k for k in range(8)]
     wall = ["W%d" % k for k in range(10)]
-    op("V", lambda: vec.memset(T.Bm[:], 0.0), [], ball)
-    op("V", lambda: vec.tensor_scalar(T.pj[:], T.pi[:], 15, None, A.bitwise_and), ["pi"], ["pj"])
     prow = ["PT0_%d" % f for f in range(11)]
-    op("V", lambda: vec.memset(T.PT[:, 0:Z + V0], 0.0), [], prow)
-    op("V", lambda: vec.tensor_scalar(T.pm192[:], T.pj[:], 192.0, None, A.mult), ["pj"], ["pm192"])
-    op("V", lambda: vec.memset(T.Wm[:], 0.0), [], wall)
-    op("V", lambda: vec.tensor_scalar(T.Cb[:, 1152:1344], T.idt[:], T.pm192[:], None, A.add), ["idt", "pm192"], ["Cb6"])
+    arow = ["PA_%d" % f for f in range(4)]
+    fill(T.Bm[:], 0.0, ball)
+    fill(T.PA[:], 0.0, arow)
+    fill(T.Wm[:], 0.0, wall)
 
-    def row(q, f, blk):
-        dma(q, T.PT[f::16, Z:Z + V0], T.Cb[:, 192 * blk:192 * blk + 192], ["Cb%d" % blk], ["PT0_%d" % f])
-    row("Y", 10, 8)
-    row("Y", 7, 7)
-    row("Y", 6, 6)
-    for k, f in enumerate((0, 2, 8)):
-        ci = T.Ci[:, 192 * k:192 * k + 192]
-        op("V", lambda: vec.tensor_scalar(T.Cj[:, 384 * k:384 * k + 192], ci, 0xFFC0, None, A.bitwise_and), ["Ci%d" % k], ["Cja%d" % k])
-        op("V", lambda: vec.tensor_scalar(T.Cj[:, 384 * k + 192:384 * k + 384], ci, 63, None, A.bitwise_and), ["Ci%d" % k], ["Cjb%d" % k])
-        if k == 0:
-            op("V", lambda: vec.tensor_copy(T.ou0[:], T.u0i[:]), ["u0i"], ["ou0"])
-        op("V", lambda: vec.tensor_copy(T.Cb[:, 384 * k:384 * k + 384], T.Cj[:, 384 * k:384 * k + 384]),
-           ["Cja%d" % k, "Cjb%d" % k], ["Cb%d" % (2 * k), "Cb%d" % (2 * k + 1)])
-        row("Y", f, 2 * k)
-        row("S", f + 1, 2 * k + 1)
-    op("V", lambda: vec.memset(T.If[:], 0.0), [], ["If0", "If1"])
-    op("V", lambda: vec.memset(T.d0s[:], 0.0), [], ["d0s"])
-    op("V", lambda: vec.memset(T.d0f[:], 0.0), [], ["d0f1", "d0f2", "d0f3", "d0f4"])
-    op("V", lambda: vec.memset(T.fb[:], 0.0), [], ["fb"])
-    op("V", lambda: vec.memset(T.hb[:], 0.0), [], ["hb"])
-    op("V", lambda: vec.memset(T.one64[:], 1.0), [], ["one64"])
-    op("V", lambda: vec.memset(T.M[:, 0:Z], 0.0), [], ["Mz"])
-    op("V", lambda: vec.memset(T.send[:, 0:16 + CAP], 0.0), [], ["sendh", "sendw"])
-    op("V", lambda: vec.memset(T.tab0[:, 16 + CAP:16 + K], 0.0), [], ["gap0"])
-    op("V", lambda: vec.memset(T.tab1[:, 16 + CAP:16 + K], 0.0), [], ["gap1"])
-    op("V", lambda: vec.tensor_copy(T.u0f[:], T.u0i[:]), ["u0i"], ["u0f"])
+    def split_hi(k):
+        op("V", lambda: vec.tensor_scalar(T.Cb[:, 384 * k:384 * k + 192], T.Ci[:, 192 * k:192 * k + 192], 16.0, 0.0, A.subtract, A.max),
+           ["Ci%d" % k], ["Cb%d" % (2 * k)])
+
+    def split_lo(k):
+        op("V", lambda: vec.tensor_tensor(T.Cb[:, 384 * k + 192:384 * k + 384], T.Ci[:, 192 * k:192 * k + 192],
+                                          T.Cb[:, 384 * k:384 * k + 192], A.subtract), ["Ci%d" % k, "Cb%d" % (2 * k)], ["Cb%d" % (2 * k + 1)])
+    split_hi(0)
+    split_hi(1)
+    split_lo(0)
+    split_lo(1)
+    for q, f in (("Y", 0), ("S", 2), ("Y", 1), ("S", 3)):
+        dma(q, T.PA[f::16, :], T.Cb[:, 192 * f:192 * f + 192], ["Cb%d" % f], ["PA_%d" % f])
+    dma("S", T.X[:, 0:V0], T.x[:], [], ["X0"])
+    dma("Y", T.Ci[:, 384:576], T.ln[:], ["Cb3"], ["Ci2"])
+    dma("Y", T.wi[:], T.w[:], [], ["wi"])
+    op("V", lambda: vec.tensor_copy(T.ou0[:], T.u0i[:]), ["u0i"], ["ou0"])
+    fill(T.If[:], 0.0, ["If0", "If1"])
+    fill(T.d0s[:], 0.0, ["d0s"])
+    op("V", lambda: vec.tensor_scalar(T.pj[:], T.pi[:], 15, None, A.bitwise_and), ["pi"], ["pj"])
+    fill(T.PT[:, 0:Z + V0], 0.0, prow)
+    op("V", lambda: vec.tensor_scalar(T.pm192[:], T.pj[:], 192.0, None, A.mult), ["pj"], ["pm192"])
     op("V", lambda: vec.tensor_copy(T.pm[:], T.pj[:]), ["pj"], ["pm"])
-    op("V", lambda: vec.tensor_copy(T.wf[:], T.wi[:]), ["wi"], ["wf"])
 
     fills = {B_ONE: [(16, 1.0), (0, 0.0)], B_DH: [(6, -0.5), (2, 0.5), (0, 0.0)], B_SH: [(6, 0.5), (0, 0.0)],
              B_SI: [(8, -1.0), (6, 0.5), (0, 0.0)], B_J: [(6, 1.0), (2, 0.0)], B_LP: [(10, BIG), (8, 0.0)], B_LN: [(10, -BIG), (8, 0.0)]}
@@ -190,55 +199,84 @@ def rank_program(g, core, T, topo):
                     top, val = fills[k][lvl]
                     sel(T.Bm[:, k * BW + 15:k * BW + 143:16], [[-16, 8]], A.is_ge, val, -top, "B%d" % k)
     bfill([B_ONE, B_DH, B_SH])
+    op("G", lambda: g.iota(T.idt[:], [[64, 3], [0, 64]], 0, 0, allow_small_or_imprecise_dtypes=True), [], ["idt"])
+    op("G", lambda: g.iota(T.Ct[:], [[16, 64]], K, 0, allow_small_or_imprecise_dtypes=True), [], ["Ct"])
+    op("G", lambda: g.iota(T.Cb[:, 1344:1536], [[0, 3], [1, 64]], 0, 0, allow_small_or_imprecise_dtypes=True), [], ["Cb7"])
+    op("G", lambda: g.iota(T.Cb[:, 1536:1728], [[0, 192]], 1, 0, allow_small_or_imprecise_dtypes=True), [], ["Cb8"])
     sel(Wk(W_I), [[-1, 128]], A.not_equal, 1.0, 0, "W%d" % W_I)
     sel(Wk(W_NI), [[-1, 128]], A.not_equal, -1.0, 0, "W%d" % W_NI)
     sel(T.If[:, 0:128], [[-1, 128]], A.not_equal, 1.0, 0, "If0")
     sel(T.If[:, 128:256], [[-1, 128]], A.not_equal, -1.0, 0, "If1")
-    op("G", lambda: g.iota(T.Ct[:], [[16, 64]], K, 0, allow_small_or_imprecise_dtypes=True), [], ["Ct"])
-    bfill([B_SI, B_J, B_LP, B_LN])
+    sel(Wk(W_N128), [[-1, 128]], A.not_equal, -128.0, 0, "W%d" % W_N128)
     sel(Wk(W_ONE), [[-16, 8], [0, 16]], A.is_ge, 1.0, -16, "W%d" % W_ONE)
     sel(Wk(W_NU), [[-16, 8], [0, 16]], A.is_ge, -1.0, -16, "W%d" % W_NU)
-    sel(Wk(W_N128), [[-1, 128]], A.not_equal, -128.0, 0, "W%d" % W_N128)
     sel(Wk(W_ONE), [[-16, 8], [0, 16]], A.is_ge, 0.0, 0, "W%d" % W_ONE)
     sel(Wk(W_NU), [[-1, 128]], A.is_ge, 0.0, 0, "W%d" % W_NU)
-    ents = {W_P: [(6, 0, 1.0), (7, 1, 1.0), (6, 4, 1.0), (7, 5, 1.0), (10, 9, 1.0), (10, 10, 1.0)],
+    ents = {W_ID0: [(6, 6, 1.0), (7, 7, 1.0), (10, 6, float(V0))],
+            W_P: [(6, 0, 1.0), (7, 1, 1.0), (6, 4, 1.0), (7, 5, 1.0), (10, 9, 1.0), (10, 10, 1.0)],
             W_J: [(2, 2, 1.0), (3, 3, 1.0), (4, 2, 1.0), (5, 3, 1.0), (8, 8, 2.0), (9, 9, 2.0), (10, 4, -BIG), (10, 5, -BIG)],
-            W_ID0: [(6, 6, 1.0), (7, 7, 1.0), (10, 6, float(V0))], W_ID1: [(6, 6, 1.0), (7, 7, 1.0), (10, 6, float(V0 + K))]}
-    for lvl in range(8):
-        for k in ents:
-            if lvl < len(ents[k]):
-                f, f2, val = ents[k][lvl]
-                sel(T.Wm[:, k * 128 + f2:(k + 1) * 128:16], [[-16, 8]], A.not_equal, val, -f, "W%d" % k)
+            W_ID1: [(6, 6, 1.0), (7, 7, 1.0), (10, 6, float(V0 + K))]}
+
+    def wfill(ks):
+        for lvl in range(8):
+            for k in ks:
+                if lvl < len(ents[k]):
+                    f, f2, val = ents[k][lvl]
+                    sel(T.Wm[:, k * 128 + f2:(k + 1) * 128:16], [[-16, 8]], A.not_equal, val, -f, "W%d" % k)
+    bfill([B_J, B_LP, B_LN])
+    wfill([W_ID0, W_P])
+    wfill([W_J, W_ID1])
     Wo = T.Wm[:, 1152:1168]
     sel(T.Wm[:, 1152:1160], [[-16, 8]], A.is_ge, 1.0, -2, "W9")
     sel(T.Wm[:, 1160:1168], [[-16, 8]], A.is_ge, 1.0, -6, "W9")
     sel(T.Wm[:, 1152:1160], [[-16, 8]], A.is_ge, 0.0, 0, "W9")
     sel(T.Wm[:, 1160:1168], [[-16, 8]], A.is_ge, 0.0, -2, "W9")
+    bfill([B_SI])
     Ip, In = T.If[:, 0:128], T.If[:, 128:256]
 
-    def late_constants():
-        op("V", lambda: vec.tensor_scalar(T.Bm[:, B_W * BW + 15:B_W * BW + 143:16], T.Bm[:, 15:143:16], T.wf[:], None, A.mult),
-           ["B0", "wf"], ["B%d" % B_W])
-        op("V", lambda: vec.tensor_scalar(T.Cf[:], T.Ct[:], T.pm[:], None, A.add), ["Ct", "pm"], ["Cf"])
+    op("V", lambda: vec.tensor_scalar(T.Cb[:, 1152:1344], T.idt[:], T.pm192[:], None, A.add), ["idt", "pm192"], ["Cb6"])
+    fill(T.d0g[:], 0.0, ["ng0", "ng1", "ng2"])
+    op("V", lambda: vec.tensor_copy(T.u0f[:], T.u0i[:]), ["u0i"], ["u0f"])
+    fill(T.fb[:], 0.0, ["fb", "fc"])
+    fill(T.one64[:], 1.0, ["one64"])
+    fill(T.send[:, 0:16 + CAP], 0.0, ["sendh", "sendw"])
+    op("V", lambda: vec.tensor_scalar(T.Cf[:], T.Ct[:], T.pm[:], None, A.add), ["Ct", "pm"], ["Cf"])
+    fill(T.M[:, 0:Z], 0.0, ["Mz"])
+    fill(T.hb[:], 0.0, ["hb"])
+
+    def row(f, blk):
+        dma("Y", T.PT[f::16, Z:Z + V0], T.Cb[:, 192 * blk:192 * blk + 192], ["Cb%d" % blk, "X0"], ["PT0_%d" % f])
+
+    def late_constants(s):
+        if s == 0:
+            fill(T.tab0[:, 16 + CAP:16 + K], 0.0, ["gap0"])
+            split_hi(2)
+            op("V", lambda: vec.tensor_copy(T.wf[:], T.wi[:]), ["wi"], ["wf"])
+            split_lo(2)
+            op("V", lambda: vec.tensor_scalar(T.Bm[:, B_W * BW + 15:B_W * BW + 143:16], T.Bm[:, 15:143:16], T.wf[:], None, A.mult),
+               ["B0", "wf"], ["B%d" % B_W])
+            for f, blk in ((0, 0), (1, 1), (2, 2), (3, 3), (6, 6), (7, 7), (10, 8), (8, 4), (9, 5)):
+                row(f, blk)
+        if s == 3:
+            fill(T.tab1[:, 16 + CAP:16 + K], 0.0, ["gap1"])
+        if s == 4:
+            fill(T.d0f[:], 0.0, ["d0f1", "nf0", "nf1", "nf2"])
 
     def emit_out_mm(t, h):
         o = V0 + K * t
         mm(T.pw1[0:16, 512 * h:512 * h + 512], Wo, T.PT[:, Z + o + 512 * h:Z + o + 512 * h + 512], True, True,
            ["W9", "PT%d_%d" % (t + 1, h)], ["pw1" + "ab"[h]])
 
-    def emit_out_copy(t, hs):
-        a, b = 512 * hs[0], 512 * hs[-1] + 512
-        op("S", lambda: act.activation(T.yo[0:16, a:b], T.pw1[0:16, a:b], F.Identity), ["pw1" + "ab"[h] for h in hs], ["yo%d" % h for h in hs])
+    def emit_out_copy(t, h):
+        a, b = 512 * h, 512 * h + 512
+        op("S", lambda: act.activation(T.yo[0:16, a:b], T.pw1[0:16, a:b], F.Identity), ["pw1" + "ab"[h]], ["yo%d" % h])
 
-    def emit_out_dma(t, q2="Y"):
-        dma("Y", T.ypar[:, K * t:K * t + K], T.yo[0:8, :], ["yo0", "yo1"], [])
-        dma(q2, T.yjump[:, K * t:K * t + K], T.yo[8:16, :], ["yo0", "yo1"], [])
+    def emit_out_dma(t, q):
+        dma(q, T.ypar[:, K * t:K * t + K], T.yo[0:8, :], ["yo0", "yo1"], [])
+        dma(q, T.yjump[:, K * t:K * t + K], T.yo[8:16, :], ["yo0", "yo1"], [])
 
     CV = 64 - CS
     LV = 16 * CV
-    rid, pid, _ = topo.addr(nxt)
-    mask = topo.mask(core, nxt)
-    neng = len(topo.engines(core, nxt))
 
     for t in range(RO):
         o = V0 + K * t
@@ -251,163 +289,222 @@ def rank_program(g, core, T, topo):
             rX = rX + ["X%db" % k for k in range(2, t + 1)]
             rq = rq + ["X%db" % (t + 1)]
         ask = T.X[:, o:o + K]
-        offs = [T.ou0, T.ou1, T.ou2]
-        scans = [T.su1, T.su2]
+        offs = [T.ou0, T.ou1, T.ou2, T.ou3]
+        scans = [T.su1, T.su2, T.su3]
         cx = [T.cx0, T.cx1]
         pg = [T.pg0, T.pg1]
+        nn = ["nf0", "nf1", "nf2"] if last else ["ng0", "ng1", "ng2"]
+        u1, u2, u3 = T.su1[:, 1::2], T.su2[:, 1::2], T.su3[:, 1::2]
+
+        def nap(s):
+            return T.d0f[:, 4 - s::5] if last else T.d0g[:, 3 - s::4]
 
         def wins(s):
             a = o - K if (s == 0 and t > 0) else 0
             return T.X[:, a:o], T.M[:, Z + a:Z + o], T.PT[:, Z + a:Z + o]
 
-        def votes_x(s, bank, bn):
-            extract(bank[:, 0:64], B_ONE, cx[s % 2], ["cx%da" % (s % 2), "cx%db" % (s % 2)], [bn])
-
-        def stays(s, bank, bn, split):
-            if split:
-                op("S", lambda: act.activation(T.na[:, 0:CV], bank[:, 0:CV], F.Relu, bias=-9.0), [bn], ["naa"])
-                op("S", lambda: act.activation(T.na[:, CV:64], bank[:, CV:64], F.Relu, bias=-2.0), [bn], ["nab"])
+        def pointers(s):
+            if t == 0:
+                gS(pg[s % 2][:], T.PA[:], offs[s][:], arow + ["ou%d" % s], ["pg%d" % (s % 2)])
             else:
-                op("S", lambda: act.activation(T.na[:], bank[:, 0:64], F.Relu, bias=-9.0), [bn], ["naa", "nab"])
-            op("S", lambda: act.activation(T.d0f[:, 4 - s::5], T.na[:], F.Relu, bias=1.0, scale=-1.0), ["naa", "nab"], ["d0f%d" % (4 - s)])
+                gS(pg[s % 2][:], wins(s)[2], offs[s][:], rP + ["ou%d" % s], ["pg%d" % (s % 2)])
 
-        for s in (0, 1):
-            wx, wm, wp = wins(s)
-            on = "ou%d" % s
-            gS(pg[s][:], wp, offs[s][:], rP + [on], ["pg%d" % s])
-            gT(T.cm[:], wm, offs[s][:], ask, A.is_ge, rM + rq + [on], ["cm"])
-            if s == 1:
-                votes_x(0, T.pc, "pc")
-            if CS:
-                gS(T.gx[:, 0:K - LV], wx, offs[s][:, CV:64], rX + [on], ["gx"])
-            gT(cx[s][:, 0:LV], wx, offs[s][:, 0:CV], T.X[:, o:o + LV], A.is_ge, rX + rq + [on],
-               ["cx%da" % s] if CS else ["cx%da" % s, "cx%db" % s])
-            if s == 0 and t > 0:
-                op("V", lambda: vec.tensor_scalar(T.u0f[:], T.h1[:], float(o - K), None, A.add), ["h1"], ["u0f"])
-            if s == 0 and t == 0:
-                late_constants()
+        def m_test(s):
+            gT(T.cm[:], wins(s)[1], offs[s][:], ask, A.is_ge, rM + rq + ["ou%d" % s], ["cm"])
+
+        def x_vec(s):
+            gT(cx[s % 2][:, 0:LV], wins(s)[0], offs[s][:, 0:CV], T.X[:, o:o + LV], A.is_ge, rX + rq + ["ou%d" % s], ["cx%da" % (s % 2)])
+
+        def x_get(s):
+            gS(T.gy[:], wins(s)[0], offs[s][:, CV:64], rX + ["ou%d" % s], ["gy"])
+
+        def x_diff():
+            mm(T.pw0[:, 0:K - LV], Wk(W_NI), T.X[:, o + LV:o + K], True, False, rq + ["W%d" % W_NI], ["pw0a"])
+            mm(T.pw0[:, 0:K - LV], Wk(W_I), T.gy[:], False, True, ["gy", "W%d" % W_I], ["pw0a"])
+
+        def x_sign(s):
+            op("S", lambda: act.activation(cx[s % 2][:, LV:K], T.pw0[:, 0:K - LV], F.Sign, bias=0.5), ["pw0a"], ["cx%db" % (s % 2)])
+
+        def votes_x(s, bank, bn, start=True):
+            extract(bank[:, 0:64], B_ONE, cx[s % 2], ["cx%da" % (s % 2), "cx%db" % (s % 2)], [bn], start=start)
+
+        def stays(s, bank, bn):
+            op("S", lambda: act.activation(T.na[:, 0:CV], bank[:, 0:CV], F.Relu, bias=-9.0), [bn], ["naa"])
+            op("S", lambda: act.activation(T.na[:, CV:64], bank[:, CV:64], F.Relu, bias=-2.0), [bn], ["nab"])
+            op("S", lambda: act.activation(nap(s), T.na[:], F.Relu, bias=1.0, scale=-1.0), ["naa", "nab"], [nn[s]])
+
+        def walk_pe(s):
             extract(T.pb[:, 0:64], B_ONE, T.cm, ["cm"], ["pb"])
             op("S", lambda: act.activation(T.d0s[:, 1::2], T.pb[:, 0:64], F.Sign, bias=-9.5), ["pb"], ["d0s"])
-            extract(T.pa[:, 0:128:2], B_DH, pg[s], ["pg%d" % s], ["pa"])
-            extract(T.pa[:, 1:128:2], B_SH, pg[s], ["pg%d" % s], ["pa"])
-            if CS:
-                mm(T.pw0[:, 0:K - LV], Wk(W_I), T.gx[:, 0:K - LV], True, False, ["gx", "W%d" % W_I], ["pw0a"])
-                mm(T.pw0[:, 0:K - LV], Wk(W_NI), T.X[:, o + LV:o + K], False, True, rq + ["W%d" % W_NI], ["pw0a"])
-            if s == 1:
-                stays(0, T.pc, "pc", CS > 0)
-            if CS:
-                op("S", lambda: act.activation(cx[s][:, LV:K], T.pw0[:, 0:K - LV], F.Sign, bias=0.5), ["pw0a"], ["cx%db" % s])
+            extract(T.pa[:, 0:128:2], B_DH, pg[s % 2], ["pg%d" % (s % 2)], ["pa"])
+            extract(T.pa[:, 1:128:2], B_SH, pg[s % 2], ["pg%d" % (s % 2)], ["pa"])
+
+        def walk_v(s):
             sn = "su%d" % (s + 1)
             op("V", lambda: vec.tensor_tensor_scan(scans[s][:], T.d0s[:], T.pa[:, 0:128], 0.0, A.mult, A.add), ["d0s", "pa"], [sn])
             op("V", lambda: vec.tensor_copy(offs[s + 1][:], scans[s][:, 1::2]), [sn], ["ou%d" % (s + 1)])
 
+        def differences(buf, c0, bn, rec, at):
+            a, e = c0 + at, c0 + 64 * rec
+            mm(buf[:, a:e:rec], Ip, u2, True, False, ["If0", "su2"], [bn])
+            mm(buf[:, a:e:rec], In, u1, False, True, ["If1", "su1"], [bn])
+            mm(buf[:, a + 1:e:rec], Ip, u1, True, False, ["If0", "su1"], [bn])
+            mm(buf[:, a + 1:e:rec], In, T.u0f[:], False, True, ["If1", "u0f"], [bn])
+            mm(buf[:, a + 2:e:rec], Ip, T.u0f[:], True, True, ["If0", "u0f"], [bn])
+
+        for s in range(2 if last else 3):
+            pointers(s)
+            m_test(s)
+            if s > 0:
+                votes_x(s - 1, T.pc, "pc")
+            if t > 0 and s < 2:
+                emit_out_mm(t - 1, s)
+            if s == 2:
+                differences(T.pw1, 512, "pw1b", 4, 1)
+                mm(T.pw1[:, 512:768:4], In, u2, True, False, ["If1", "su2"], ["pw1b"])
+            if t == 0 and s == 0:
+                late_constants(0)
+            x_get(s)
+            x_vec(s)
+            if s == 0 and t > 0:
+                op("V", lambda: vec.tensor_scalar(T.u0f[:], T.h1[:], float(o - K), None, A.add), ["h1"], ["u0f"])
+            if t == 1:
+                late_constants(3 + s)
+            walk_pe(s)
+            x_diff()
+            if s > 0:
+                stays(s - 1, T.pc, "pc")
+            if t > 0 and s < 2:
+                emit_out_copy(t - 1, s)
+                if s == 1:
+                    emit_out_dma(t - 1, "Y")
+            x_sign(s)
+            walk_v(s)
+
         wx, wm, wp = wins(2)
-        u1, u2 = T.su1[:, 1::2], T.su2[:, 1::2]
-        gS(pg[0][:], wp, T.ou2[:], rP + ["ou2"], ["pg0"])
-        gT(cx[0][:], wx, T.ou2[:], ask, A.is_ge, rX + rq + ["ou2"], ["cx0a", "cx0b"])
-        gT(T.cm[:], wm, T.ou2[:], ask, A.is_ge, rM + rq + ["ou2"], ["cm"])
-        votes_x(1, T.pc, "pc")
-        mm(T.pa[:, 2:320:5], Ip, u2, True, False, ["If0", "su2"], ["pa"])
-        mm(T.pa[:, 2:320:5], In, u1, False, True, ["If1", "su1"], ["pa"])
-        mm(T.pa[:, 3:320:5], Ip, u1, True, False, ["If0", "su1"], ["pa"])
-        mm(T.pa[:, 3:320:5], In, T.u0f[:], False, True, ["If1", "u0f"], ["pa"])
-        mm(T.pa[:, 4:320:5], Ip, T.u0f[:], True, True, ["If0", "u0f"], ["pa"])
-        if t > 0:
-            emit_out_mm(t - 1, 0)
-            emit_out_mm(t - 1, 1)
-        stays(1, T.pc, "pc", CS > 0)
-        votes_x(2, T.pd, "pd")
-        stays(2, T.pd, "pd", False)
-        extract(T.pa[:, 0:320:5], B_DH, pg[0], ["pg0"], ["pa"])
-        extract(T.pa[:, 1:320:5], B_SI, pg[0], ["pg0"], ["pa"])
-        if t > 0:
-            emit_out_copy(t - 1, (0, 1))
-            emit_out_dma(t - 1)
-        extract(T.pb[:, 0:64], B_ONE, T.cm, ["cm"], ["pb"])
-        op("S", lambda: act.activation(T.d0f[:, 1::5], T.pb[:, 0:64], F.Sign, bias=-9.5), ["pb"], ["d0f1"])
-        op("V", lambda: vec.tensor_tensor_scan(T.sp[:], T.d0f[:], T.pa[:, 0:320], 0.0, A.mult, A.add),
-           ["d0f1", "d0f2", "d0f3", "d0f4", "pa"], ["sp"])
-        op("V", lambda: vec.tensor_copy(T.op[:], T.sp[:, 4::5]), ["sp"], ["op"])
-        pf = T.sp[:, 4::5]
         wz_m, wz_p = T.M[:, 0:Z + o], T.PT[:, 0:Z + o]
 
         def pick_zero():
             op("S", lambda: act.activation(T.ad[:, 0:64], T.pb[:, 0:64], F.Abs), ["pb"], ["ada"])
             op("S", lambda: act.activation(T.ad[:, 64:128], T.pb[:, 0:64], F.Abs), ["pb"], ["adb"])
 
-        def pick_zero_v():
+        def pick_a():
             op("V", lambda: vec.tensor_tensor(T.yy[:], T.pa[:, 0:128], T.ad[:], A.subtract), ["pa", "ada", "adb"], ["yy"])
+
+        def pick_b():
             op("V", lambda: vec.tensor_scalar(T.opj[:], T.yy[:], float(Z), None, A.add), ["yy"], ["opj"])
+
+        def half(h):
+            return slice(512 * h, 512 * h + 512)
 
         if not last:
             tab = T["tab%d" % t]
-            gT(cx[0][:], wx, T.op[:], ask, A.is_ge, rX + rq + ["op"], ["cx0a", "cx0b"])
-            gS(T.pgp[:], wp, T.op[:], rP + ["op"], ["pgp0", "pgp1"])
+            x_get(3)
+            x_vec(3)
+            votes_x(2, T.pd, "pd")
+            mm(T.pw1[:, 512:768:4], Ip, u3, False, True, ["If0", "su3"], ["pw1b"])
+            x_diff()
+            stays(2, T.pd, "pd")
+            x_sign(3)
+            for s in range(3):
+                mm(T.pc[:, 0:64], Wk(W_N128), nap(s), s == 0, False, [nn[s], "W%d" % W_N128], ["pc"])
+            op("V", lambda: vec.tensor_tensor_scan(T.sp[:, 0:256], T.d0g[:], T.pw1[:, 512:768], 0.0, A.mult, A.add), nn + ["pw1b"], ["sp"])
+            pf = T.sp[:, 3:256:4]
+            op("V", lambda: vec.tensor_copy(T.op[:], pf), ["sp"], ["op"])
+            votes_x(3, T.pc, "pc", start=False)
             mm(T.pd[:, 1:128:2], Ip, T.Cf[:], True, True, ["If0", "Cf"], ["pd"])
             mm(T.pd[:, 0:128:2], In, T.Cf[:], True, False, ["If1", "Cf"], ["pd"])
+            gS(T.pgp[:], wp, T.op[:], rP + ["op"], ["pgp0", "pgp1"])
+            op("V", lambda: vec.tensor_scalar(T.fb[:, 1:2 * CV:2], T.pc[:, 0:CV], 9.5 - 384.0, None, A.is_lt), ["pc"], ["fb"])
+            op("V", lambda: vec.tensor_scalar(T.fb[:, 2 * CV + 1::2], T.pc[:, CV:64], 3.0 - 384.0, None, A.is_lt), ["pc"], ["fc"])
+            op("V", lambda: vec.tensor_tensor_scan(T.Sc[:], T.one64[:], T.fb[:, 1::2], 0.0, A.mult, A.add), ["one64", "fb", "fc"], ["Sc"])
+            mm(T.pd[:, 0:128:2], Wk(W_NU), T.fb[:, 1::2], False, False, ["fb", "fc", "W%d" % W_NU], ["pd"])
+            mm(T.pd[:, 0:128:2], Wk(W_ONE), T.Sc[:], False, True, ["Sc", "W%d" % W_ONE], ["pd"])
+            mm(T.pc[:, 64:65], Wk(W_ONE), T.Sc[:, 63:64], True, True, ["Sc", "W%d" % W_ONE], ["pc"])
             mm(T.pa[:, 0:64], Ip, pf, True, True, ["If0", "sp"], ["pa"])
             for h in (0, 1):
-                mm(T.pw1[:, 512 * h:512 * h + 512], Wk(W_ID0 + t), T.PT[:, Z + 512 * h:Z + 512 * h + 512], True, False,
+                mm(T.pw1[:, half(h)], Wk(W_ID0 + t), T.PT[:, Z + 512 * h:Z + 512 * h + 512], True, False,
                    prow + ["W%d" % (W_ID0 + t)], ["pw1" + "ab"[h]])
-            votes_x(0, T.pc, "pc")
-            op("V", lambda: vec.tensor_scalar(T.fb[:, 1::2], T.pc[:, 0:64], 9.5, None, A.is_lt), ["pc"], ["fb"])
             extract(T.pa[:, 64:128], B_J, T.pgp, ["pgp0", "pgp1"], ["pa"])
-            gS(T.gx[:], wx, T.op[:], rX + ["op"], ["gx"])
-            op("V", lambda: vec.tensor_tensor_scan(T.Sc[:], T.one64[:], T.fb[:, 1::2], 0.0, A.mult, A.add), ["one64", "fb"], ["Sc"])
-            mm(T.pd[:, 0:128:2], Wk(W_ONE), T.Sc[:], False, False, ["Sc", "W%d" % W_ONE], ["pd"])
-            mm(T.pd[:, 0:128:2], Wk(W_NU), T.fb[:, 1::2], False, True, ["fb", "W%d" % W_NU], ["pd"])
-            mm(T.pc[:, 64:65], Wk(W_ONE), T.Sc[:, 63:64], True, True, ["Sc", "W%d" % W_ONE], ["pc"])
-            op("V", lambda: vec.tensor_copy(T.oj[:], T.pa[:, 64:128]), ["pa"], ["oj"])
-            op("V", lambda: vec.tensor_tensor_scan(T.spos[:], T.fb[:], T.pd[:, 0:128], 0.0, A.mult, A.add), ["fb", "pd"], ["spos"])
+            gS(T.gx[:, half(0)], wx, T.op[:, 0:32], rX + ["op"], ["gxa"])
+            op("V", lambda: vec.tensor_tensor_scan(T.spos[:], T.fb[:], T.pd[:, 0:128], 0.0, A.mult, A.add), ["fb", "fc", "pd"], ["spos"])
             op("V", lambda: vec.tensor_scalar(T.send[:, 15:16], T.pc[:, 64:65], float(CAP), 192.0, A.min, A.subtract), ["pc"], ["sendh"])
+            remote(tab[:, 0:16], T.send[:, 0:16], "h%d" % t, ["sendh"], "landh%d" % t)
             op("V", lambda: vec.tensor_copy(T.opos[:], T.spos[:, 1::2]), ["spos"], ["opos"])
-            op("V", lambda: vec.tensor_copy(T.send[:, 16:16 + 2 * K].indirect(T.opos[:]), ask), rq + ["opos"], ["sendw"])
-            order("G", "D", ["sendh", "sendw"], [])
-            g.remote_dma(tab[:, 0:16 + CAP], T.send[:, 0:16 + CAP], T.sem["arr%d" % t], T.sem["sent%d" % t], pid, rid, mask)
-            total["sent%d" % t] = neng
-            total["arr%d" % t] = neng
-            note(("D", "sent%d" % t, neng), "G", ["sendh", "sendw"], [])
-            lastw["land%d" % t] = ("D", "arr%d" % t, neng)
+            op("V", lambda: vec.tensor_copy(T.send[:, 16:16 + 2 * K].indirect(T.opos[:, 0:SC0]), T.X[:, o:o + 16 * SC0]), rq + ["opos"], ["sendw"])
+            op("V", lambda: vec.tensor_copy(T.oj[:], T.pa[:, 64:128]), ["pa"], ["oj"])
+            op("V", lambda: vec.tensor_copy(T.send[:, 16:16 + 2 * K].indirect(T.opos[:, SC0:64]), T.X[:, o + 16 * SC0:o + K]), rq + ["opos"], ["sendw"])
+            remote(tab[:, 16:16 + CAP], T.send[:, 16:16 + CAP], "d%d" % t, ["sendw"], "land%d" % t)
             extract(T.pb[:, 0:64], B_LP, T.pgp, ["pgp0", "pgp1"], ["pb"], stop=False)
             gS(T.pgj[:], wp, T.oj[:], rP + ["oj"], ["pgj0", "pgj1"])
             for h in (0, 1):
-                mm(T.pw1[:, 512 * h:512 * h + 512], Wk(W_P), T.pgp[:, 512 * h:512 * h + 512], False, False,
-                   ["pgp0", "pgp1", "W%d" % W_P], ["pw1" + "ab"[h]])
-            for h in (0, 1):
-                c = slice(512 * h, 512 * h + 512)
-                mm(T.pw0[:, c], Wk(W_I), T.gx[:, c], True, False, ["gx", "W%d" % W_I], ["pw0" + "ab"[h]])
-                mm(T.pw0[:, c], Wk(W_I), T.X[:, o + 512 * h:o + 512 * h + 512], False, True, rq, ["pw0" + "ab"[h]])
+                mm(T.pw1[:, half(h)], Wk(W_P), T.pgp[:, half(h)], False, False, ["pgp0", "pgp1", "W%d" % W_P], ["pw1" + "ab"[h]])
+
+            def sums(h, more):
+                b = "pw0" + "ab"[h]
+                mm(T.pw0[:, half(h)], Wk(W_I), T.X[:, o + 512 * h:o + 512 * h + 512], True, False, rq + ["W%d" % W_I], [b])
+                mm(T.pw0[:, half(h)], Wk(W_I), T.gx[:, half(h)], False, not more, ["gx" + "ab"[h]], [b])
+                if more:
+                    mm(T.pw0[:, half(h)], Wk(W_N128), T.ge[:, half(h)], False, True, ["ge%d" % h, "W%d" % W_N128], [b])
+
+            def wraps(h):
+                op("S", lambda: act.activation(T.ge[:, half(h)], T.pw0[:, half(h)], F.Sign, bias=t - 255.5), ["pw0" + "ab"[h]], ["ge%d" % h])
+
+            def kept(h):
+                op("S", lambda: act.activation(tab[:, 16 + K + 512 * h:16 + K + 512 * h + 512], T.pw0[:, half(h)], F.Identity, bias=t - 128.0),
+                   ["pw0" + "ab"[h]], ["tabc%d_%d" % (t, h)])
+            sums(0, False)
+            wraps(0)
             extract(T.pb[:, 0:64], B_LN, T.pgj, ["pgj0", "pgj1"], ["pb"], start=False)
-            op("S", lambda: act.activation(T.ge[:], T.pw0[:], F.Sign, bias=t - 255.5), ["pw0a", "pw0b"], ["ge"])
             pick_zero()
-            for h in (0, 1):
-                c = slice(512 * h, 512 * h + 512)
-                mm(T.pw0[:, c], Wk(W_I), T.gx[:, c], True, False, ["gx"], ["pw0" + "ab"[h]])
-                mm(T.pw0[:, c], Wk(W_I), T.X[:, o + 512 * h:o + 512 * h + 512], False, False, rq, ["pw0" + "ab"[h]])
-                mm(T.pw0[:, c], Wk(W_N128), T.ge[:, c], False, True, ["ge", "W%d" % W_N128], ["pw0" + "ab"[h]])
-            op("S", lambda: act.activation(tab[:, 16 + K:16 + 2 * K], T.pw0[:], F.Identity, bias=t - 128.0), ["pw0a", "pw0b"], ["tabc%d" % t])
-            pick_zero_v()
-            gS(T.pgz[:], wz_p, T.opj[:, 64:128], rP + ["opj"], ["pgz0", "pgz1"])
+            sums(0, True)
+            gS(T.gx[:, half(1)], wx, T.op[:, 32:64], rX + ["op"], ["gxb"])
+            sums(1, False)
+            kept(0)
+            wraps(1)
+            sums(1, True)
+            pick_a()
+            op("V", lambda: vec.tensor_scalar(T.hb[:, 1::2], T.spos[:, 1::2], 192.0, tab[:, 15:16], A.subtract, A.is_lt),
+               ["spos", "landh%d" % t], ["hb"])
+            pick_b()
+            op("V", lambda: vec.tensor_tensor_scan(T.sidx[:], T.hb[:], T.pd[:, 0:128], 0.0, A.mult, A.add), ["hb", "pd"], ["sidx"])
+            gS(T.pgz[:, half(0)], wz_p, T.opj[:, 64:96], rP + ["opj"], ["pgz0"])
+            kept(1)
+            gS(T.pgz[:, half(1)], wz_p, T.opj[:, 96:128], rP + ["opj"], ["pgz1"])
             gT(T.tm[:], wz_m, T.opj[:, 0:64], ask, A.max, rM + rq + ["Mz", "opj"], ["tm0", "tm1"])
+            op("V", lambda: vec.tensor_copy(T.oidx[:], T.sidx[:, 1::2]), ["sidx"], ["oidx"])
             gT(T.M[:, Z + o:Z + o + K], wz_m, T.opj[:, 64:128], T.tm[:], A.max, rM + ["Mz", "opj", "tm0", "tm1"],
                ["M%d_0" % (t + 1), "M%d_1" % (t + 1)])
             for h in (0, 1):
-                mm(T.pw1[:, 512 * h:512 * h + 512], Wk(W_J), T.pgz[:, 512 * h:512 * h + 512], False, True,
-                   ["pgz0", "pgz1", "W%d" % W_J], ["pw1" + "ab"[h]])
-            op("S", lambda: act.activation(T.PT[:, Z + o:Z + o + K], T.pw1[:], F.Relu), ["pw1a", "pw1b"], ["PT%d_0" % (t + 1), "PT%d_1" % (t + 1)])
+                mm(T.pw1[:, half(h)], Wk(W_J), T.pgz[:, half(h)], False, True, ["pgz%d" % h, "W%d" % W_J], ["pw1" + "ab"[h]])
             dma("Y", T.ym[:, K * t:K * t + K], T.M[:, Z + o:Z + o + K], ["M%d_0" % (t + 1), "M%d_1" % (t + 1)], [])
-            op("V", lambda: vec.tensor_scalar(T.hb[:, 1::2], T.spos[:, 1::2], 192.0, tab[:, 15:16], A.subtract, A.is_lt),
-               ["spos", "land%d" % t], ["hb"])
-            op("V", lambda: vec.tensor_tensor_scan(T.sidx[:], T.hb[:], T.pd[:, 0:128], 0.0, A.mult, A.add), ["hb", "pd"], ["sidx"])
-            op("V", lambda: vec.tensor_copy(T.oidx[:], T.sidx[:, 1::2]), ["sidx"], ["oidx"])
-            rt = ["land%d" % t, "gap%d" % t, "tabc%d" % t, "oidx"]
+            rt = ["land%d" % t, "gap%d" % t, "tabc%d_0" % t, "tabc%d_1" % t, "oidx"]
             gV(T.X[:, o + K:o + K + 512], tab[:, 16:16 + 2 * K], T.oidx[:, 0:32], rt, ["X%d" % (t + 2)])
             gS(T.X[:, o + K + 512:o + 2 * K], tab[:, 16:16 + 2 * K], T.oidx[:, 32:64], rt, ["X%db" % (t + 2)])
+            op("S", lambda: act.activation(T.PT[:, Z + o:Z + o + K], T.pw1[:], F.Relu), ["pw1a", "pw1b"], ["PT%d_0" % (t + 1), "PT%d_1" % (t + 1)])
             extract(T.pc[:, 0:64], B_W, T.X, ["X%d" % (t + 2), "X%db" % (t + 2)], ["pc"], c0=o + K)
             op("V", lambda: vec.tensor_copy(T.h0[:], T.pc[:, 0:64]), ["pc"], ["h0"])
             op("V", lambda: vec.tensor_scalar(T.h1[:], T.h0[:], K - 1, None, A.bitwise_and), ["h0"], ["h1"])
             op("V", lambda: vec.tensor_copy(T.ou0[:], T.h1[:]), ["h1"], ["ou0"])
         else:
+            x_get(2)
+            x_vec(2)
+            x_diff()
+            pointers(2)
+            m_test(2)
+            votes_x(1, T.pc, "pc")
+            differences(T.pa, 0, "pa", 5, 2)
+            x_sign(2)
+            stays(1, T.pc, "pc")
+            extract(T.pa[:, 0:320:5], B_DH, pg[0], ["pg0"], ["pa"])
+            votes_x(2, T.pd, "pd")
+            stays(2, T.pd, "pd")
+            extract(T.pb[:, 0:64], B_ONE, T.cm, ["cm"], ["pb"])
+            op("S", lambda: act.activation(T.d0f[:, 1::5], T.pb[:, 0:64], F.Sign, bias=-9.5), ["pb"], ["d0f1"])
+            extract(T.pa[:, 1:320:5], B_SI, pg[0], ["pg0"], ["pa"])
+            op("V", lambda: vec.tensor_tensor_scan(T.sp[:], T.d0f[:], T.pa[:, 0:320], 0.0, A.mult, A.add), nn + ["d0f1", "pa"], ["sp"])
+            pf = T.sp[:, 4::5]
+            op("V", lambda: vec.tensor_copy(T.op[:], pf), ["sp"], ["op"])
             gS(T.pgp[:, 512:K], wp, T.op[:, 32:64], rP + ["op"], ["pgp1"])
             gV(T.pgp[:, 0:512], wp, T.op[:, 0:32], rP + ["op"], ["pgp0"])
             mm(T.pa[:, 0:64], Ip, pf, True, True, ["If0", "sp"], ["pa"])
@@ -417,32 +514,29 @@ def rank_program(g, core, T, topo):
             gS(T.pgj[:, 512:K], wp, T.oj[:, 32:64], rP + ["oj"], ["pgj1"])
             gV(T.pgj[:, 0:512], wp, T.oj[:, 0:32], rP + ["oj"], ["pgj0"])
             for h in (0, 1):
-                mm(T.pw0[:, 512 * h:512 * h + 512], Wk(W_P), T.pgp[:, 512 * h:512 * h + 512], True, False,
-                   ["pgp0", "pgp1", "W%d" % W_P], ["pw0" + "ab"[h]])
+                mm(T.pw0[:, half(h)], Wk(W_P), T.pgp[:, half(h)], True, False, ["pgp0", "pgp1", "W%d" % W_P], ["pw0" + "ab"[h]])
             extract(T.pb[:, 0:64], B_LN, T.pgj, ["pgj0", "pgj1"], ["pb"], start=False)
             pick_zero()
-            pick_zero_v()
+            pick_a()
+            pick_b()
             for h in (0, 1):
-                c = slice(512 * h, 512 * h + 512)
-                gS(T.pgz[:, c], wz_p, T.opj[:, 64 + 32 * h:96 + 32 * h], rP + ["opj"], ["pgz%d" % h])
-                mm(T.pw0[:, c], Wk(W_J), T.pgz[:, c], False, True, ["pgz%d" % h, "W%d" % W_J], ["pw0" + "ab"[h]])
+                gS(T.pgz[:, half(h)], wz_p, T.opj[:, 64 + 32 * h:96 + 32 * h], rP + ["opj"], ["pgz%d" % h])
+                mm(T.pw0[:, half(h)], Wk(W_J), T.pgz[:, half(h)], False, True, ["pgz%d" % h, "W%d" % W_J], ["pw0" + "ab"[h]])
             for h in (0, 1):
-                c = slice(512 * h, 512 * h + 512)
-                a = Z + o + 512 * h
-                gT(T.tm[:, c], wz_m, T.opj[:, 32 * h:32 * h + 32], T.X[:, o + 512 * h:o + 512 * h + 512], A.max,
+                gT(T.tm[:, half(h)], wz_m, T.opj[:, 32 * h:32 * h + 32], T.X[:, o + 512 * h:o + 512 * h + 512], A.max,
                    rM + rq + ["Mz", "opj"], ["tm%d" % h])
-                gT(T.M[:, a:a + 512], wz_m, T.opj[:, 64 + 32 * h:96 + 32 * h], T.tm[:, c], A.max,
+            for h in (0, 1):
+                a = Z + o + 512 * h
+                gT(T.M[:, a:a + 512], wz_m, T.opj[:, 64 + 32 * h:96 + 32 * h], T.tm[:, half(h)], A.max,
                    rM + ["Mz", "opj", "tm%d" % h], ["M%d_%d" % (t + 1, h)])
                 dma("Y", T.ym[:, K * t + 512 * h:K * t + 512 * h + 512], T.M[:, a:a + 512], ["M%d_%d" % (t + 1, h)], [])
             for h in (0, 1):
                 a = Z + o + 512 * h
-                op("S", lambda: act.activation(T.PT[:, a:a + 512], T.pw0[:, 512 * h:512 * h + 512], F.Relu),
-                   ["pw0" + "ab"[h]], ["PT%d_%d" % (t + 1, h)])
+                op("S", lambda: act.activation(T.PT[:, a:a + 512], T.pw0[:, half(h)], F.Relu), ["pw0" + "ab"[h]], ["PT%d_%d" % (t + 1, h)])
                 emit_out_mm(t, h)
-            emit_out_copy(t, (0,))
-            emit_out_copy(t, (1,))
-            dma("S", T.ypar[:, K * t:K * t + K], T.yo[0:8, :], ["yo0", "yo1"], [])
-            dma("S", T.yjump[:, K * t:K * t + K], T.yo[8:16, :], ["yo0", "yo1"], [])
+            emit_out_copy(t, 0)
+            emit_out_copy(t, 1)
+            emit_out_dma(t, "S")
 
     for s in total:
         g.wait_ge(T.sem[s], total[s])

@@ -2,42 +2,50 @@ from concourse.mybir import AluOpType as A, ActivationFunctionType as F
 
 V0, K, CAP, RO = 3072, 1024, 384, 3
 Z = 16
-CS = 16
-SC0 = 16
+CV = 48
+C1 = 36
+CF = 20
+GX = 40
+MA = 1792
 BIG = 8192.0
 BW = 144
-B_ONE, B_DH, B_SH, B_SI, B_J, B_LP, B_LN, B_W = range(8)
-W_I, W_NI, W_N128, W_ONE, W_NU, W_P, W_J, W_ID0, W_ID1 = range(9)
+WD = 3104
+B_ONE, B_SH, B_SI, B_J, B_LP, B_LN, B_W = range(7)
+W_P, W_J, W_ID0, W_ID1, W_I, W_NI, W_N128, W_ONE, W_NU, W_NF, W_TRI, W_N4K, W_MK = range(13)
 
 bf, f32, i32, u16 = "bfloat16", "float32", "int32", "uint16"
 SCRATCH = {
     "X": ("sbuf", [128, V0 + RO * K], bf), "M": ("sbuf", [128, Z + V0 + RO * K], bf), "PT": ("sbuf", [128, Z + V0 + RO * K], bf),
     "PA": ("sbuf", [128, V0], bf),
     "Ci": ("sbuf", [128, 576], i32), "Cb": ("sbuf", [128, 1728], bf), "idt": ("sbuf", [128, 192], bf),
-    "u0i": ("sbuf", [128, 64], i32), "wi": ("sbuf", [128, 1], i32), "wf": ("sbuf", [128, 1], f32),
-    "pi": ("sbuf", [128, 1], i32), "pj": ("sbuf", [128, 1], i32), "pm": ("sbuf", [128, 1], f32), "pm192": ("sbuf", [128, 1], f32),
-    "Ct": ("sbuf", [128, 64], f32), "Cf": ("sbuf", [128, 64], f32),
+    "u0i": ("sbuf", [128, 64], i32), "wi": ("sbuf", [128, 1], i32), "pi": ("sbuf", [128, 1], i32), "pj": ("sbuf", [128, 1], i32),
+    "cl": ("sbuf", [128, 8], f32), "zs": ("sbuf", [128, 1], bf),
+    "Ct": ("sbuf", [128, 64], f32), "Cf": ("sbuf", [128, 64], f32), "col": ("sbuf", [128, 64], bf), "c15": ("sbuf", [128, 64], bf),
+    "six": ("sbuf", [128, 64], bf), "dn": ("sbuf", [128, CAP], bf), "far": ("sbuf", [128, 64], bf),
     "ou0": ("sbuf", [128, 64], u16), "ou1": ("sbuf", [128, 64], u16), "ou2": ("sbuf", [128, 64], u16), "ou3": ("sbuf", [128, 64], u16),
-    "op": ("sbuf", [128, 64], u16),
-    "oj": ("sbuf", [128, 64], u16), "opj": ("sbuf", [128, 128], u16), "opos": ("sbuf", [128, 64], u16), "oidx": ("sbuf", [128, 64], u16),
+    "op": ("sbuf", [128, 64], u16), "oj": ("sbuf", [128, 64], u16), "opj": ("sbuf", [128, 128], u16), "oidx": ("sbuf", [128, 64], u16),
+    "ost": ("sbuf", [128, 4], u16),
     "cm": ("sbuf", [128, K], bf), "cx0": ("sbuf", [128, K], bf), "cx1": ("sbuf", [128, K], bf), "gx": ("sbuf", [128, K], bf),
-    "gy": ("sbuf", [128, 16 * CS], bf),
+    "gy": ("sbuf", [128, K - 16 * CV], bf),
     "pg0": ("sbuf", [128, K], bf), "pg1": ("sbuf", [128, K], bf), "pgp": ("sbuf", [128, K], bf), "pgj": ("sbuf", [128, K], bf),
     "pgz": ("sbuf", [128, K], bf), "ge": ("sbuf", [128, K], bf), "tm": ("sbuf", [128, K], bf),
-    "u0f": ("sbuf", [128, 64], f32), "su1": ("sbuf", [128, 128], f32), "su2": ("sbuf", [128, 128], f32), "su3": ("sbuf", [128, 128], f32),
-    "sp": ("sbuf", [128, 320], f32), "spos": ("sbuf", [128, 128], f32), "sidx": ("sbuf", [128, 128], f32),
-    "d0s": ("sbuf", [128, 128], bf), "d0f": ("sbuf", [128, 320], bf), "d0g": ("sbuf", [128, 256], bf),
-    "fb": ("sbuf", [128, 128], bf), "hb": ("sbuf", [128, 128], bf),
-    "one64": ("sbuf", [128, 64], bf), "na": ("sbuf", [128, 64], f32), "ad": ("sbuf", [128, 128], f32), "yy": ("sbuf", [128, 128], f32),
-    "h0": ("sbuf", [128, 64], i32), "h1": ("sbuf", [128, 64], i32), "Sc": ("sbuf", [128, 64], bf),
-    "send": ("sbuf", [128, 16 + 2 * K], bf), "tab0": ("sbuf", [128, 16 + 2 * K], bf), "tab1": ("sbuf", [128, 16 + 2 * K], bf),
-    "Bm": ("sbuf", [128, 8 * BW], bf), "Wm": ("sbuf", [128, 9 * 128 + 16], bf), "If": ("sbuf", [128, 256], f32),
-    "yo": ("sbuf", [128, K], f32),
+    "uf": ("sbuf", [128, 256], f32), "sg": ("sbuf", [128, 128], bf), "tu": ("sbuf", [128, 136], f32),
+    "sp": ("sbuf", [128, 256], f32), "sst": ("sbuf", [128, 128], f32), "sidx": ("sbuf", [128, 128], f32),
+    "d0g": ("sbuf", [128, 256], bf), "d0m": ("sbuf", [128, 128], bf),
+    "fb": ("sbuf", [128, 64], bf), "hb": ("sbuf", [128, 128], bf), "Rk": ("sbuf", [128, 64], bf),
+    "one64": ("sbuf", [128, 64], bf), "na": ("sbuf", [128, 64], f32), "ad": ("sbuf", [128, 64], f32), "yy": ("sbuf", [128, 128], f32),
+    "h0": ("sbuf", [128, 64], i32), "h1": ("sbuf", [128, 64], i32), "Sc": ("sbuf", [128, 72], bf),
+    "Wd": ("sbuf", [128, 2 * WD], bf), "Zr": ("sbuf", [128, CAP], bf), "Zc": ("sbuf", [128, CAP], bf),
+    "cnt": ("sbuf", [128, 16], bf), "got0": ("sbuf", [128, 16], bf), "got1": ("sbuf", [128, 16], bf),
+    "inv": ("sbuf", [128, 24], u16), "who0": ("sbuf", [128, 24], u16), "who1": ("sbuf", [128, 24], u16),
+    "qp0": ("sbuf", [128, K], bf), "qp1": ("sbuf", [128, K], bf), "tab": ("sbuf", [128, CAP + K], bf),
+    "Bm": ("sbuf", [128, 7 * BW], bf), "Wm": ("sbuf", [128, 13 * 128], bf), "Ws": ("sbuf", [128, 32 + CAP], bf), "Wo": ("sbuf", [128, 136], bf),
+    "If": ("sbuf", [128, 256], f32), "yo": ("sbuf", [128, 128], f32),
     "pw0": ("psum", [128, 1024], f32), "pw1": ("psum", [128, 1024], f32),
     "pa": ("psum", [128, 512], f32), "pb": ("psum", [128, 512], f32), "pc": ("psum", [128, 512], f32), "pd": ("psum", [128, 512], f32),
 }
-NDMA = 44
-SEMAPHORES = (["sV", "sS", "sP", "sG"] + [a + b + c for a in ("arr", "sent") for b in "hd" for c in "01"]
+NDMA = 36
+SEMAPHORES = (["sV", "sS", "sP", "sG"] + [a + b + c for a in ("arr", "sent") for b in "qhd" for c in "01"]
               + ["d%d" % k for k in range(NDMA)])
 BANKS = ("pw0a", "pw0b", "pw1a", "pw1b", "pa", "pb", "pc", "pd")
 
@@ -125,15 +133,28 @@ def rank_program(g, core, T, topo):
     def Wk(k):
         return T.Wm[:, k * 128:(k + 1) * 128]
 
-    def extract(out, k, src, r, w, start=True, stop=True, c0=0):
+    def wn(k):
+        return "W%d" % k
+
+    def extract(out, k, src, r, w, start=True, stop=True, c0=0, n=K):
         def fn():
             for i in range(16):
-                ins = pe.matmul(out, Bi(k, i), src[:, c0 + i:c0 + K:16], start and i == 0, stop and i == 15)
+                ins = pe.matmul(out, Bi(k, i), src[:, c0 + i:c0 + n:16], start and i == 0, stop and i == 15)
             return ins
         op("P", fn, r + ["B%d" % k], w)
 
+    def turn(bank, wts, src, r, w):
+        def fn():
+            for b in range(8):
+                ins = pe.matmul(bank[:, b:128:8], src[:, b:K:8], wts, True, True)
+            return ins
+        op("P", fn, r, w)
+
     def mm(out, lhsT, rhs, start, stop, r, w):
         op("P", lambda: pe.matmul(out, lhsT, rhs, start, stop), r, w)
+
+    def mw(out, k, rhs, start, stop, r, w):
+        mm(out, Wk(k), rhs, start, stop, r + [wn(k)], w)
 
     def gS(out, win, off, r, w):
         op("S", lambda: act.activation(out, win.indirect(off), F.Identity), r, w)
@@ -144,74 +165,86 @@ def rank_program(g, core, T, topo):
     def gT(out, win, off, in1, alu, r, w):
         op("V", lambda: vec.tensor_tensor(out, win.indirect(off), in1, alu), r, w)
 
-    def sel(ap, pattern, cmp, fill, base, name):
-        op("G", lambda: g.affine_select(ap, ap, pattern, cmp, fill, base, 1), [name], [name])
+    def sel(ap, pattern, cmp, fill, base, name, src=None, cm=1):
+        if src is None:
+            op("G", lambda: g.affine_select(ap, ap, pattern, cmp, fill, base, cm), [name], [name])
+        else:
+            op("G", lambda: g.affine_select(ap, src[0], pattern, cmp, fill, base, cm), [src[1]], [name])
+
+    def iota(ap, pattern, base, name):
+        op("G", lambda: g.iota(ap, pattern, base, 0, allow_small_or_imprecise_dtypes=True), [], [name])
 
     def fill(ap, val, names):
         op("V", lambda: vec.memset(ap, val), [], names)
 
-    dma("Y", T.Ci[:, 0:192], T.par[:], [], ["Ci0"])
-    dma("S", T.Ci[:, 192:384], T.jump[:], [], ["Ci1"])
+    def copyV(out, in_, r, w):
+        op("V", lambda: vec.tensor_copy(out, in_), r, w)
+
+    def ts(out, in_, s1, s2, ops, r, w):
+        op("V", lambda: vec.tensor_scalar(out, in_, s1, s2, *ops), r, w)
+
+    def tt(out, in0, in1, alu, r, w):
+        op("V", lambda: vec.tensor_tensor(out, in0, in1, alu), r, w)
+
+    def scan(out, d0, d1, op0, op1, r, w):
+        op("V", lambda: vec.tensor_tensor_scan(out, d0, d1, 0.0, op0, op1), r, w)
+
+    def actS(out, in_, func, r, w, bias=0.0, scale=1.0):
+        op("S", lambda: act.activation(out, in_, func, bias=bias, scale=scale), r, w)
+
+    def fillS(ap, val, names):
+        actS(ap, T.Ws[:, 32:32 + ap.shape[1]], F.Identity, ["zt"] + names[1:], names[:1], bias=val)
+
+    dma("Y", T.Ci[0:64, 0:384], T.par[:], [], ["Ci0"])
+    dma("S", T.Ci[64:128, 0:384], T.jump[:], [], ["Ci1"])
     dma("Y", T.u0i[:], T.u0[:], [], ["u0i"])
     dma("S", T.X[:, V0:V0 + K], T.q[:], [], ["X1"])
-    dma("Y", T.M[:, Z:Z + V0], T.m[:], [], ["M0"])
+    dma("Y", T.M[:, Z:Z + MA], T.m[:, 0:MA], [], ["M0"])
 
-    op("G", lambda: g.iota(T.pi[:], [[0, 1]], 0, 1), [], ["pi"])
-    ball = ["B%d" % k for k in range(8)]
-    wall = ["W%d" % k for k in range(10)]
     prow = ["PT0_%d" % f for f in range(11)]
     arow = ["PA_%d" % f for f in range(4)]
-    fill(T.Bm[:], 0.0, ball)
+    Wv, Wh, zt = T.Ws[:, 0:16], T.Ws[:, 16:32], (T.Ws[:, 32:160], "zt")
+    Ip, In = T.If[:, 0:128], T.If[:, 128:256]
+    pm, lastrow, pm192, pmneg, lastm1, wf = [T.cl[:, k:k + 1] for k in range(6)]
+    op("G", lambda: g.iota(T.pi[:], [[0, 1]], 0, 1), [], ["pi"])
+    fill(T.Ws[:], 0.0, ["Wv", "Wh", "zt"])
+    fill(T.Bm[:, 0:2 * BW], 0.0, ["B0", "B1"])
     fill(T.PA[:], 0.0, arow)
-    fill(T.Wm[:], 0.0, wall)
+    ts(T.pj[:], T.pi[:], 15, None, (A.bitwise_and,), ["pi"], ["pj"])
 
-    def split_hi(k):
-        op("V", lambda: vec.tensor_scalar(T.Cb[:, 384 * k:384 * k + 192], T.Ci[:, 192 * k:192 * k + 192], 16.0, 0.0, A.subtract, A.max),
-           ["Ci%d" % k], ["Cb%d" % (2 * k)])
+    def split(a, n, o, r, w):
+        ts(T.Cb[:, o:o + n], T.Ci[:, a:a + n], 16.0, 0.0, (A.subtract, A.max), r, [w + "h"])
+        tt(T.Cb[:, o + n:o + 2 * n], T.Ci[:, a:a + n], T.Cb[:, o:o + n], A.subtract, r + [w + "h"], [w + "l"])
 
-    def split_lo(k):
-        op("V", lambda: vec.tensor_tensor(T.Cb[:, 384 * k + 192:384 * k + 384], T.Ci[:, 192 * k:192 * k + 192],
-                                          T.Cb[:, 384 * k:384 * k + 192], A.subtract), ["Ci%d" % k, "Cb%d" % (2 * k)], ["Cb%d" % (2 * k + 1)])
-    split_hi(0)
-    split_hi(1)
-    split_lo(0)
-    split_lo(1)
-    for q, f in (("Y", 0), ("S", 2), ("Y", 1), ("S", 3)):
-        dma(q, T.PA[f::16, :], T.Cb[:, 192 * f:192 * f + 192], ["Cb%d" % f], ["PA_%d" % f])
-    dma("S", T.X[:, 0:V0], T.x[:], [], ["X0"])
-    dma("Y", T.Ci[:, 384:576], T.ln[:], ["Cb3"], ["Ci2"])
+    def piece(f):
+        return T.Cb[64 * (f // 2):64 * (f // 2) + 64, 384 * (f % 2):384 * (f % 2) + 384], "Cp" + "hl"[f % 2]
+    copyV(pm, T.pj[:], ["pj"], ["pm"])
+    ts(lastrow, T.pj[:], 15.0, None, (A.is_equal,), ["pj"], ["last"])
+    split(0, 384, 0, ["Ci0", "Ci1"], "Cp")
+    for f in (0, 2, 1, 3):
+        dma("Y", T.PA[f::16, :], piece(f)[0], [piece(f)[1]], ["PA_%d" % f])
+    dma("Y", T.M[:, Z + MA:Z + V0], T.m[:, MA:V0], [], ["M0b"])
+    dma("Y", T.Ci[:, 384:576], T.ln[:], [], ["Ci2"])
+    dma("Y", T.X[:, 0:V0], T.x[:], [], ["X0"])
     dma("Y", T.wi[:], T.w[:], [], ["wi"])
-    op("V", lambda: vec.tensor_copy(T.ou0[:], T.u0i[:]), ["u0i"], ["ou0"])
-    fill(T.If[:], 0.0, ["If0", "If1"])
-    fill(T.d0s[:], 0.0, ["d0s"])
-    op("V", lambda: vec.tensor_scalar(T.pj[:], T.pi[:], 15, None, A.bitwise_and), ["pi"], ["pj"])
-    fill(T.PT[:, 0:Z + V0], 0.0, prow)
-    op("V", lambda: vec.tensor_scalar(T.pm192[:], T.pj[:], 192.0, None, A.mult), ["pj"], ["pm192"])
-    op("V", lambda: vec.tensor_copy(T.pm[:], T.pj[:]), ["pj"], ["pm"])
+    copyV(T.ou0[:], T.u0i[:], ["u0i"], ["ou0"])
+    fill(T.PT[:, 0:Z + V0], 0.0, ["PTa"])
+    copyV(T.uf[:, 0:64], T.u0i[:], ["u0i"], ["uf0"])
 
-    fills = {B_ONE: [(16, 1.0), (0, 0.0)], B_DH: [(6, -0.5), (2, 0.5), (0, 0.0)], B_SH: [(6, 0.5), (0, 0.0)],
-             B_SI: [(8, -1.0), (6, 0.5), (0, 0.0)], B_J: [(6, 1.0), (2, 0.0)], B_LP: [(10, BIG), (8, 0.0)], B_LN: [(10, -BIG), (8, 0.0)]}
+    fills = {"Wv": [(16, 1.0), (0, 0.0)], "Wh": [(6, -0.5), (2, 0.5), (0, 0.0)],
+             "B0": [(16, 1.0), (0, 0.0)], "B1": [(6, 0.5), (0, 0.0)], "B2": [(8, -1.0), (6, 0.5), (0, 0.0)], "B3": [(6, 1.0), (2, 0.0)],
+             "B4": [(10, 1.0), (8, 0.0)], "B5": [(10, -1.0), (8, 0.0)],
+             "Wp": [(2, 1.0), (0, 0.0)], "Wj": [(6, 1.0), (2, 0.0)]}
+    cols = {"Wv": T.Ws[:, 0:16:2], "Wh": T.Ws[:, 16:32:2], "Wp": T.Wo[:, 7:71:8], "Wj": T.Wo[:, 71:135:8]}
+    for k in range(6):
+        cols["B%d" % k] = T.Bm[:, k * BW + 15:k * BW + 143:16]
 
     def bfill(ks):
         for lvl in range(3):
             for k in ks:
                 if lvl < len(fills[k]):
                     top, val = fills[k][lvl]
-                    sel(T.Bm[:, k * BW + 15:k * BW + 143:16], [[-16, 8]], A.is_ge, val, -top, "B%d" % k)
-    bfill([B_ONE, B_DH, B_SH])
-    op("G", lambda: g.iota(T.idt[:], [[64, 3], [0, 64]], 0, 0, allow_small_or_imprecise_dtypes=True), [], ["idt"])
-    op("G", lambda: g.iota(T.Ct[:], [[16, 64]], K, 0, allow_small_or_imprecise_dtypes=True), [], ["Ct"])
-    op("G", lambda: g.iota(T.Cb[:, 1344:1536], [[0, 3], [1, 64]], 0, 0, allow_small_or_imprecise_dtypes=True), [], ["Cb7"])
-    op("G", lambda: g.iota(T.Cb[:, 1536:1728], [[0, 192]], 1, 0, allow_small_or_imprecise_dtypes=True), [], ["Cb8"])
-    sel(Wk(W_I), [[-1, 128]], A.not_equal, 1.0, 0, "W%d" % W_I)
-    sel(Wk(W_NI), [[-1, 128]], A.not_equal, -1.0, 0, "W%d" % W_NI)
-    sel(T.If[:, 0:128], [[-1, 128]], A.not_equal, 1.0, 0, "If0")
-    sel(T.If[:, 128:256], [[-1, 128]], A.not_equal, -1.0, 0, "If1")
-    sel(Wk(W_N128), [[-1, 128]], A.not_equal, -128.0, 0, "W%d" % W_N128)
-    sel(Wk(W_ONE), [[-16, 8], [0, 16]], A.is_ge, 1.0, -16, "W%d" % W_ONE)
-    sel(Wk(W_NU), [[-16, 8], [0, 16]], A.is_ge, -1.0, -16, "W%d" % W_NU)
-    sel(Wk(W_ONE), [[-16, 8], [0, 16]], A.is_ge, 0.0, 0, "W%d" % W_ONE)
-    sel(Wk(W_NU), [[-1, 128]], A.is_ge, 0.0, 0, "W%d" % W_NU)
+                    sel(cols[k], [[-16, 8]], A.is_ge, val, -top, k)
     ents = {W_ID0: [(6, 6, 1.0), (7, 7, 1.0), (10, 6, float(V0))],
             W_P: [(6, 0, 1.0), (7, 1, 1.0), (6, 4, 1.0), (7, 5, 1.0), (10, 9, 1.0), (10, 10, 1.0)],
             W_J: [(2, 2, 1.0), (3, 3, 1.0), (4, 2, 1.0), (5, 3, 1.0), (8, 8, 2.0), (9, 9, 2.0), (10, 4, -BIG), (10, 5, -BIG)],
@@ -222,82 +255,121 @@ def rank_program(g, core, T, topo):
             for k in ks:
                 if lvl < len(ents[k]):
                     f, f2, val = ents[k][lvl]
-                    sel(T.Wm[:, k * 128 + f2:(k + 1) * 128:16], [[-16, 8]], A.not_equal, val, -f, "W%d" % k)
-    bfill([B_J, B_LP, B_LN])
-    wfill([W_ID0, W_P])
-    wfill([W_J, W_ID1])
-    Wo = T.Wm[:, 1152:1168]
-    sel(T.Wm[:, 1152:1160], [[-16, 8]], A.is_ge, 1.0, -2, "W9")
-    sel(T.Wm[:, 1160:1168], [[-16, 8]], A.is_ge, 1.0, -6, "W9")
-    sel(T.Wm[:, 1152:1160], [[-16, 8]], A.is_ge, 0.0, 0, "W9")
-    sel(T.Wm[:, 1160:1168], [[-16, 8]], A.is_ge, 0.0, -2, "W9")
-    bfill([B_SI])
-    Ip, In = T.If[:, 0:128], T.If[:, 128:256]
+                    sel(T.Wm[:, k * 128 + f2:(k + 1) * 128:16], [[-16, 8]], A.not_equal, val, -f, wn(k))
 
-    op("V", lambda: vec.tensor_scalar(T.Cb[:, 1152:1344], T.idt[:], T.pm192[:], None, A.add), ["idt", "pm192"], ["Cb6"])
-    fill(T.d0g[:], 0.0, ["ng0", "ng1", "ng2"])
-    op("V", lambda: vec.tensor_copy(T.u0f[:], T.u0i[:]), ["u0i"], ["u0f"])
-    fill(T.fb[:], 0.0, ["fb", "fc"])
-    fill(T.one64[:], 1.0, ["one64"])
-    fill(T.send[:, 0:16 + CAP], 0.0, ["sendh", "sendw"])
-    op("V", lambda: vec.tensor_scalar(T.Cf[:], T.Ct[:], T.pm[:], None, A.add), ["Ct", "pm"], ["Cf"])
-    fill(T.M[:, 0:Z], 0.0, ["Mz"])
-    fill(T.hb[:], 0.0, ["hb"])
+    def zeros(buf, a, b, names):
+        for c in range(a, b, CAP):
+            actS(buf[:, c:min(c + CAP, b)], T.Ws[:, 32:32 + min(CAP, b - c)], F.Identity, ["zt"], names)
+    zeros(T.Bm, 2 * BW, 7 * BW, ["B%d" % k for k in range(2, 7)])
+    zeros(T.Wm, 0, 512, [wn(k) for k in range(4)])
+    zeros(T.Wo, 0, 136, ["Wp", "Wj"])
+    bfill(["Wv", "Wh"])
+    sel(Wk(W_I), [[-1, 128]], A.not_equal, 1.0, 0, wn(W_I), zt)
+    bfill(["B1", "B0"])
+    fillS(T.tu[:, 0:8], 0.0, ["tuz"])
+    fillS(T.six[:, 0:CV], 0.0, ["sixa"])
+    fillS(T.six[:, CV:64], 6.0, ["sixb"])
+    actS(pm192, pm, F.Identity, ["pm"], ["pm192"], scale=192.0)
+    actS(Ip, Wk(W_I), F.Identity, [wn(W_I)], ["If0"])
+    actS(Wk(W_NI), Wk(W_I), F.Identity, [wn(W_I)], [wn(W_NI)], scale=-1.0)
+    iota(T.idt[:], [[64, 3], [0, 64]], 0, "idt")
+    iota(T.Cb[:, 1344:1536], [[0, 3], [1, 64]], 0, "Cb7")
+    fillS(T.Cb[:, 1536:1728], 1.0, ["Cb8"])
+    actS(T.Cb[:, 1152:1344], T.idt[:], F.Identity, ["idt", "pm192"], ["Cb6"], bias=pm192)
+    actS(In, Wk(W_I), F.Identity, [wn(W_I)], ["If1"], scale=-1.0)
+    actS(Wk(W_N128), Wk(W_I), F.Identity, [wn(W_I)], [wn(W_N128)], scale=-128.0)
+    fillS(T.d0g[:], 0.0, ["n0"])
+    lastw["n1"] = lastw["n2"] = lastw["n0"]
+    fillS(T.d0m[:], 1.0, ["d0m"])
+    actS(pmneg, pm, F.Identity, ["pm"], ["pmneg"], scale=-16384.0)
+    actS(lastm1, lastrow, F.Identity, ["last"], ["lastm1"], bias=-1.0)
+    actS(T.zs[:], lastrow, F.Identity, ["last"], ["zs"], bias=-1.0, scale=17.0)
+    fillS(T.d0m[:, 0::32], 0.0, ["d0m"])
+    fillS(T.one64[:], 1.0, ["one64"])
+    fillS(T.Sc[:, 0:8], 0.0, ["Scz"])
+    fillS(T.cnt[:], 0.0, ["cnt"])
+    block = [[-16, 8], [0, 16]]
+    iota(T.Ct[:], [[16, 64]], CAP, "Ct")
+    iota(T.col[:], [[1, 64]], 0, "col")
+    iota(Wk(W_MK), [[0, 4], [1, 16], [0, 2]], 0, wn(W_MK))
+    sel(Wk(W_ONE), block, A.is_ge, 1.0, -16, wn(W_ONE), zt)
+    sel(Wk(W_NU), block, A.is_ge, -1.0, -16, wn(W_NU), zt)
+    sel(Wk(W_ONE), block, A.is_ge, 0.0, 0, wn(W_ONE))
+    sel(Wk(W_NU), [[-1, 128]], A.is_ge, 0.0, 0, wn(W_NU))
+    iota(T.far[:], [[16, 64]], K, "far")
+    sel(Wk(W_TRI), [[1, 128]], A.is_ge, 0.0, 0, wn(W_TRI), (Wk(W_ONE), wn(W_ONE)), -1)
+    sel(Wk(W_NF), [[-1, 128]], A.not_equal, -512.0, 0, wn(W_NF), (Wk(W_NU), wn(W_NU)))
+    sel(T.Wm[:, W_TRI * 128 + 15:(W_TRI + 1) * 128:16], [[0, 8]], A.is_gt, 0.0, 0, wn(W_TRI), None, 0)
+    bfill(["B3", "B4", "B5"])
+    wfill([W_ID0, W_P, W_J, W_ID1])
 
-    def row(f, blk):
-        dma("Y", T.PT[f::16, Z:Z + V0], T.Cb[:, 192 * blk:192 * blk + 192], ["Cb%d" % blk, "X0"], ["PT0_%d" % f])
+    def row(f, src, name):
+        dma("Y", T.PT[f::16, Z:Z + V0], src, [name, "X0", "PTa"], ["PT0_%d" % f])
 
-    def late_constants(s):
-        if s == 0:
-            fill(T.tab0[:, 16 + CAP:16 + K], 0.0, ["gap0"])
-            split_hi(2)
-            op("V", lambda: vec.tensor_copy(T.wf[:], T.wi[:]), ["wi"], ["wf"])
-            split_lo(2)
-            op("V", lambda: vec.tensor_scalar(T.Bm[:, B_W * BW + 15:B_W * BW + 143:16], T.Bm[:, 15:143:16], T.wf[:], None, A.mult),
-               ["B0", "wf"], ["B%d" % B_W])
-            for f, blk in ((0, 0), (1, 1), (2, 2), (3, 3), (6, 6), (7, 7), (10, 8), (8, 4), (9, 5)):
-                row(f, blk)
-        if s == 3:
-            fill(T.tab1[:, 16 + CAP:16 + K], 0.0, ["gap1"])
-        if s == 4:
-            fill(T.d0f[:], 0.0, ["d0f1", "nf0", "nf1", "nf2"])
+    def late(n):
+        if n == 0:
+            split(384, 192, 768, ["Ci2"], "Cl")
+            for f in range(4):
+                row(f, *piece(f))
+            for f, c, name in ((6, 1152, "Cb6"), (7, 1344, "Cb7"), (10, 1536, "Cb8"), (8, 768, "Clh"), (9, 960, "Cll")):
+                row(f, T.Cb[:, c:c + 192], name)
+            remote(T.qp0[:], T.X[:, V0:V0 + K], "q0", ["X1"] + prow, "qp0")
+            bfill(["Wp", "Wj", "B2"])
+        if n == 1:
+            actS(Wk(W_MK), Wk(W_MK), F.Abs, [wn(W_MK), "pmneg"], [wn(W_MK)], bias=pmneg, scale=16384.0)
+            actS(T.Cf[:], T.Ct[:], F.Identity, ["Ct", "pm"], ["Cf"], bias=pm)
+            actS(T.c15[:], T.col[:], F.Identity, ["col", "last"], ["c15"], scale=lastrow)
+            fillS(T.dn[:], lastm1, ["dn", "lastm1"])
+            fillS(T.Wd[:, 0:CAP], 0.0, ["Wd0"])
+            actS(Wk(W_N4K), Wk(W_ONE), F.Identity, [wn(W_ONE)], [wn(W_N4K)], scale=-4096.0)
+        if n == 2:
+            fillS(T.hb[:], 0.0, ["hb"])
+            fillS(T.M[:, 0:Z], 0.0, ["Mz"])
+            copyV(wf, T.wi[:], ["wi"], ["wf"])
+        if n == 3:
+            actS(T.Bm[:, B_W * BW + 15:B_W * BW + 143:16], T.Bm[:, 15:143:16], F.Identity, ["B0", "wf"], ["B%d" % B_W], scale=wf)
+        if n == 4:
+            fillS(T.Wd[:, WD:WD + CAP], 0.0, ["Wd1"])
 
-    def emit_out_mm(t, h):
-        o = V0 + K * t
-        mm(T.pw1[0:16, 512 * h:512 * h + 512], Wo, T.PT[:, Z + o + 512 * h:Z + o + 512 * h + 512], True, True,
-           ["W9", "PT%d_%d" % (t + 1, h)], ["pw1" + "ab"[h]])
+    def out_mm(t, h):
+        def fn():
+            for a in range(4 * h, 4 * h + 4):
+                c = Z + V0 + K * t + 128 * a
+                ins = pe.matmul(T.pw1[:, 0:128], T.Wo[:, 7 - a:135 - a], T.PT[:, c:c + 128], a == 0, a == 7)
+            return ins
+        op("P", fn, ["Wp", "Wj", "PT%d_%d" % (t + 1, h)], ["pw1a"])
 
-    def emit_out_copy(t, h):
-        a, b = 512 * h, 512 * h + 512
-        op("S", lambda: act.activation(T.yo[0:16, a:b], T.pw1[0:16, a:b], F.Identity), ["pw1" + "ab"[h]], ["yo%d" % h])
+    def out_store(t, q):
+        actS(T.yo[:], T.pw1[:, 0:128], F.Identity, ["pw1a"], ["yo"])
+        dma(q, T.ypar[:, K * t:K * t + K], T.yo[0:64, :], ["yo"], [])
+        dma(q, T.yjump[:, K * t:K * t + K], T.yo[64:128, :], ["yo"], [])
 
-    def emit_out_dma(t, q):
-        dma(q, T.ypar[:, K * t:K * t + K], T.yo[0:8, :], ["yo0", "yo1"], [])
-        dma(q, T.yjump[:, K * t:K * t + K], T.yo[8:16, :], ["yo0", "yo1"], [])
-
-    CV = 64 - CS
     LV = 16 * CV
 
     for t in range(RO):
         o = V0 + K * t
         last = t == RO - 1
         rX = ["X%d" % k for k in range(t + 1)]
-        rM = ["M0"] + ["M%d_%d" % (k, h) for k in range(1, t + 1) for h in (0, 1)]
-        rP = prow + ["PT%d_%d" % (k, h) for k in range(1, t + 1) for h in (0, 1)]
+        rM = ["M0", "M0b"] + ["M%d_%d" % (k, h) for k in range(1, t + 1) for h in (0, 1)]
+        rP = prow + ["PTa"] + ["PT%d_%d" % (k, h) for k in range(1, t + 1) for h in (0, 1)]
         rq = ["X%d" % (t + 1)]
         if t > 0:
             rX = rX + ["X%db" % k for k in range(2, t + 1)]
             rq = rq + ["X%db" % (t + 1)]
         ask = T.X[:, o:o + K]
         offs = [T.ou0, T.ou1, T.ou2, T.ou3]
-        scans = [T.su1, T.su2, T.su3]
         cx = [T.cx0, T.cx1]
         pg = [T.pg0, T.pg1]
-        nn = ["nf0", "nf1", "nf2"] if last else ["ng0", "ng1", "ng2"]
-        u1, u2, u3 = T.su1[:, 1::2], T.su2[:, 1::2], T.su3[:, 1::2]
+        nn = ["n0", "n1", "n2"]
+
+        def uf(s):
+            return T.uf[:, 64 * s:64 * s + 64]
 
         def nap(s):
-            return T.d0f[:, 4 - s::5] if last else T.d0g[:, 3 - s::4]
+            return T.d0g[:, 3 - s::4]
+
+        def quarters(name, a, b):
+            return ["%s%d" % (name, k) for k in range(a // 4, b // 4)]
 
         def wins(s):
             a = o - K if (s == 0 and t > 0) else 0
@@ -312,231 +384,270 @@ def rank_program(g, core, T, topo):
         def m_test(s):
             gT(T.cm[:], wins(s)[1], offs[s][:], ask, A.is_ge, rM + rq + ["ou%d" % s], ["cm"])
 
-        def x_vec(s):
-            gT(cx[s % 2][:, 0:LV], wins(s)[0], offs[s][:, 0:CV], T.X[:, o:o + LV], A.is_ge, rX + rq + ["ou%d" % s], ["cx%da" % (s % 2)])
+        def x_vec(s, a, b):
+            gT(cx[s % 2][:, 16 * a:16 * b], wins(s)[0], offs[s][:, a:b], T.X[:, o + 16 * a:o + 16 * b], A.is_ge, rX + rq + ["ou%d" % s],
+               quarters("cx%d_" % (s % 2), a, b))
 
         def x_get(s):
             gS(T.gy[:], wins(s)[0], offs[s][:, CV:64], rX + ["ou%d" % s], ["gy"])
 
         def x_diff():
-            mm(T.pw0[:, 0:K - LV], Wk(W_NI), T.X[:, o + LV:o + K], True, False, rq + ["W%d" % W_NI], ["pw0a"])
-            mm(T.pw0[:, 0:K - LV], Wk(W_I), T.gy[:], False, True, ["gy", "W%d" % W_I], ["pw0a"])
+            mw(T.pw0[:, 0:K - LV], W_NI, T.X[:, o + LV:o + K], True, False, rq, ["pw0a"])
+            mw(T.pw0[:, 0:K - LV], W_I, T.gy[:], False, True, ["gy"], ["pw0a"])
 
         def x_sign(s):
-            op("S", lambda: act.activation(cx[s % 2][:, LV:K], T.pw0[:, 0:K - LV], F.Sign, bias=0.5), ["pw0a"], ["cx%db" % (s % 2)])
+            actS(cx[s % 2][:, LV:K], T.pw0[:, 0:K - LV], F.Sign, ["pw0a"], quarters("cx%d_" % (s % 2), CV, 64), bias=0.5)
 
         def votes_x(s, bank, bn, start=True):
-            extract(bank[:, 0:64], B_ONE, cx[s % 2], ["cx%da" % (s % 2), "cx%db" % (s % 2)], [bn], start=start)
+            mw(bank[:, 0:64], W_I, T.six[:], start, False, ["sixa", "sixb"], [bn])
+            extract(bank[:, 0:64], B_ONE, cx[s % 2], quarters("cx%d_" % (s % 2), 0, 64), [bn], start=False)
 
-        def stays(s, bank, bn):
-            op("S", lambda: act.activation(T.na[:, 0:CV], bank[:, 0:CV], F.Relu, bias=-9.0), [bn], ["naa"])
-            op("S", lambda: act.activation(T.na[:, CV:64], bank[:, CV:64], F.Relu, bias=-2.0), [bn], ["nab"])
-            op("S", lambda: act.activation(nap(s), T.na[:], F.Relu, bias=1.0, scale=-1.0), ["naa", "nab"], [nn[s]])
+        def stays(s):
+            actS(T.na[:], T.pd[:, 0:64], F.Relu, ["pd"], ["na"], bias=-9.0)
+            actS(nap(s), T.na[:], F.Relu, ["na"], [nn[s]], bias=1.0, scale=-1.0)
 
-        def walk_pe(s):
-            extract(T.pb[:, 0:64], B_ONE, T.cm, ["cm"], ["pb"])
-            op("S", lambda: act.activation(T.d0s[:, 1::2], T.pb[:, 0:64], F.Sign, bias=-9.5), ["pb"], ["d0s"])
-            extract(T.pa[:, 0:128:2], B_DH, pg[s % 2], ["pg%d" % (s % 2)], ["pa"])
-            extract(T.pa[:, 1:128:2], B_SH, pg[s % 2], ["pg%d" % (s % 2)], ["pa"])
+        def differences():
+            for a, (p, m) in enumerate(((2, 1), (1, 0))):
+                mm(T.pw1[:, 513 + a:768:4], Ip, uf(p), True, False, ["If0", "uf%d" % p], ["pw1b"])
+                mm(T.pw1[:, 513 + a:768:4], In, uf(m), False, True, ["If1", "uf%d" % m], ["pw1b"])
+            mm(T.pw1[:, 515:768:4], Ip, uf(0), True, True, ["If0", "uf0"], ["pw1b"])
 
-        def walk_v(s):
-            sn = "su%d" % (s + 1)
-            op("V", lambda: vec.tensor_tensor_scan(scans[s][:], T.d0s[:], T.pa[:, 0:128], 0.0, A.mult, A.add), ["d0s", "pa"], [sn])
-            op("V", lambda: vec.tensor_copy(offs[s + 1][:], scans[s][:, 1::2]), [sn], ["ou%d" % (s + 1)])
+        def turn_back(out, bn):
+            mm(out, T.tu[:, 8:136], T.If[:, 0:128:2], False, False, ["tu", "If0"], [bn])
+            mm(out, T.tu[:, 0:128], T.If[:, 1:128:2], False, True, ["tu", "tuz", "If0"], [bn])
 
-        def differences(buf, c0, bn, rec, at):
-            a, e = c0 + at, c0 + 64 * rec
-            mm(buf[:, a:e:rec], Ip, u2, True, False, ["If0", "su2"], [bn])
-            mm(buf[:, a:e:rec], In, u1, False, True, ["If1", "su1"], [bn])
-            mm(buf[:, a + 1:e:rec], Ip, u1, True, False, ["If0", "su1"], [bn])
-            mm(buf[:, a + 1:e:rec], In, T.u0f[:], False, True, ["If1", "u0f"], [bn])
-            mm(buf[:, a + 2:e:rec], Ip, T.u0f[:], True, True, ["If0", "u0f"], [bn])
+        def choose_p():
+            scan(T.sp[:], T.d0g[:], T.pw1[:, 512:768], A.mult, A.add, nn + ["pw1b"], ["sp"])
+            copyV(T.op[:], T.sp[:, 3::4], ["sp"], ["op"])
 
-        for s in range(2 if last else 3):
+        for s in range(3):
+            final = last and s == 2
+            first = t == 0 and s == 0
+            pn = "pg%d" % (s % 2)
+            gaps = [[(s, 0, C1)], [(s, C1, CV)]]
+            if t == 0 and s < 2:
+                gaps = [[[], [(0, 0, 32)]], [[(0, 32, CV), (1, 0, 24)], [(1, 24, CV)]]][s]
+            if s == 2:
+                actS(uf(2), T.pc[:, 0:64], F.Identity, ["pc"], ["uf2"])
             pointers(s)
             m_test(s)
-            if s > 0:
-                votes_x(s - 1, T.pc, "pc")
-            if t > 0 and s < 2:
-                emit_out_mm(t - 1, s)
+            if t == 1 and s == 0:
+                remote(T.qp1[:], ask, "q1", rq, "qp1")
+            if s > 0 and not (t == 0 and s == 1):
+                votes_x(s - 1, T.pd, "pd")
+            if t > 0 and s == 0:
+                out_mm(t - 1, 0)
+                out_mm(t - 1, 1)
             if s == 2:
-                differences(T.pw1, 512, "pw1b", 4, 1)
-                mm(T.pw1[:, 512:768:4], In, u2, True, False, ["If1", "su2"], ["pw1b"])
-            if t == 0 and s == 0:
-                late_constants(0)
-            x_get(s)
-            x_vec(s)
-            if s == 0 and t > 0:
-                op("V", lambda: vec.tensor_scalar(T.u0f[:], T.h1[:], float(o - K), None, A.add), ["h1"], ["u0f"])
-            if t == 1:
-                late_constants(3 + s)
-            walk_pe(s)
-            x_diff()
-            if s > 0:
-                stays(s - 1, T.pc, "pc")
-            if t > 0 and s < 2:
-                emit_out_copy(t - 1, s)
-                if s == 1:
-                    emit_out_dma(t - 1, "Y")
+                differences()
+                if not final:
+                    mm(T.pw1[:, 512:768:4], In, uf(2), True, False, ["If1", "uf2"], ["pw1b"])
+            turn(T.pa, Wv, T.cm, ["cm", "Wv"], ["pa"])
+            turn(T.pb, Wh, pg[s % 2], [pn, "Wh"], ["pb"])
+            if first:
+                late(1)
+            else:
+                x_get(s)
+            for x in gaps[0]:
+                x_vec(*x)
+            actS(T.sg[:], T.pa[:, 0:128], F.Sign, ["pa"], ["sg"], bias=-9.5)
+            if first:
+                late(0)
+                x_get(s)
+            if t < 2 and s == 1:
+                late(2 + 2 * t)
+            if final:
+                extract(T.pw1[:, 512:768:4], B_SI, pg[s % 2], [pn], ["pw1b"], stop=False)
+            else:
+                extract(T.pc[:, 0:64], B_SH, pg[s % 2], [pn], ["pc"], stop=False)
+            tt(T.tu[:, 8:136], T.pb[:, 0:128], T.sg[:], A.mult, ["pb", "sg"], ["tu"])
+            if not first:
+                x_diff()
+            if final:
+                turn_back(T.pw1[:, 512:768:4], "pw1b")
+            else:
+                turn_back(T.pc[:, 0:64], "pc")
+            if first:
+                x_diff()
+            if s > 0 and not (t == 0 and s == 1):
+                stays(s - 1)
             x_sign(s)
-            walk_v(s)
+            if t > 0 and s == 0:
+                out_store(t - 1, "Y")
+            for x in gaps[1]:
+                x_vec(*x)
+            if t == 0 and s == 1:
+                votes_x(0, T.pd, "pd")
+                stays(0)
+            if s == 0 and t > 0:
+                ts(uf(0), T.h1[:], float(o - K), None, (A.add,), ["h1"], ["uf0"])
+            if s == 1:
+                copyV(uf(1), offs[1][:], ["ou1"], ["uf1"])
+            if not final:
+                copyV(offs[s + 1][:], T.pc[:, 0:64], ["pc"], ["ou%d" % (s + 1)])
 
         wx, wm, wp = wins(2)
         wz_m, wz_p = T.M[:, 0:Z + o], T.PT[:, 0:Z + o]
+        pf = T.sp[:, 3::4]
 
-        def pick_zero():
-            op("S", lambda: act.activation(T.ad[:, 0:64], T.pb[:, 0:64], F.Abs), ["pb"], ["ada"])
-            op("S", lambda: act.activation(T.ad[:, 64:128], T.pb[:, 0:64], F.Abs), ["pb"], ["adb"])
-
-        def pick_a():
-            op("V", lambda: vec.tensor_tensor(T.yy[:], T.pa[:, 0:128], T.ad[:], A.subtract), ["pa", "ada", "adb"], ["yy"])
-
-        def pick_b():
-            op("V", lambda: vec.tensor_scalar(T.opj[:], T.yy[:], float(Z), None, A.add), ["yy"], ["opj"])
+        def pick():
+            ts(T.ad[:], T.pa[:, 0:64], 0.0, BIG, (A.not_equal, A.mult), ["pa"], ["ad"])
+            for h in (0, 1):
+                tt(T.yy[:, 64 * h:64 * h + 64], T.pd[:, 64 * h:64 * h + 64], T.ad[:], A.subtract, ["pd", "ad"], ["yy" + "ab"[h]])
+            ts(T.opj[:], T.yy[:], float(Z), None, (A.add,), ["yya", "yyb"], ["opj"])
 
         def half(h):
             return slice(512 * h, 512 * h + 512)
 
-        if not last:
-            tab = T["tab%d" % t]
-            x_get(3)
-            x_vec(3)
-            votes_x(2, T.pd, "pd")
-            mm(T.pw1[:, 512:768:4], Ip, u3, False, True, ["If0", "su3"], ["pw1b"])
-            x_diff()
-            stays(2, T.pd, "pd")
-            x_sign(3)
-            for s in range(3):
-                mm(T.pc[:, 0:64], Wk(W_N128), nap(s), s == 0, False, [nn[s], "W%d" % W_N128], ["pc"])
-            op("V", lambda: vec.tensor_tensor_scan(T.sp[:, 0:256], T.d0g[:], T.pw1[:, 512:768], 0.0, A.mult, A.add), nn + ["pw1b"], ["sp"])
-            pf = T.sp[:, 3:256:4]
-            op("V", lambda: vec.tensor_copy(T.op[:], pf), ["sp"], ["op"])
-            votes_x(3, T.pc, "pc", start=False)
-            mm(T.pd[:, 1:128:2], Ip, T.Cf[:], True, True, ["If0", "Cf"], ["pd"])
-            mm(T.pd[:, 0:128:2], In, T.Cf[:], True, False, ["If1", "Cf"], ["pd"])
-            gS(T.pgp[:], wp, T.op[:], rP + ["op"], ["pgp0", "pgp1"])
-            op("V", lambda: vec.tensor_scalar(T.fb[:, 1:2 * CV:2], T.pc[:, 0:CV], 9.5 - 384.0, None, A.is_lt), ["pc"], ["fb"])
-            op("V", lambda: vec.tensor_scalar(T.fb[:, 2 * CV + 1::2], T.pc[:, CV:64], 3.0 - 384.0, None, A.is_lt), ["pc"], ["fc"])
-            op("V", lambda: vec.tensor_tensor_scan(T.Sc[:], T.one64[:], T.fb[:, 1::2], 0.0, A.mult, A.add), ["one64", "fb", "fc"], ["Sc"])
-            mm(T.pd[:, 0:128:2], Wk(W_NU), T.fb[:, 1::2], False, False, ["fb", "fc", "W%d" % W_NU], ["pd"])
-            mm(T.pd[:, 0:128:2], Wk(W_ONE), T.Sc[:], False, True, ["Sc", "W%d" % W_ONE], ["pd"])
-            mm(T.pc[:, 64:65], Wk(W_ONE), T.Sc[:, 63:64], True, True, ["Sc", "W%d" % W_ONE], ["pc"])
-            mm(T.pa[:, 0:64], Ip, pf, True, True, ["If0", "sp"], ["pa"])
-            for h in (0, 1):
-                mm(T.pw1[:, half(h)], Wk(W_ID0 + t), T.PT[:, Z + 512 * h:Z + 512 * h + 512], True, False,
-                   prow + ["W%d" % (W_ID0 + t)], ["pw1" + "ab"[h]])
-            extract(T.pa[:, 64:128], B_J, T.pgp, ["pgp0", "pgp1"], ["pa"])
-            gS(T.gx[:, half(0)], wx, T.op[:, 0:32], rX + ["op"], ["gxa"])
-            op("V", lambda: vec.tensor_tensor_scan(T.spos[:], T.fb[:], T.pd[:, 0:128], 0.0, A.mult, A.add), ["fb", "fc", "pd"], ["spos"])
-            op("V", lambda: vec.tensor_scalar(T.send[:, 15:16], T.pc[:, 64:65], float(CAP), 192.0, A.min, A.subtract), ["pc"], ["sendh"])
-            remote(tab[:, 0:16], T.send[:, 0:16], "h%d" % t, ["sendh"], "landh%d" % t)
-            op("V", lambda: vec.tensor_copy(T.opos[:], T.spos[:, 1::2]), ["spos"], ["opos"])
-            op("V", lambda: vec.tensor_copy(T.send[:, 16:16 + 2 * K].indirect(T.opos[:, 0:SC0]), T.X[:, o:o + 16 * SC0]), rq + ["opos"], ["sendw"])
-            op("V", lambda: vec.tensor_copy(T.oj[:], T.pa[:, 64:128]), ["pa"], ["oj"])
-            op("V", lambda: vec.tensor_copy(T.send[:, 16:16 + 2 * K].indirect(T.opos[:, SC0:64]), T.X[:, o + 16 * SC0:o + K]), rq + ["opos"], ["sendw"])
-            remote(tab[:, 16:16 + CAP], T.send[:, 16:16 + CAP], "d%d" % t, ["sendw"], "land%d" % t)
-            extract(T.pb[:, 0:64], B_LP, T.pgp, ["pgp0", "pgp1"], ["pb"], stop=False)
-            gS(T.pgj[:], wp, T.oj[:], rP + ["oj"], ["pgj0", "pgj1"])
-            for h in (0, 1):
-                mm(T.pw1[:, half(h)], Wk(W_P), T.pgp[:, half(h)], False, False, ["pgp0", "pgp1", "W%d" % W_P], ["pw1" + "ab"[h]])
+        def part(gather, name, win, off, a, b, r, c0=0):
+            gather(T[name][:, 16 * a:16 * b], win, off[:, c0 + a:c0 + b], r, quarters(name, a, b))
 
-            def sums(h, more):
-                b = "pw0" + "ab"[h]
-                mm(T.pw0[:, half(h)], Wk(W_I), T.X[:, o + 512 * h:o + 512 * h + 512], True, False, rq + ["W%d" % W_I], [b])
-                mm(T.pw0[:, half(h)], Wk(W_I), T.gx[:, half(h)], False, not more, ["gx" + "ab"[h]], [b])
-                if more:
-                    mm(T.pw0[:, half(h)], Wk(W_N128), T.ge[:, half(h)], False, True, ["ge%d" % h, "W%d" % W_N128], [b])
+        def whole(name):
+            return quarters(name, 0, 64)
+
+        def halfof(name, h):
+            return quarters(name, 32 * h, 32 * h + 32)
+
+        if not last:
+            x_get(3)
+            actS(uf(3), T.pc[:, 0:64], F.Identity, ["pc"], ["uf3"])
+            x_vec(3, 0, CV)
+            votes_x(2, T.pd, "pd")
+            x_diff()
+            mm(T.pw1[:, 512:768:4], Ip, uf(3), False, True, ["If0", "uf3"], ["pw1b"])
+            stays(2)
+            x_sign(3)
+            mm(T.pc[:, 1:128:2], Ip, T.Cf[:], True, True, ["If0", "Cf"], ["pc"])
+            mw(T.pb[:, 0:128], W_NI, Wk(W_MK), True, False, [wn(W_MK)], ["pb"])
+            mw(T.pb[:, 1:128:2], W_I, T.far[:], False, False, ["far"], ["pb"])
+            for s in range(3):
+                mw(T.pa[:, 0:64], W_N128, nap(s), s == 0, False, [nn[s]], ["pa"])
+            choose_p()
+            votes_x(3, T.pa, "pa", start=False)
+            if t == 0:
+                late(3)
+            part(gS, "pgp", wp, T.op, 16, 64, rP + ["op"])
+            part(gV, "pgp", wp, T.op, 0, 8, rP + ["op"])
+            ts(T.fb[:], T.pa[:, 0:64], 9.5 - 384.0, None, (A.is_lt,), ["pa"], ["fb"])
+            scan(T.Sc[:, 8:72], T.one64[:], T.fb[:], A.mult, A.add, ["one64", "fb"], ["Sc"])
+            incl, excl = T.Sc[:, 8:72], T.Sc[:, 7:71]
+            mw(T.pa[:, 0:64], W_I, T.c15[:], True, False, ["c15"], ["pa"])
+            mw(T.pa[:, 0:64], W_TRI, T.fb[:], False, True, ["fb"], ["pa"])
+            mw(T.pb[:, 1:128:2], W_N4K, T.fb[:], False, False, ["fb"], ["pb"])
+            mw(T.pb[:, 0:128:2], W_ONE, excl, False, False, ["Sc", "Scz"], ["pb"])
+            mw(T.pb[:, 1:128:2], W_ONE, excl, False, True, ["Sc", "Scz"], ["pb"])
+            mw(T.pc[:, 256:257], W_ONE, T.Sc[:, 71:72], True, True, ["Sc"], ["pc"])
+            part(gV, "pgp", wp, T.op, 8, 16, rP + ["op"])
+            copyV(T.Rk[:], T.pa[:, 0:64], ["pa"], ["Rk"])
+            scan(T.sst[:], T.d0m[:], T.pb[:, 0:128], A.mult, A.max, ["d0m", "pb"], ["sst"])
+            ts(T.cnt[:, 15:16], T.pc[:, 256:257], float(CAP), 192.0, (A.min, A.subtract), ["pc"], ["cnt"])
+            remote(T["got%d" % t][:], T.cnt[:], "h%d" % t, ["cnt"], "got%d" % t)
+            copyV(T.ost[:], T.sst[:, 31::32], ["sst"], ["ost"])
+            mm(T.pd[:, 0:64], Ip, pf, True, True, ["If0", "sp"], ["pd"])
+            extract(T.pd[:, 64:128], B_J, T.pgp, whole("pgp"), ["pd"])
+            part(gS, "gx", wx, T.op, 0, GX, rX + ["op"])
+            op("V", lambda: vec.tensor_copy(T.Wd[:, WD * t:WD * t + WD].indirect(T.ost[:]), T.Rk[:]), ["Rk", "ost"], ["Wd%d" % t])
+            copyV(T.oj[:], T.pd[:, 64:128], ["pd"], ["oj"])
+            scan(T.Zr[:], T.Wd[:, WD * t:WD * t + CAP], T.dn[:], A.max, A.add, ["Wd%d" % t, "dn"], ["Zr"])
+            ts(T.Zc[:], T.Zr[:], T.zs[:], 0.0, (A.mult, A.max), ["Zr", "zs"], ["Zc"])
+            mm(T.pc[:, 0:128:2], In, T.Cf[:], True, False, ["If1", "Cf"], ["pc"])
+            mw(T.pc[:, 0:128:2], W_NU, T.fb[:], False, False, ["fb"], ["pc"])
+            mw(T.pc[:, 0:128:2], W_ONE, incl, False, True, ["Sc"], ["pc"])
+            mw(T.pc[:, 128:192], W_NF, T.fb[:], True, False, ["fb"], ["pc"])
+            mw(T.pc[:, 128:192], W_ONE, incl, False, True, ["Sc"], ["pc"])
+
+            def sums(bank, bn, h, stop):
+                mw(bank[:, half(h)], W_I, T.X[:, o + 512 * h:o + 512 * h + 512], True, False, rq, [bn + "ab"[h]])
+                mw(bank[:, half(h)], W_I, T.gx[:, half(h)], False, stop, halfof("gx", h), [bn + "ab"[h]])
 
             def wraps(h):
-                op("S", lambda: act.activation(T.ge[:, half(h)], T.pw0[:, half(h)], F.Sign, bias=t - 255.5), ["pw0" + "ab"[h]], ["ge%d" % h])
+                actS(T.ge[:, half(h)], T.pw0[:, half(h)], F.Sign, ["pw0" + "ab"[h]], ["ge%d" % h], bias=t - 255.5)
 
             def kept(h):
-                op("S", lambda: act.activation(tab[:, 16 + K + 512 * h:16 + K + 512 * h + 512], T.pw0[:, half(h)], F.Identity, bias=t - 128.0),
-                   ["pw0" + "ab"[h]], ["tabc%d_%d" % (t, h)])
-            sums(0, False)
+                mw(T.pw1[:, half(h)], W_N128, T.ge[:, half(h)], False, True, ["ge%d" % h], ["pw1" + "ab"[h]])
+                actS(T.tab[:, CAP + 512 * h:CAP + 512 * h + 512], T.pw1[:, half(h)], F.Identity, ["pw1" + "ab"[h]], ["tabc%d" % h], bias=t - 128.0)
+
+            def born(h):
+                mw(T.pw0[:, half(h)], W_ID0 + t, T.PT[:, Z + 512 * h:Z + 512 * h + 512], True, False, rP, ["pw0" + "ab"[h]])
+                mw(T.pw0[:, half(h)], W_P, T.pgp[:, half(h)], False, False, halfof("pgp", h), ["pw0" + "ab"[h]])
+
+            def bounds(h):
+                gT(T.M[:, Z + o + 512 * h:Z + o + 512 * h + 512], wz_m, T.opj[:, 64 + 32 * h:96 + 32 * h], T.tm[:, half(h)], A.max,
+                   rM + ["Mz", "opj", "tm"], ["M%d_%d" % (t + 1, h)])
+
+            def rows(h):
+                mw(T.pw0[:, half(h)], W_J, T.pgz[:, half(h)], False, True, halfof("pgz", h), ["pw0" + "ab"[h]])
+                actS(T.PT[:, Z + o + 512 * h:Z + o + 512 * h + 512], T.pw0[:, half(h)], F.Relu, ["pw0" + "ab"[h]], ["PT%d_%d" % (t + 1, h)])
+            extract(T.pa[:, 0:64], B_LP, T.pgp, whole("pgp"), ["pa"], stop=False)
+            part(gS, "pgj", wp, T.oj, 32, 64, rP + ["oj"])
+            part(gV, "pgj", wp, T.oj, 0, 32, rP + ["oj"])
+            sums(T.pw0, "pw0", 0, True)
+            extract(T.pb[:, 0:24], B_ONE, T.Zc, ["Zc"], ["pb"], n=CAP)
+            copyV(T.inv[:], T.pb[:, 0:24], ["pb"], ["inv"])
+            remote(T["who%d" % t][:], T.inv[:], "d%d" % t, ["inv"], "who%d" % t)
+            extract(T.pa[:, 0:64], B_LN, T.pgj, whole("pgj"), ["pa"], start=False)
+            part(gS, "gx", wx, T.op, GX, 64, rX + ["op"])
             wraps(0)
-            extract(T.pb[:, 0:64], B_LN, T.pgj, ["pgj0", "pgj1"], ["pb"], start=False)
-            pick_zero()
-            sums(0, True)
-            gS(T.gx[:, half(1)], wx, T.op[:, 32:64], rX + ["op"], ["gxb"])
-            sums(1, False)
-            kept(0)
+            sums(T.pw0, "pw0", 1, True)
+            sums(T.pw1, "pw1", 0, False)
+            pick()
             wraps(1)
-            sums(1, True)
-            pick_a()
-            op("V", lambda: vec.tensor_scalar(T.hb[:, 1::2], T.spos[:, 1::2], 192.0, tab[:, 15:16], A.subtract, A.is_lt),
-               ["spos", "landh%d" % t], ["hb"])
-            pick_b()
-            op("V", lambda: vec.tensor_tensor_scan(T.sidx[:], T.hb[:], T.pd[:, 0:128], 0.0, A.mult, A.add), ["hb", "pd"], ["sidx"])
-            gS(T.pgz[:, half(0)], wz_p, T.opj[:, 64:96], rP + ["opj"], ["pgz0"])
+            kept(0)
+            sums(T.pw1, "pw1", 1, False)
             kept(1)
-            gS(T.pgz[:, half(1)], wz_p, T.opj[:, 96:128], rP + ["opj"], ["pgz1"])
-            gT(T.tm[:], wz_m, T.opj[:, 0:64], ask, A.max, rM + rq + ["Mz", "opj"], ["tm0", "tm1"])
-            op("V", lambda: vec.tensor_copy(T.oidx[:], T.sidx[:, 1::2]), ["sidx"], ["oidx"])
-            gT(T.M[:, Z + o:Z + o + K], wz_m, T.opj[:, 64:128], T.tm[:], A.max, rM + ["Mz", "opj", "tm0", "tm1"],
-               ["M%d_0" % (t + 1), "M%d_1" % (t + 1)])
-            for h in (0, 1):
-                mm(T.pw1[:, half(h)], Wk(W_J), T.pgz[:, half(h)], False, True, ["pgz%d" % h, "W%d" % W_J], ["pw1" + "ab"[h]])
+            born(0)
+            born(1)
+            ts(T.hb[:, 1::2], T.pc[:, 128:192], 511.0 - 192.0, T["got%d" % t][:, 15:16], (A.add, A.is_lt), ["pc", "got%d" % t], ["hb"])
+            gT(T.tm[:], wz_m, T.opj[:, 0:64], ask, A.max, rM + rq + ["Mz", "opj"], ["tm"])
+            scan(T.sidx[:], T.hb[:], T.pc[:, 0:128], A.mult, A.add, ["hb", "pc"], ["sidx"])
+            part(gS, "pgz", wz_p, T.opj, 0, 20, rP + ["opj"], 64)
+            gS(T.tab[:, 0:CAP], T["qp%d" % t][:], T["who%d" % t][:], ["qp%d" % t, "who%d" % t], ["taba"])
+            copyV(T.oidx[:], T.sidx[:, 1::2], ["sidx"], ["oidx"])
+            bounds(0)
+            rt = ["taba", "tabc0", "tabc1", "oidx"]
+            part(gS, "pgz", wz_p, T.opj, 20, 32, rP + ["opj"], 64)
+            gS(T.X[:, o + K + 16 * CF:o + 2 * K], T.tab[:], T.oidx[:, CF:64], rt, ["X%db" % (t + 2)])
+            gV(T.X[:, o + K:o + K + 16 * CF], T.tab[:], T.oidx[:, 0:CF], rt, ["X%d" % (t + 2)])
+            bounds(1)
             dma("Y", T.ym[:, K * t:K * t + K], T.M[:, Z + o:Z + o + K], ["M%d_0" % (t + 1), "M%d_1" % (t + 1)], [])
-            rt = ["land%d" % t, "gap%d" % t, "tabc%d_0" % t, "tabc%d_1" % t, "oidx"]
-            gV(T.X[:, o + K:o + K + 512], tab[:, 16:16 + 2 * K], T.oidx[:, 0:32], rt, ["X%d" % (t + 2)])
-            gS(T.X[:, o + K + 512:o + 2 * K], tab[:, 16:16 + 2 * K], T.oidx[:, 32:64], rt, ["X%db" % (t + 2)])
-            op("S", lambda: act.activation(T.PT[:, Z + o:Z + o + K], T.pw1[:], F.Relu), ["pw1a", "pw1b"], ["PT%d_0" % (t + 1), "PT%d_1" % (t + 1)])
-            extract(T.pc[:, 0:64], B_W, T.X, ["X%d" % (t + 2), "X%db" % (t + 2)], ["pc"], c0=o + K)
-            op("V", lambda: vec.tensor_copy(T.h0[:], T.pc[:, 0:64]), ["pc"], ["h0"])
-            op("V", lambda: vec.tensor_scalar(T.h1[:], T.h0[:], K - 1, None, A.bitwise_and), ["h0"], ["h1"])
-            op("V", lambda: vec.tensor_copy(T.ou0[:], T.h1[:]), ["h1"], ["ou0"])
+            part(gS, "pgz", wz_p, T.opj, 32, 64, rP + ["opj"], 64)
+            rows(0)
+            extract(T.pb[:, 0:64], B_W, T.X, ["X%d" % (t + 2), "X%db" % (t + 2)], ["pb"], c0=o + K)
+            rows(1)
+            copyV(T.h0[:], T.pb[:, 0:64], ["pb"], ["h0"])
+            ts(T.h1[:], T.h0[:], K - 1, None, (A.bitwise_and,), ["h0"], ["h1"])
+            copyV(T.ou0[:], T.h1[:], ["h1"], ["ou0"])
         else:
-            x_get(2)
-            x_vec(2)
-            x_diff()
-            pointers(2)
-            m_test(2)
-            votes_x(1, T.pc, "pc")
-            differences(T.pa, 0, "pa", 5, 2)
-            x_sign(2)
-            stays(1, T.pc, "pc")
-            extract(T.pa[:, 0:320:5], B_DH, pg[0], ["pg0"], ["pa"])
             votes_x(2, T.pd, "pd")
-            stays(2, T.pd, "pd")
-            extract(T.pb[:, 0:64], B_ONE, T.cm, ["cm"], ["pb"])
-            op("S", lambda: act.activation(T.d0f[:, 1::5], T.pb[:, 0:64], F.Sign, bias=-9.5), ["pb"], ["d0f1"])
-            extract(T.pa[:, 1:320:5], B_SI, pg[0], ["pg0"], ["pa"])
-            op("V", lambda: vec.tensor_tensor_scan(T.sp[:], T.d0f[:], T.pa[:, 0:320], 0.0, A.mult, A.add), nn + ["d0f1", "pa"], ["sp"])
-            pf = T.sp[:, 4::5]
-            op("V", lambda: vec.tensor_copy(T.op[:], pf), ["sp"], ["op"])
-            gS(T.pgp[:, 512:K], wp, T.op[:, 32:64], rP + ["op"], ["pgp1"])
-            gV(T.pgp[:, 0:512], wp, T.op[:, 0:32], rP + ["op"], ["pgp0"])
-            mm(T.pa[:, 0:64], Ip, pf, True, True, ["If0", "sp"], ["pa"])
-            extract(T.pa[:, 64:128], B_J, T.pgp, ["pgp0", "pgp1"], ["pa"])
-            op("V", lambda: vec.tensor_copy(T.oj[:], T.pa[:, 64:128]), ["pa"], ["oj"])
-            extract(T.pb[:, 0:64], B_LP, T.pgp, ["pgp0", "pgp1"], ["pb"], stop=False)
-            gS(T.pgj[:, 512:K], wp, T.oj[:, 32:64], rP + ["oj"], ["pgj1"])
-            gV(T.pgj[:, 0:512], wp, T.oj[:, 0:32], rP + ["oj"], ["pgj0"])
+            stays(2)
+            choose_p()
+            part(gS, "pgp", wp, T.op, 32, 64, rP + ["op"])
+            part(gV, "pgp", wp, T.op, 0, 32, rP + ["op"])
+            mm(T.pd[:, 0:64], Ip, pf, True, True, ["If0", "sp"], ["pd"])
+            extract(T.pd[:, 64:128], B_J, T.pgp, whole("pgp"), ["pd"])
+            copyV(T.oj[:], T.pd[:, 64:128], ["pd"], ["oj"])
+            extract(T.pa[:, 0:64], B_LP, T.pgp, whole("pgp"), ["pa"], stop=False)
+            part(gS, "pgj", wp, T.oj, 32, 64, rP + ["oj"])
+            part(gV, "pgj", wp, T.oj, 0, 32, rP + ["oj"])
             for h in (0, 1):
-                mm(T.pw0[:, half(h)], Wk(W_P), T.pgp[:, half(h)], True, False, ["pgp0", "pgp1", "W%d" % W_P], ["pw0" + "ab"[h]])
-            extract(T.pb[:, 0:64], B_LN, T.pgj, ["pgj0", "pgj1"], ["pb"], start=False)
-            pick_zero()
-            pick_a()
-            pick_b()
+                mw(T.pw0[:, half(h)], W_P, T.pgp[:, half(h)], True, False, halfof("pgp", h), ["pw0" + "ab"[h]])
+            extract(T.pa[:, 0:64], B_LN, T.pgj, whole("pgj"), ["pa"], start=False)
+            pick()
             for h in (0, 1):
-                gS(T.pgz[:, half(h)], wz_p, T.opj[:, 64 + 32 * h:96 + 32 * h], rP + ["opj"], ["pgz%d" % h])
-                mm(T.pw0[:, half(h)], Wk(W_J), T.pgz[:, half(h)], False, True, ["pgz%d" % h, "W%d" % W_J], ["pw0" + "ab"[h]])
+                part(gS, "pgz", wz_p, T.opj, 32 * h, 32 * h + 32, rP + ["opj"], 64)
+                mw(T.pw0[:, half(h)], W_J, T.pgz[:, half(h)], False, True, halfof("pgz", h), ["pw0" + "ab"[h]])
             for h in (0, 1):
                 gT(T.tm[:, half(h)], wz_m, T.opj[:, 32 * h:32 * h + 32], T.X[:, o + 512 * h:o + 512 * h + 512], A.max,
                    rM + rq + ["Mz", "opj"], ["tm%d" % h])
-            for h in (0, 1):
                 a = Z + o + 512 * h
                 gT(T.M[:, a:a + 512], wz_m, T.opj[:, 64 + 32 * h:96 + 32 * h], T.tm[:, half(h)], A.max,
                    rM + ["Mz", "opj", "tm%d" % h], ["M%d_%d" % (t + 1, h)])
                 dma("Y", T.ym[:, K * t + 512 * h:K * t + 512 * h + 512], T.M[:, a:a + 512], ["M%d_%d" % (t + 1, h)], [])
             for h in (0, 1):
                 a = Z + o + 512 * h
-                op("S", lambda: act.activation(T.PT[:, a:a + 512], T.pw0[:, half(h)], F.Relu), ["pw0" + "ab"[h]], ["PT%d_%d" % (t + 1, h)])
-                emit_out_mm(t, h)
-            emit_out_copy(t, 0)
-            emit_out_copy(t, 1)
-            emit_out_dma(t, "S")
+                actS(T.PT[:, a:a + 512], T.pw0[:, half(h)], F.Relu, ["pw0" + "ab"[h]], ["PT%d_%d" % (t + 1, h)])
+                out_mm(t, h)
+            out_store(t, "S")
 
     for s in total:
         g.wait_ge(T.sem[s], total[s])

@@ -4,18 +4,20 @@ V0, K, CAP, RO = 3072, 1024, 384, 3
 Z = 16
 CV = 48
 C1 = 36
-CF = 20
-GX = 40
-MA = 1792
+CF = 32
+GX = 48
+PJ = 16
+PZ = 36
+CL = 24
 BIG = 8192.0
 BW = 144
 WD = 3104
-B_ONE, B_SH, B_SI, B_J, B_LP, B_LN, B_W = range(7)
+B_ONE, B_SH, B_SI, B_J, B_LP, B_LN, B_ID, B_W = range(8)
 W_P, W_J, W_ID0, W_ID1, W_I, W_NI, W_N128, W_ONE, W_NU, W_NF, W_TRI, W_N4K, W_MK = range(13)
 
 bf, f32, i32, u16 = "bfloat16", "float32", "int32", "uint16"
 SCRATCH = {
-    "X": ("sbuf", [128, V0 + RO * K], bf), "M": ("sbuf", [128, Z + V0 + RO * K], bf), "PT": ("sbuf", [128, Z + V0 + RO * K], bf),
+    "X": ("sbuf", [128, V0 + RO * K + K], bf), "M": ("sbuf", [128, Z + V0 + RO * K], bf), "PT": ("sbuf", [128, Z + V0 + RO * K], bf),
     "PA": ("sbuf", [128, V0], bf),
     "Ci": ("sbuf", [128, 576], i32), "Cb": ("sbuf", [128, 1728], bf), "idt": ("sbuf", [128, 192], bf),
     "u0i": ("sbuf", [128, 64], i32), "wi": ("sbuf", [128, 1], i32), "pi": ("sbuf", [128, 1], i32), "pj": ("sbuf", [128, 1], i32),
@@ -25,7 +27,7 @@ SCRATCH = {
     "ou0": ("sbuf", [128, 64], u16), "ou1": ("sbuf", [128, 64], u16), "ou2": ("sbuf", [128, 64], u16), "ou3": ("sbuf", [128, 64], u16),
     "op": ("sbuf", [128, 64], u16), "oj": ("sbuf", [128, 64], u16), "opj": ("sbuf", [128, 128], u16), "oidx": ("sbuf", [128, 64], u16),
     "ost": ("sbuf", [128, 4], u16),
-    "cm": ("sbuf", [128, K], bf), "cx0": ("sbuf", [128, K], bf), "cx1": ("sbuf", [128, K], bf), "gx": ("sbuf", [128, K], bf),
+    "cm": ("sbuf", [128, K], bf), "cx0": ("sbuf", [128, K], bf), "cx1": ("sbuf", [128, K], bf), "cx2": ("sbuf", [128, K], bf), "gx": ("sbuf", [128, K], bf),
     "gy": ("sbuf", [128, K - 16 * CV], bf),
     "pg0": ("sbuf", [128, K], bf), "pg1": ("sbuf", [128, K], bf), "pgp": ("sbuf", [128, K], bf), "pgj": ("sbuf", [128, K], bf),
     "pgz": ("sbuf", [128, K], bf), "ge": ("sbuf", [128, K], bf), "tm": ("sbuf", [128, K], bf),
@@ -39,7 +41,7 @@ SCRATCH = {
     "cnt": ("sbuf", [128, 16], bf), "got0": ("sbuf", [128, 16], bf), "got1": ("sbuf", [128, 16], bf),
     "inv": ("sbuf", [128, 24], u16), "who0": ("sbuf", [128, 24], u16), "who1": ("sbuf", [128, 24], u16),
     "qp0": ("sbuf", [128, K], bf), "qp1": ("sbuf", [128, K], bf), "tab": ("sbuf", [128, CAP + K], bf),
-    "Bm": ("sbuf", [128, 7 * BW], bf), "Wm": ("sbuf", [128, 13 * 128], bf), "Ws": ("sbuf", [128, 32 + CAP], bf), "Wo": ("sbuf", [128, 136], bf),
+    "Bm": ("sbuf", [128, 8 * BW], bf), "Wm": ("sbuf", [128, 13 * 128], bf), "Ws": ("sbuf", [128, 32 + CAP], bf), "Wo": ("sbuf", [128, 136], bf),
     "If": ("sbuf", [128, 256], f32), "yo": ("sbuf", [128, 128], f32),
     "pw0": ("psum", [128, 1024], f32), "pw1": ("psum", [128, 1024], f32),
     "pa": ("psum", [128, 512], f32), "pb": ("psum", [128, 512], f32), "pc": ("psum", [128, 512], f32), "pd": ("psum", [128, 512], f32),
@@ -199,7 +201,7 @@ def rank_program(g, core, T, topo):
     dma("S", T.Ci[64:128, 0:384], T.jump[:], [], ["Ci1"])
     dma("Y", T.u0i[:], T.u0[:], [], ["u0i"])
     dma("S", T.X[:, V0:V0 + K], T.q[:], [], ["X1"])
-    dma("Y", T.M[:, Z:Z + MA], T.m[:, 0:MA], [], ["M0"])
+    dma("Y", T.M[:, Z:Z + V0], T.m[:], [], ["M0"])
 
     prow = ["PT0_%d" % f for f in range(11)]
     arow = ["PA_%d" % f for f in range(4)]
@@ -209,8 +211,8 @@ def rank_program(g, core, T, topo):
     op("G", lambda: g.iota(T.pi[:], [[0, 1]], 0, 1), [], ["pi"])
     fill(T.Ws[:], 0.0, ["Wv", "Wh", "zt"])
     fill(T.Bm[:, 0:2 * BW], 0.0, ["B0", "B1"])
-    fill(T.PA[:], 0.0, arow)
     ts(T.pj[:], T.pi[:], 15, None, (A.bitwise_and,), ["pi"], ["pj"])
+    fill(T.PA[:], 0.0, arow)
 
     def split(a, n, o, r, w):
         ts(T.Cb[:, o:o + n], T.Ci[:, a:a + n], 16.0, 0.0, (A.subtract, A.max), r, [w + "h"])
@@ -223,20 +225,19 @@ def rank_program(g, core, T, topo):
     split(0, 384, 0, ["Ci0", "Ci1"], "Cp")
     for f in (0, 2, 1, 3):
         dma("Y", T.PA[f::16, :], piece(f)[0], [piece(f)[1]], ["PA_%d" % f])
-    dma("Y", T.M[:, Z + MA:Z + V0], T.m[:, MA:V0], [], ["M0b"])
     dma("Y", T.Ci[:, 384:576], T.ln[:], [], ["Ci2"])
-    dma("Y", T.X[:, 0:V0], T.x[:], [], ["X0"])
     dma("Y", T.wi[:], T.w[:], [], ["wi"])
+    dma("Y", T.X[:, 0:V0], T.x[:], [], ["X0"])
     copyV(T.ou0[:], T.u0i[:], ["u0i"], ["ou0"])
     fill(T.PT[:, 0:Z + V0], 0.0, ["PTa"])
     copyV(T.uf[:, 0:64], T.u0i[:], ["u0i"], ["uf0"])
 
     fills = {"Wv": [(16, 1.0), (0, 0.0)], "Wh": [(6, -0.5), (2, 0.5), (0, 0.0)],
              "B0": [(16, 1.0), (0, 0.0)], "B1": [(6, 0.5), (0, 0.0)], "B2": [(8, -1.0), (6, 0.5), (0, 0.0)], "B3": [(6, 1.0), (2, 0.0)],
-             "B4": [(10, 1.0), (8, 0.0)], "B5": [(10, -1.0), (8, 0.0)],
+             "B4": [(10, 1.0), (8, 0.0)], "B5": [(10, -1.0), (8, 0.0)], "B6": [(8, 1.0), (6, 0.0)],
              "Wp": [(2, 1.0), (0, 0.0)], "Wj": [(6, 1.0), (2, 0.0)]}
     cols = {"Wv": T.Ws[:, 0:16:2], "Wh": T.Ws[:, 16:32:2], "Wp": T.Wo[:, 7:71:8], "Wj": T.Wo[:, 71:135:8]}
-    for k in range(6):
+    for k in range(7):
         cols["B%d" % k] = T.Bm[:, k * BW + 15:k * BW + 143:16]
 
     def bfill(ks):
@@ -260,7 +261,7 @@ def rank_program(g, core, T, topo):
     def zeros(buf, a, b, names):
         for c in range(a, b, CAP):
             actS(buf[:, c:min(c + CAP, b)], T.Ws[:, 32:32 + min(CAP, b - c)], F.Identity, ["zt"], names)
-    zeros(T.Bm, 2 * BW, 7 * BW, ["B%d" % k for k in range(2, 7)])
+    zeros(T.Bm, 2 * BW, 8 * BW, ["B%d" % k for k in range(2, 8)])
     zeros(T.Wm, 0, 512, [wn(k) for k in range(4)])
     zeros(T.Wo, 0, 136, ["Wp", "Wj"])
     bfill(["Wv", "Wh"])
@@ -288,6 +289,9 @@ def rank_program(g, core, T, topo):
     fillS(T.one64[:], 1.0, ["one64"])
     fillS(T.Sc[:, 0:8], 0.0, ["Scz"])
     fillS(T.cnt[:], 0.0, ["cnt"])
+    fillS(T.hb[:], 0.0, ["hb"])
+    fillS(T.M[:, 0:Z], 0.0, ["Mz"])
+    fillS(T.Wd[:, 0:CAP], 0.0, ["Wd0"])
     block = [[-16, 8], [0, 16]]
     iota(T.Ct[:], [[16, 64]], CAP, "Ct")
     iota(T.col[:], [[1, 64]], 0, "col")
@@ -308,24 +312,19 @@ def rank_program(g, core, T, topo):
 
     def late(n):
         if n == 0:
-            split(384, 192, 768, ["Ci2"], "Cl")
+            copyV(wf, T.wi[:], ["wi"], ["wf"])
             for f in range(4):
                 row(f, *piece(f))
             for f, c, name in ((6, 1152, "Cb6"), (7, 1344, "Cb7"), (10, 1536, "Cb8"), (8, 768, "Clh"), (9, 960, "Cll")):
                 row(f, T.Cb[:, c:c + 192], name)
             remote(T.qp0[:], T.X[:, V0:V0 + K], "q0", ["X1"] + prow, "qp0")
-            bfill(["Wp", "Wj", "B2"])
+            bfill(["Wp", "Wj", "B2", "B6"])
         if n == 1:
             actS(Wk(W_MK), Wk(W_MK), F.Abs, [wn(W_MK), "pmneg"], [wn(W_MK)], bias=pmneg, scale=16384.0)
             actS(T.Cf[:], T.Ct[:], F.Identity, ["Ct", "pm"], ["Cf"], bias=pm)
             actS(T.c15[:], T.col[:], F.Identity, ["col", "last"], ["c15"], scale=lastrow)
             fillS(T.dn[:], lastm1, ["dn", "lastm1"])
-            fillS(T.Wd[:, 0:CAP], 0.0, ["Wd0"])
             actS(Wk(W_N4K), Wk(W_ONE), F.Identity, [wn(W_ONE)], [wn(W_N4K)], scale=-4096.0)
-        if n == 2:
-            fillS(T.hb[:], 0.0, ["hb"])
-            fillS(T.M[:, 0:Z], 0.0, ["Mz"])
-            copyV(wf, T.wi[:], ["wi"], ["wf"])
         if n == 3:
             actS(T.Bm[:, B_W * BW + 15:B_W * BW + 143:16], T.Bm[:, 15:143:16], F.Identity, ["B0", "wf"], ["B%d" % B_W], scale=wf)
         if n == 4:
@@ -350,7 +349,7 @@ def rank_program(g, core, T, topo):
         o = V0 + K * t
         last = t == RO - 1
         rX = ["X%d" % k for k in range(t + 1)]
-        rM = ["M0", "M0b"] + ["M%d_%d" % (k, h) for k in range(1, t + 1) for h in (0, 1)]
+        rM = ["M0"] + ["M%d_%d" % (k, h) for k in range(1, t + 1) for h in range(16)]
         rP = prow + ["PTa"] + ["PT%d_%d" % (k, h) for k in range(1, t + 1) for h in (0, 1)]
         rq = ["X%d" % (t + 1)]
         if t > 0:
@@ -358,7 +357,7 @@ def rank_program(g, core, T, topo):
             rq = rq + ["X%db" % (t + 1)]
         ask = T.X[:, o:o + K]
         offs = [T.ou0, T.ou1, T.ou2, T.ou3]
-        cx = [T.cx0, T.cx1]
+        cx = [T.cx0, T.cx1, T.cx2]
         pg = [T.pg0, T.pg1]
         nn = ["n0", "n1", "n2"]
 
@@ -375,35 +374,35 @@ def rank_program(g, core, T, topo):
             a = o - K if (s == 0 and t > 0) else 0
             return T.X[:, a:o], T.M[:, Z + a:Z + o], T.PT[:, Z + a:Z + o]
 
-        def pointers(s):
-            if t == 0:
-                gS(pg[s % 2][:], T.PA[:], offs[s][:], arow + ["ou%d" % s], ["pg%d" % (s % 2)])
-            else:
-                gS(pg[s % 2][:], wins(s)[2], offs[s][:], rP + ["ou%d" % s], ["pg%d" % (s % 2)])
+        def pointers(s, gather=gS, a=0, b=64):
+            win, r = (T.PA[:], arow) if t == 0 else (wins(s)[2], rP)
+            gather(pg[s % 2][:, 16 * a:16 * b], win, offs[s][:, a:b], r + ["ou%d" % s], quarters("pg%d_" % (s % 2), a, b))
 
         def m_test(s):
             gT(T.cm[:], wins(s)[1], offs[s][:], ask, A.is_ge, rM + rq + ["ou%d" % s], ["cm"])
 
         def x_vec(s, a, b):
-            gT(cx[s % 2][:, 16 * a:16 * b], wins(s)[0], offs[s][:, a:b], T.X[:, o + 16 * a:o + 16 * b], A.is_ge, rX + rq + ["ou%d" % s],
-               quarters("cx%d_" % (s % 2), a, b))
+            gT(cx[s % 3][:, 16 * a:16 * b], wins(s)[0], offs[s][:, a:b], T.X[:, o + 16 * a:o + 16 * b], A.is_ge, rX + rq + ["ou%d" % s],
+               quarters("cx%d_" % (s % 3), a, b))
 
         def x_get(s):
             gS(T.gy[:], wins(s)[0], offs[s][:, CV:64], rX + ["ou%d" % s], ["gy"])
 
-        def x_diff():
+        def x_open():
             mw(T.pw0[:, 0:K - LV], W_NI, T.X[:, o + LV:o + K], True, False, rq, ["pw0a"])
+
+        def x_diff():
             mw(T.pw0[:, 0:K - LV], W_I, T.gy[:], False, True, ["gy"], ["pw0a"])
 
         def x_sign(s):
-            actS(cx[s % 2][:, LV:K], T.pw0[:, 0:K - LV], F.Sign, ["pw0a"], quarters("cx%d_" % (s % 2), CV, 64), bias=0.5)
+            actS(cx[s % 3][:, LV:K], T.pw0[:, 0:K - LV], F.Sign, ["pw0a"], quarters("cx%d_" % (s % 3), CV, 64), bias=0.5)
 
-        def votes_x(s, bank, bn, start=True):
-            mw(bank[:, 0:64], W_I, T.six[:], start, False, ["sixa", "sixb"], [bn])
-            extract(bank[:, 0:64], B_ONE, cx[s % 2], quarters("cx%d_" % (s % 2), 0, 64), [bn], start=False)
+        def votes_x(s, bank, bn, start=True, c=0):
+            mw(bank[:, c:c + 64], W_I, T.six[:], start, False, ["sixa", "sixb"], [bn])
+            extract(bank[:, c:c + 64], B_ONE, cx[s % 3], quarters("cx%d_" % (s % 3), 0, 64), [bn], start=False)
 
-        def stays(s):
-            actS(T.na[:], T.pd[:, 0:64], F.Relu, ["pd"], ["na"], bias=-9.0)
+        def stays(s, bank=T.pd, bn="pd", c=0):
+            actS(T.na[:], bank[:, c:c + 64], F.Relu, [bn], ["na"], bias=-9.0)
             actS(nap(s), T.na[:], F.Relu, ["na"], [nn[s]], bias=1.0, scale=-1.0)
 
         def differences():
@@ -420,81 +419,129 @@ def rank_program(g, core, T, topo):
             scan(T.sp[:], T.d0g[:], T.pw1[:, 512:768], A.mult, A.add, nn + ["pw1b"], ["sp"])
             copyV(T.op[:], T.sp[:, 3::4], ["sp"], ["op"])
 
-        for s in range(3):
-            final = last and s == 2
-            first = t == 0 and s == 0
-            pn = "pg%d" % (s % 2)
-            gaps = [[(s, 0, C1)], [(s, C1, CV)]]
-            if t == 0 and s < 2:
-                gaps = [[[], [(0, 0, 32)]], [[(0, 32, CV), (1, 0, 24)], [(1, 24, CV)]]][s]
-            if s == 2:
-                actS(uf(2), T.pc[:, 0:64], F.Identity, ["pc"], ["uf2"])
-            pointers(s)
-            m_test(s)
-            if t == 1 and s == 0:
-                remote(T.qp1[:], ask, "q1", rq, "qp1")
-            if s > 0 and not (t == 0 and s == 1):
-                votes_x(s - 1, T.pd, "pd")
-            if t > 0 and s == 0:
-                out_mm(t - 1, 0)
-                out_mm(t - 1, 1)
-            if s == 2:
-                differences()
-                if not final:
-                    mm(T.pw1[:, 512:768:4], In, uf(2), True, False, ["If1", "uf2"], ["pw1b"])
+        def turns(s):
             turn(T.pa, Wv, T.cm, ["cm", "Wv"], ["pa"])
-            turn(T.pb, Wh, pg[s % 2], [pn, "Wh"], ["pb"])
-            if first:
-                late(1)
-            else:
-                x_get(s)
-            for x in gaps[0]:
-                x_vec(*x)
+            turn(T.pb, Wh, pg[s % 2], quarters("pg%d_" % (s % 2), 0, 64) + ["Wh"], ["pb"])
+
+        def sign():
             actS(T.sg[:], T.pa[:, 0:128], F.Sign, ["pa"], ["sg"], bias=-9.5)
-            if first:
-                late(0)
-                x_get(s)
-            if t < 2 and s == 1:
-                late(2 + 2 * t)
-            if final:
-                extract(T.pw1[:, 512:768:4], B_SI, pg[s % 2], [pn], ["pw1b"], stop=False)
-            else:
-                extract(T.pc[:, 0:64], B_SH, pg[s % 2], [pn], ["pc"], stop=False)
+
+        def middle(s, k=B_SH, out=T.pc[:, 0:64], bn="pc"):
+            extract(out, k, pg[s % 2], quarters("pg%d_" % (s % 2), 0, 64), [bn], stop=False)
+
+        def signed():
             tt(T.tu[:, 8:136], T.pb[:, 0:128], T.sg[:], A.mult, ["pb", "sg"], ["tu"])
-            if not first:
-                x_diff()
-            if final:
-                turn_back(T.pw1[:, 512:768:4], "pw1b")
-            else:
+
+        def advance(s):
+            copyV(offs[s + 1][:], T.pc[:, 0:64], ["pc"], ["ou%d" % (s + 1)])
+
+        def open_choice():
+            actS(uf(2), T.pc[:, 0:64], F.Identity, ["pc"], ["uf2"])
+
+        for s in range(3):
+            if t == 0 and s == 0:
+                m_test(0)
+                pointers(0, gS, 24, 64)
+                pointers(0, gV, 0, 24)
+                turns(0)
+                sign()
+                split(384, 192, 768, ["Ci2"], "Cl")
+                middle(0)
+                signed()
+                late(1)
+                x_open()
                 turn_back(T.pc[:, 0:64], "pc")
-            if first:
+                late(0)
+                x_get(0)
+                advance(0)
                 x_diff()
-            if s > 0 and not (t == 0 and s == 1):
-                stays(s - 1)
-            x_sign(s)
-            if t > 0 and s == 0:
-                out_store(t - 1, "Y")
-            for x in gaps[1]:
-                x_vec(*x)
-            if t == 0 and s == 1:
-                votes_x(0, T.pd, "pd")
-                stays(0)
-            if s == 0 and t > 0:
-                ts(uf(0), T.h1[:], float(o - K), None, (A.add,), ["h1"], ["uf0"])
-            if s == 1:
-                copyV(uf(1), offs[1][:], ["ou1"], ["uf1"])
-            if not final:
-                copyV(offs[s + 1][:], T.pc[:, 0:64], ["pc"], ["ou%d" % (s + 1)])
+            elif t == 0 and s == 1:
+                pointers(1)
+                m_test(1)
+                x_sign(0)
+                turns(1)
+                x_vec(0, 0, 40)
+                sign()
+                x_get(1)
+                middle(1)
+                signed()
+                x_open()
+                turn_back(T.pc[:, 0:64], "pc")
+                x_diff()
+                x_sign(1)
+                x_vec(0, 40, CV)
+                x_vec(1, 0, 16)
+                advance(1)
+            elif last and s == 2:
+                x_get(2)
+                open_choice()
+                pointers(2)
+                m_test(2)
+                votes_x(1, T.pd, "pd")
+                x_open()
+                x_diff()
+                differences()
+                turns(2)
+                x_vec(2, 0, CV)
+                x_sign(2)
+                sign()
+                stays(1)
+                middle(2, B_SI, T.pw1[:, 512:768:4], "pw1b")
+                signed()
+                votes_x(2, T.pw0, "pw0b", c=512)
+                turn_back(T.pw1[:, 512:768:4], "pw1b")
+                ts(nap(2), T.pw0[:, 512:576], 9.5, None, (A.is_lt,), ["pw0b"], ["n2"])
+            else:
+                gaps = [[(s, 0, C1)], [(s, C1, CV)]]
+                if t == 0:
+                    gaps = [[(1, 16, CV), (2, 0, 8)], [(2, 8, CV)]]
+                    copyV(uf(1), offs[1][:], ["ou1"], ["uf1"])
+                if s == 2:
+                    open_choice()
+                pointers(s)
+                m_test(s)
+                if t == 1 and s == 0:
+                    remote(T.qp1[:], ask, "q1", rq, "qp1")
+                if s > 0:
+                    votes_x(s - 1 - (t == 0), T.pd, "pd")
+                if s == 0:
+                    out_mm(t - 1, 0)
+                    out_mm(t - 1, 1)
+                if s == 2:
+                    differences()
+                    mm(T.pw1[:, 512:768:4], In, uf(2), True, False, ["If1", "uf2"], ["pw1b"])
+                x_open()
+                turns(s)
+                x_get(s)
+                x_diff()
+                for x in gaps[0]:
+                    x_vec(*x)
+                sign()
+                if t == 1 and s == 1:
+                    late(4)
+                middle(s)
+                signed()
+                turn_back(T.pc[:, 0:64], "pc")
+                x_sign(s)
+                if s > 0:
+                    stays(s - 1 - (t == 0))
+                if s == 0:
+                    out_store(t - 1, "Y")
+                if t == 0:
+                    votes_x(1, T.pw0, "pw0b", c=512)
+                for x in gaps[1]:
+                    x_vec(*x)
+                if s == 0:
+                    ts(uf(0), T.h1[:], float(o - K), None, (A.add,), ["h1"], ["uf0"])
+                if s == 1:
+                    copyV(uf(1), offs[1][:], ["ou1"], ["uf1"])
+                advance(s)
+                if t == 0:
+                    ts(nap(1), T.pw0[:, 512:576], 9.5, None, (A.is_lt,), ["pw0b"], ["n1"])
 
         wx, wm, wp = wins(2)
         wz_m, wz_p = T.M[:, 0:Z + o], T.PT[:, 0:Z + o]
         pf = T.sp[:, 3::4]
-
-        def pick():
-            ts(T.ad[:], T.pa[:, 0:64], 0.0, BIG, (A.not_equal, A.mult), ["pa"], ["ad"])
-            for h in (0, 1):
-                tt(T.yy[:, 64 * h:64 * h + 64], T.pd[:, 64 * h:64 * h + 64], T.ad[:], A.subtract, ["pd", "ad"], ["yy" + "ab"[h]])
-            ts(T.opj[:], T.yy[:], float(Z), None, (A.add,), ["yya", "yyb"], ["opj"])
 
         def half(h):
             return slice(512 * h, 512 * h + 512)
@@ -513,6 +560,7 @@ def rank_program(g, core, T, topo):
             actS(uf(3), T.pc[:, 0:64], F.Identity, ["pc"], ["uf3"])
             x_vec(3, 0, CV)
             votes_x(2, T.pd, "pd")
+            x_open()
             x_diff()
             mm(T.pw1[:, 512:768:4], Ip, uf(3), False, True, ["If0", "uf3"], ["pw1b"])
             stays(2)
@@ -524,9 +572,12 @@ def rank_program(g, core, T, topo):
                 mw(T.pa[:, 0:64], W_N128, nap(s), s == 0, False, [nn[s]], ["pa"])
             choose_p()
             votes_x(3, T.pa, "pa", start=False)
+            for bn in ("pw0", "pw1"):
+                for h in (0, 1):
+                    mw(T[bn][:, half(h)], W_I, T.X[:, o + 512 * h:o + 512 * h + 512], True, False, rq, [bn + "ab"[h]])
             if t == 0:
                 late(3)
-            part(gS, "pgp", wp, T.op, 16, 64, rP + ["op"])
+            part(gS, "pgp", wp, T.op, 20, 64, rP + ["op"])
             part(gV, "pgp", wp, T.op, 0, 8, rP + ["op"])
             ts(T.fb[:], T.pa[:, 0:64], 9.5 - 384.0, None, (A.is_lt,), ["pa"], ["fb"])
             scan(T.Sc[:, 8:72], T.one64[:], T.fb[:], A.mult, A.add, ["one64", "fb"], ["Sc"])
@@ -537,7 +588,7 @@ def rank_program(g, core, T, topo):
             mw(T.pb[:, 0:128:2], W_ONE, excl, False, False, ["Sc", "Scz"], ["pb"])
             mw(T.pb[:, 1:128:2], W_ONE, excl, False, True, ["Sc", "Scz"], ["pb"])
             mw(T.pc[:, 256:257], W_ONE, T.Sc[:, 71:72], True, True, ["Sc"], ["pc"])
-            part(gV, "pgp", wp, T.op, 8, 16, rP + ["op"])
+            part(gV, "pgp", wp, T.op, 8, 20, rP + ["op"])
             copyV(T.Rk[:], T.pa[:, 0:64], ["pa"], ["Rk"])
             scan(T.sst[:], T.d0m[:], T.pb[:, 0:128], A.mult, A.max, ["d0m", "pb"], ["sst"])
             ts(T.cnt[:, 15:16], T.pc[:, 256:257], float(CAP), 192.0, (A.min, A.subtract), ["pc"], ["cnt"])
@@ -556,9 +607,8 @@ def rank_program(g, core, T, topo):
             mw(T.pc[:, 128:192], W_NF, T.fb[:], True, False, ["fb"], ["pc"])
             mw(T.pc[:, 128:192], W_ONE, incl, False, True, ["Sc"], ["pc"])
 
-            def sums(bank, bn, h, stop):
-                mw(bank[:, half(h)], W_I, T.X[:, o + 512 * h:o + 512 * h + 512], True, False, rq, [bn + "ab"[h]])
-                mw(bank[:, half(h)], W_I, T.gx[:, half(h)], False, stop, halfof("gx", h), [bn + "ab"[h]])
+            def sums(bn, h):
+                mw(T[bn][:, half(h)], W_I, T.gx[:, half(h)], False, bn == "pw0", halfof("gx", h), [bn + "ab"[h]])
 
             def wraps(h):
                 actS(T.ge[:, half(h)], T.pw0[:, half(h)], F.Sign, ["pw0" + "ab"[h]], ["ge%d" % h], bias=t - 255.5)
@@ -571,83 +621,105 @@ def rank_program(g, core, T, topo):
                 mw(T.pw0[:, half(h)], W_ID0 + t, T.PT[:, Z + 512 * h:Z + 512 * h + 512], True, False, rP, ["pw0" + "ab"[h]])
                 mw(T.pw0[:, half(h)], W_P, T.pgp[:, half(h)], False, False, halfof("pgp", h), ["pw0" + "ab"[h]])
 
-            def bounds(h):
-                gT(T.M[:, Z + o + 512 * h:Z + o + 512 * h + 512], wz_m, T.opj[:, 64 + 32 * h:96 + 32 * h], T.tm[:, half(h)], A.max,
-                   rM + ["Mz", "opj", "tm"], ["M%d_%d" % (t + 1, h)])
+            def bounds(a, b):
+                gT(T.M[:, Z + o + 16 * a:Z + o + 16 * b], wz_m, T.opj[:, 64 + a:64 + b], T.tm[:, 16 * a:16 * b], A.max,
+                   rM + ["Mz", "opj", "tm"], quarters("M%d_" % (t + 1), a, b))
 
             def rows(h):
-                mw(T.pw0[:, half(h)], W_J, T.pgz[:, half(h)], False, True, halfof("pgz", h), ["pw0" + "ab"[h]])
                 actS(T.PT[:, Z + o + 512 * h:Z + o + 512 * h + 512], T.pw0[:, half(h)], F.Relu, ["pw0" + "ab"[h]], ["PT%d_%d" % (t + 1, h)])
             extract(T.pa[:, 0:64], B_LP, T.pgp, whole("pgp"), ["pa"], stop=False)
-            part(gS, "pgj", wp, T.oj, 32, 64, rP + ["oj"])
-            part(gV, "pgj", wp, T.oj, 0, 32, rP + ["oj"])
-            sums(T.pw0, "pw0", 0, True)
+            part(gS, "pgj", wp, T.oj, PJ, 64, rP + ["oj"])
+            part(gV, "gx", wx, T.op, GX, 64, rX + ["op"])
+            part(gV, "pgj", wp, T.oj, 0, PJ, rP + ["oj"])
+            sums("pw0", 0)
+            sums("pw1", 0)
             extract(T.pb[:, 0:24], B_ONE, T.Zc, ["Zc"], ["pb"], n=CAP)
+            sums("pw0", 1)
             copyV(T.inv[:], T.pb[:, 0:24], ["pb"], ["inv"])
             remote(T["who%d" % t][:], T.inv[:], "d%d" % t, ["inv"], "who%d" % t)
             extract(T.pa[:, 0:64], B_LN, T.pgj, whole("pgj"), ["pa"], start=False)
-            part(gS, "gx", wx, T.op, GX, 64, rX + ["op"])
             wraps(0)
-            sums(T.pw0, "pw0", 1, True)
-            sums(T.pw1, "pw1", 0, False)
-            pick()
             wraps(1)
             kept(0)
-            sums(T.pw1, "pw1", 1, False)
+            sums("pw1", 1)
             kept(1)
             born(0)
             born(1)
+            ts(T.ad[:], T.pa[:, 0:64], 0.0, BIG, (A.not_equal, A.mult), ["pa"], ["ad"])
             ts(T.hb[:, 1::2], T.pc[:, 128:192], 511.0 - 192.0, T["got%d" % t][:, 15:16], (A.add, A.is_lt), ["pc", "got%d" % t], ["hb"])
-            gT(T.tm[:], wz_m, T.opj[:, 0:64], ask, A.max, rM + rq + ["Mz", "opj"], ["tm"])
+            for h in (0, 1):
+                tt(T.yy[:, 64 * h:64 * h + 64], T.pd[:, 64 * h:64 * h + 64], T.ad[:], A.subtract, ["pd", "ad"], ["yy" + "ab"[h]])
             scan(T.sidx[:], T.hb[:], T.pc[:, 0:128], A.mult, A.add, ["hb", "pc"], ["sidx"])
-            part(gS, "pgz", wz_p, T.opj, 0, 20, rP + ["opj"], 64)
-            gS(T.tab[:, 0:CAP], T["qp%d" % t][:], T["who%d" % t][:], ["qp%d" % t, "who%d" % t], ["taba"])
+            ts(T.opj[:], T.yy[:], float(Z), None, (A.add,), ["yya", "yyb"], ["opj"])
             copyV(T.oidx[:], T.sidx[:, 1::2], ["sidx"], ["oidx"])
-            bounds(0)
+            gT(T.tm[:], wz_m, T.opj[:, 0:64], ask, A.max, rM + rq + ["Mz", "opj"], ["tm"])
+            part(gS, "pgz", wz_p, T.opj, 0, PZ, rP + ["opj"], 64)
+            gS(T.tab[:, 0:CAP], T["qp%d" % t][:], T["who%d" % t][:], ["qp%d" % t, "who%d" % t], ["taba"])
+            bounds(0, 20)
             rt = ["taba", "tabc0", "tabc1", "oidx"]
-            part(gS, "pgz", wz_p, T.opj, 20, 32, rP + ["opj"], 64)
             gS(T.X[:, o + K + 16 * CF:o + 2 * K], T.tab[:], T.oidx[:, CF:64], rt, ["X%db" % (t + 2)])
             gV(T.X[:, o + K:o + K + 16 * CF], T.tab[:], T.oidx[:, 0:CF], rt, ["X%d" % (t + 2)])
-            bounds(1)
-            dma("Y", T.ym[:, K * t:K * t + K], T.M[:, Z + o:Z + o + K], ["M%d_0" % (t + 1), "M%d_1" % (t + 1)], [])
-            part(gS, "pgz", wz_p, T.opj, 32, 64, rP + ["opj"], 64)
-            rows(0)
+            bounds(20, 52)
+            part(gS, "pgz", wz_p, T.opj, PZ, 64, rP + ["opj"], 64)
+            mw(T.pw0[:, half(0)], W_J, T.pgz[:, half(0)], False, True, halfof("pgz", 0), ["pw0a"])
             extract(T.pb[:, 0:64], B_W, T.X, ["X%d" % (t + 2), "X%db" % (t + 2)], ["pb"], c0=o + K)
+            mw(T.pw0[:, half(1)], W_J, T.pgz[:, half(1)], False, True, halfof("pgz", 1), ["pw0b"])
+            rows(0)
             rows(1)
             copyV(T.h0[:], T.pb[:, 0:64], ["pb"], ["h0"])
+            bounds(52, 60)
             ts(T.h1[:], T.h0[:], K - 1, None, (A.bitwise_and,), ["h0"], ["h1"])
+            bounds(60, 64)
             copyV(T.ou0[:], T.h1[:], ["h1"], ["ou0"])
+            dma("Y", T.ym[:, K * t:K * t + K], T.M[:, Z + o:Z + o + K], whole("M%d_" % (t + 1)), [])
         else:
-            votes_x(2, T.pd, "pd")
-            stays(2)
+            def across(out, k, src, name, bn, start, stop):
+                def fn():
+                    for a in range(16):
+                        ins = pe.matmul(out, Bi(k, a), src[:, 64 * a:64 * a + 64], start and a == 0, stop and a == 15)
+                    return ins
+                op("P", fn, whole(name) + ["B%d" % k], [bn])
+
+            def with_p(a, b):
+                gT(T.tm[:, 16 * a:16 * b], wm, T.op[:, a:b], T.X[:, o + 16 * a:o + 16 * b], A.max, rM + rq + ["op"], quarters("tm", a, b))
+
+            def with_j(a, b):
+                gT(T.X[:, o + K + 16 * a:o + K + 16 * b], wm, T.oj[:, a:b], T.tm[:, 16 * a:16 * b], A.max, rM + ["oj"] + quarters("tm", a, b),
+                   quarters("both", a, b))
             choose_p()
             part(gS, "pgp", wp, T.op, 32, 64, rP + ["op"])
             part(gV, "pgp", wp, T.op, 0, 32, rP + ["op"])
-            mm(T.pd[:, 0:64], Ip, pf, True, True, ["If0", "sp"], ["pd"])
-            extract(T.pd[:, 64:128], B_J, T.pgp, whole("pgp"), ["pd"])
-            copyV(T.oj[:], T.pd[:, 64:128], ["pd"], ["oj"])
+            extract(T.pd[:, 0:64], B_J, T.pgp, whole("pgp"), ["pd"])
+            with_p(0, 32)
+            copyV(T.oj[:], T.pd[:, 0:64], ["pd"], ["oj"])
+            across(T.pb[:, 0:64], B_ID, T.pgp, "pgp", "pb", True, True)
             extract(T.pa[:, 0:64], B_LP, T.pgp, whole("pgp"), ["pa"], stop=False)
-            part(gS, "pgj", wp, T.oj, 32, 64, rP + ["oj"])
-            part(gV, "pgj", wp, T.oj, 0, 32, rP + ["oj"])
-            for h in (0, 1):
-                mw(T.pw0[:, half(h)], W_P, T.pgp[:, half(h)], True, False, halfof("pgp", h), ["pw0" + "ab"[h]])
+            across(T.pc[:, 0:64], B_LP, T.pgp, "pgp", "pc", True, False)
+            part(gS, "pgj", wp, T.oj, 0, 64, rP + ["oj"])
+            with_p(32, 64)
+            copyV(T.yo[:, 0:64], T.pb[:, 0:64], ["pb"], ["yo"])
+            with_j(0, 32)
+            with_j(32, 64)
+            dma("Y", T.ypar[:, K * t:K * t + K], T.yo[:, 0:64], ["yo"], [])
+            mm(T.pb[:, 0:64], In, T.yo[:, 0:64], True, False, ["If1", "yo"], ["pb"])
             extract(T.pa[:, 0:64], B_LN, T.pgj, whole("pgj"), ["pa"], start=False)
-            pick()
-            for h in (0, 1):
-                part(gS, "pgz", wz_p, T.opj, 32 * h, 32 * h + 32, rP + ["opj"], 64)
-                mw(T.pw0[:, half(h)], W_J, T.pgz[:, half(h)], False, True, halfof("pgz", h), ["pw0" + "ab"[h]])
-            for h in (0, 1):
-                gT(T.tm[:, half(h)], wz_m, T.opj[:, 32 * h:32 * h + 32], T.X[:, o + 512 * h:o + 512 * h + 512], A.max,
-                   rM + rq + ["Mz", "opj"], ["tm%d" % h])
-                a = Z + o + 512 * h
-                gT(T.M[:, a:a + 512], wz_m, T.opj[:, 64 + 32 * h:96 + 32 * h], T.tm[:, half(h)], A.max,
-                   rM + ["Mz", "opj", "tm%d" % h], ["M%d_%d" % (t + 1, h)])
-                dma("Y", T.ym[:, K * t + 512 * h:K * t + 512 * h + 512], T.M[:, a:a + 512], ["M%d_%d" % (t + 1, h)], [])
-            for h in (0, 1):
-                a = Z + o + 512 * h
-                actS(T.PT[:, a:a + 512], T.pw0[:, half(h)], F.Relu, ["pw0" + "ab"[h]], ["PT%d_%d" % (t + 1, h)])
-                out_mm(t, h)
-            out_store(t, "S")
+            across(T.pc[:, 0:64], B_LN, T.pgj, "pgj", "pc", False, True)
+            across(T.pb[:, 0:64], B_J, T.pgj, "pgj", "pb", False, True)
+            ts(T.ad[:], T.pa[:, 0:64], 0.0, float(K), (A.is_equal, A.mult), ["pa"], ["ad"])
+            tt(T.yy[:, 0:64], T.ad[:], T.Cf[:], A.add, ["ad", "Cf"], ["yya"])
+            ts(T.oidx[:], T.yy[:, 0:64], float(CAP), None, (A.subtract,), ["yya"], ["oidx"])
+            ts(T.na[:], T.pc[:, 0:64], 0.0, None, (A.is_equal,), ["pc"], ["na"])
+            rt = rq + whole("both") + ["oidx"]
+
+            def store(gather, q, a, b):
+                part(gather, "gx", T.X[:, o:o + 2 * K], T.oidx, a, b, rt)
+                dma(q, T.ym[:, K * t + 16 * a:K * t + 16 * b], T.gx[:, 16 * a:16 * b], quarters("gx", a, b), [])
+            store(gS, "Y", CL, 48)
+            tt(T.yy[:, 64:128], T.pb[:, 0:64], T.na[:], A.mult, ["pb", "na"], ["yyb"])
+            store(gV, "Y", 0, CL)
+            tt(T.yo[:, 64:128], T.yy[:, 64:128], T.yo[:, 0:64], A.add, ["yyb", "yo"], ["yoj"])
+            store(gS, "S", 48, 64)
+            dma("Y", T.yjump[:, K * t:K * t + K], T.yo[:, 64:128], ["yoj"], [])
 
     for s in total:
         g.wait_ge(T.sem[s], total[s])

@@ -3,12 +3,10 @@ from concourse.mybir import AluOpType as A, ActivationFunctionType as F
 V0, K, CAP, RO = 3072, 1024, 384, 3
 Z = 16
 CV = 48
-C1 = 36
+C1 = 28
 CF = 32
 GX = 48
-PJ = 16
-PZ = 36
-CL = 24
+PJ = 32
 BIG = 8192.0
 BW = 144
 WD = 3104
@@ -30,12 +28,12 @@ SCRATCH = {
     "cm": ("sbuf", [128, K], bf), "cx0": ("sbuf", [128, K], bf), "cx1": ("sbuf", [128, K], bf), "cx2": ("sbuf", [128, K], bf), "gx": ("sbuf", [128, K], bf),
     "gy": ("sbuf", [128, K - 16 * CV], bf),
     "pg0": ("sbuf", [128, K], bf), "pg1": ("sbuf", [128, K], bf), "pgp": ("sbuf", [128, K], bf), "pgj": ("sbuf", [128, K], bf),
-    "pgz": ("sbuf", [128, K], bf), "ge": ("sbuf", [128, K], bf), "tm": ("sbuf", [128, K], bf),
-    "uf": ("sbuf", [128, 256], f32), "sg": ("sbuf", [128, 128], bf), "tu": ("sbuf", [128, 136], f32),
+    "Wl": ("sbuf", [128, 16 * 128], bf), "ge": ("sbuf", [128, K], bf), "tm": ("sbuf", [128, K], bf),
+    "uf": ("sbuf", [128, 256], f32), "sg": ("sbuf", [128, 64], bf), "tu": ("sbuf", [128, 17, 8], f32),
     "sp": ("sbuf", [128, 256], f32), "sst": ("sbuf", [128, 128], f32), "sidx": ("sbuf", [128, 128], f32),
     "d0g": ("sbuf", [128, 256], bf), "d0m": ("sbuf", [128, 128], bf),
     "fb": ("sbuf", [128, 64], bf), "hb": ("sbuf", [128, 128], bf), "Rk": ("sbuf", [128, 64], bf),
-    "one64": ("sbuf", [128, 64], bf), "na": ("sbuf", [128, 64], f32), "ad": ("sbuf", [128, 64], f32), "yy": ("sbuf", [128, 128], f32),
+    "one64": ("sbuf", [128, 64], bf), "na": ("sbuf", [128, 64], f32), "ad": ("sbuf", [128, 64], bf), "yy": ("sbuf", [128, 128], f32),
     "h0": ("sbuf", [128, 64], i32), "h1": ("sbuf", [128, 64], i32), "Sc": ("sbuf", [128, 72], bf),
     "Wd": ("sbuf", [128, 2 * WD], bf), "Zr": ("sbuf", [128, CAP], bf), "Zc": ("sbuf", [128, CAP], bf),
     "cnt": ("sbuf", [128, 16], bf), "got0": ("sbuf", [128, 16], bf), "got1": ("sbuf", [128, 16], bf),
@@ -46,7 +44,7 @@ SCRATCH = {
     "pw0": ("psum", [128, 1024], f32), "pw1": ("psum", [128, 1024], f32),
     "pa": ("psum", [128, 512], f32), "pb": ("psum", [128, 512], f32), "pc": ("psum", [128, 512], f32), "pd": ("psum", [128, 512], f32),
 }
-NDMA = 36
+NDMA = 46
 SEMAPHORES = (["sV", "sS", "sP", "sG"] + [a + b + c for a in ("arr", "sent") for b in "qhd" for c in "01"]
               + ["d%d" % k for k in range(NDMA)])
 BANKS = ("pw0a", "pw0b", "pw1a", "pw1b", "pa", "pb", "pc", "pd")
@@ -62,6 +60,7 @@ def rank_program(g, core, T, topo):
     known = {q: {} for q in Q}
     clock = {}
     lastw, readers = {}, {}
+    waited, ending = {}, {}
     ndma = [0]
 
     def need(q, ev):
@@ -69,6 +68,7 @@ def rank_program(g, core, T, topo):
         if known[q].get(s, 0) >= c:
             return
         Q[q].wait_ge(T.sem[s], c)
+        waited[s] = max(waited.get(s, 0), c)
         known[q][s] = c
         for s2, c2 in clock.get((s, c), {}).items():
             if known[q].get(s2, 0) < c2:
@@ -112,6 +112,7 @@ def rank_program(g, core, T, topo):
         s = "d%d" % ndma[0]
         ndma[0] += 1
         total[s] = 16
+        ending[s] = q
         Q[q].dma_start(out, in_).then_inc(T.sem[s], 16)
         note(("D", s, 16), q, r, w)
 
@@ -145,10 +146,10 @@ def rank_program(g, core, T, topo):
             return ins
         op("P", fn, r + ["B%d" % k], w)
 
-    def turn(bank, wts, src, r, w):
+    def turn(bank, wts, src, r, w, m0, m1):
         def fn():
             for b in range(8):
-                ins = pe.matmul(bank[:, b:128:8], src[:, b:K:8], wts, True, True)
+                ins = pe.matmul(bank[m0:m1, b:64:8], src[:, 8 * m0 + b:8 * m1:8], wts, True, True)
             return ins
         op("P", fn, r, w)
 
@@ -203,40 +204,42 @@ def rank_program(g, core, T, topo):
     dma("S", T.X[:, V0:V0 + K], T.q[:], [], ["X1"])
     dma("Y", T.M[:, Z:Z + V0], T.m[:], [], ["M0"])
 
-    prow = ["PT0_%d" % f for f in range(11)]
+    prow = ["PT0_%d" % f for f in range(16)]
     arow = ["PA_%d" % f for f in range(4)]
-    Wv, Wh, zt = T.Ws[:, 0:16], T.Ws[:, 16:32], (T.Ws[:, 32:160], "zt")
+    Wv, Wh, zt = T.Ws[:, 0:8], T.Ws[:, 16:24], (T.Ws[:, 32:160], "zt")
     Ip, In = T.If[:, 0:128], T.If[:, 128:256]
     pm, lastrow, pm192, pmneg, lastm1, wf = [T.cl[:, k:k + 1] for k in range(6)]
     op("G", lambda: g.iota(T.pi[:], [[0, 1]], 0, 1), [], ["pi"])
     fill(T.Ws[:], 0.0, ["Wv", "Wh", "zt"])
-    fill(T.Bm[:, 0:2 * BW], 0.0, ["B0", "B1"])
-    ts(T.pj[:], T.pi[:], 15, None, (A.bitwise_and,), ["pi"], ["pj"])
-    fill(T.PA[:], 0.0, arow)
+    fill(T.PA[:, 0:2560], 0.0, ["PAa"])
 
-    def split(a, n, o, r, w):
-        ts(T.Cb[:, o:o + n], T.Ci[:, a:a + n], 16.0, 0.0, (A.subtract, A.max), r, [w + "h"])
-        tt(T.Cb[:, o + n:o + 2 * n], T.Ci[:, a:a + n], T.Cb[:, o:o + n], A.subtract, r + [w + "h"], [w + "l"])
+    def split(a, n, o, r, w, parts="hl"):
+        if "h" in parts:
+            ts(T.Cb[:, o:o + n], T.Ci[:, a:a + n], 16.0, 0.0, (A.subtract, A.max), r, [w + "h"])
+        if "l" in parts:
+            tt(T.Cb[:, o + n:o + 2 * n], T.Ci[:, a:a + n], T.Cb[:, o:o + n], A.subtract, r + [w + "h"], [w + "l"])
 
     def piece(f):
         return T.Cb[64 * (f // 2):64 * (f // 2) + 64, 384 * (f % 2):384 * (f % 2) + 384], "Cp" + "hl"[f % 2]
+    split(0, 384, 0, ["Ci0", "Ci1"], "Cp", "h")
+    fill(T.PA[:, 2560:V0], 0.0, ["PAb"])
+    split(0, 384, 0, ["Ci0", "Ci1"], "Cp", "l")
+    for f in (0, 2, 1, 3):
+        dma("Y", T.PA[f::16, :], piece(f)[0], [piece(f)[1], "PAa", "PAb"], ["PA_%d" % f])
+    dma("Y", T.Ci[:, 384:576], T.ln[:], [], ["Ci2"])
+    dma("Y", T.X[:, 0:V0], T.x[:], [], ["X0"])
+    for f, step in ((0, 16), (1, 16), (2, 8), (3, 16), (4, 8), (5, 8), (14, 16), (15, 16)):
+        dma("Y", T.PT[f::step, Z:Z + V0], T.PA[f::step, :], arow, ["PT0_%d" % f])
+    ts(T.pj[:], T.pi[:], 15, None, (A.bitwise_and,), ["pi"], ["pj"])
+    copyV(T.ou0[:], T.u0i[:], ["u0i"], ["ou0"])
     copyV(pm, T.pj[:], ["pj"], ["pm"])
     ts(lastrow, T.pj[:], 15.0, None, (A.is_equal,), ["pj"], ["last"])
-    split(0, 384, 0, ["Ci0", "Ci1"], "Cp")
-    for f in (0, 2, 1, 3):
-        dma("Y", T.PA[f::16, :], piece(f)[0], [piece(f)[1]], ["PA_%d" % f])
-    dma("Y", T.Ci[:, 384:576], T.ln[:], [], ["Ci2"])
-    dma("Y", T.wi[:], T.w[:], [], ["wi"])
-    dma("Y", T.X[:, 0:V0], T.x[:], [], ["X0"])
-    copyV(T.ou0[:], T.u0i[:], ["u0i"], ["ou0"])
-    fill(T.PT[:, 0:Z + V0], 0.0, ["PTa"])
-    copyV(T.uf[:, 0:64], T.u0i[:], ["u0i"], ["uf0"])
 
     fills = {"Wv": [(16, 1.0), (0, 0.0)], "Wh": [(6, -0.5), (2, 0.5), (0, 0.0)],
              "B0": [(16, 1.0), (0, 0.0)], "B1": [(6, 0.5), (0, 0.0)], "B2": [(8, -1.0), (6, 0.5), (0, 0.0)], "B3": [(6, 1.0), (2, 0.0)],
-             "B4": [(10, 1.0), (8, 0.0)], "B5": [(10, -1.0), (8, 0.0)], "B6": [(8, 1.0), (6, 0.0)],
+             "B4": [(11, 1.0), (8, 0.0)], "B5": [(11, -1.0), (8, 0.0)], "B6": [(8, 1.0), (6, 0.0)],
              "Wp": [(2, 1.0), (0, 0.0)], "Wj": [(6, 1.0), (2, 0.0)]}
-    cols = {"Wv": T.Ws[:, 0:16:2], "Wh": T.Ws[:, 16:32:2], "Wp": T.Wo[:, 7:71:8], "Wj": T.Wo[:, 71:135:8]}
+    cols = {"Wv": Wv, "Wh": Wh, "Wp": T.Wo[:, 7:71:8], "Wj": T.Wo[:, 71:135:8]}
     for k in range(7):
         cols["B%d" % k] = T.Bm[:, k * BW + 15:k * BW + 143:16]
 
@@ -246,10 +249,10 @@ def rank_program(g, core, T, topo):
                 if lvl < len(fills[k]):
                     top, val = fills[k][lvl]
                     sel(cols[k], [[-16, 8]], A.is_ge, val, -top, k)
-    ents = {W_ID0: [(6, 6, 1.0), (7, 7, 1.0), (10, 6, float(V0))],
-            W_P: [(6, 0, 1.0), (7, 1, 1.0), (6, 4, 1.0), (7, 5, 1.0), (10, 9, 1.0), (10, 10, 1.0)],
-            W_J: [(2, 2, 1.0), (3, 3, 1.0), (4, 2, 1.0), (5, 3, 1.0), (8, 8, 2.0), (9, 9, 2.0), (10, 4, -BIG), (10, 5, -BIG)],
-            W_ID1: [(6, 6, 1.0), (7, 7, 1.0), (10, 6, float(V0 + K))]}
+    ents = {W_ID0: [(6, 6, 1.0), (7, 7, 1.0), (11, 6, float(V0))],
+            W_P: [(6, 0, 1.0), (7, 1, 1.0), (6, 4, 1.0), (7, 5, 1.0), (11, 10, 1.0), (11, 11, 1.0), (11, 4, -BIG), (11, 5, -BIG)],
+            W_J: [(2, 2, 1.0), (3, 3, 1.0), (4, 2, 1.0), (5, 3, 1.0), (8, 8, 2.0), (9, 9, 2.0), (10, 9, 2.0)],
+            W_ID1: [(6, 6, 1.0), (7, 7, 1.0), (11, 6, float(V0 + K))]}
 
     def wfill(ks):
         for lvl in range(8):
@@ -261,37 +264,26 @@ def rank_program(g, core, T, topo):
     def zeros(buf, a, b, names):
         for c in range(a, b, CAP):
             actS(buf[:, c:min(c + CAP, b)], T.Ws[:, 32:32 + min(CAP, b - c)], F.Identity, ["zt"], names)
-    zeros(T.Bm, 2 * BW, 8 * BW, ["B%d" % k for k in range(2, 8)])
-    zeros(T.Wm, 0, 512, [wn(k) for k in range(4)])
+    for k in (0, 2, 4, 6):
+        zeros(T.Bm, k * BW, (k + 2) * BW, ["B%d" % k, "B%d" % (k + 1)])
+    zeros(T.Wm, 0, 384, [wn(k) for k in range(3)])
+    zeros(T.Wm, 384, 512, [wn(3)])
     zeros(T.Wo, 0, 136, ["Wp", "Wj"])
     bfill(["Wv", "Wh"])
     sel(Wk(W_I), [[-1, 128]], A.not_equal, 1.0, 0, wn(W_I), zt)
     bfill(["B1", "B0"])
-    fillS(T.tu[:, 0:8], 0.0, ["tuz"])
     fillS(T.six[:, 0:CV], 0.0, ["sixa"])
     fillS(T.six[:, CV:64], 6.0, ["sixb"])
-    actS(pm192, pm, F.Identity, ["pm"], ["pm192"], scale=192.0)
     actS(Ip, Wk(W_I), F.Identity, [wn(W_I)], ["If0"])
     actS(Wk(W_NI), Wk(W_I), F.Identity, [wn(W_I)], [wn(W_NI)], scale=-1.0)
     iota(T.idt[:], [[64, 3], [0, 64]], 0, "idt")
     iota(T.Cb[:, 1344:1536], [[0, 3], [1, 64]], 0, "Cb7")
     fillS(T.Cb[:, 1536:1728], 1.0, ["Cb8"])
-    actS(T.Cb[:, 1152:1344], T.idt[:], F.Identity, ["idt", "pm192"], ["Cb6"], bias=pm192)
     actS(In, Wk(W_I), F.Identity, [wn(W_I)], ["If1"], scale=-1.0)
     actS(Wk(W_N128), Wk(W_I), F.Identity, [wn(W_I)], [wn(W_N128)], scale=-128.0)
     fillS(T.d0g[:], 0.0, ["n0"])
     lastw["n1"] = lastw["n2"] = lastw["n0"]
     fillS(T.d0m[:], 1.0, ["d0m"])
-    actS(pmneg, pm, F.Identity, ["pm"], ["pmneg"], scale=-16384.0)
-    actS(lastm1, lastrow, F.Identity, ["last"], ["lastm1"], bias=-1.0)
-    actS(T.zs[:], lastrow, F.Identity, ["last"], ["zs"], bias=-1.0, scale=17.0)
-    fillS(T.d0m[:, 0::32], 0.0, ["d0m"])
-    fillS(T.one64[:], 1.0, ["one64"])
-    fillS(T.Sc[:, 0:8], 0.0, ["Scz"])
-    fillS(T.cnt[:], 0.0, ["cnt"])
-    fillS(T.hb[:], 0.0, ["hb"])
-    fillS(T.M[:, 0:Z], 0.0, ["Mz"])
-    fillS(T.Wd[:, 0:CAP], 0.0, ["Wd0"])
     block = [[-16, 8], [0, 16]]
     iota(T.Ct[:], [[16, 64]], CAP, "Ct")
     iota(T.col[:], [[1, 64]], 0, "col")
@@ -305,27 +297,41 @@ def rank_program(g, core, T, topo):
     sel(Wk(W_NF), [[-1, 128]], A.not_equal, -512.0, 0, wn(W_NF), (Wk(W_NU), wn(W_NU)))
     sel(T.Wm[:, W_TRI * 128 + 15:(W_TRI + 1) * 128:16], [[0, 8]], A.is_gt, 0.0, 0, wn(W_TRI), None, 0)
     bfill(["B3", "B4", "B5"])
-    wfill([W_ID0, W_P, W_J, W_ID1])
 
     def row(f, src, name):
-        dma("Y", T.PT[f::16, Z:Z + V0], src, [name, "X0", "PTa"], ["PT0_%d" % f])
+        dma("Y", T.PT[f::16, Z:Z + V0], src, [name, "X0"], ["PT0_%d" % f])
+
+    def spread(*fs):
+        for f in fs:
+            op("G", lambda: g.affine_select(T.Wl[:, f::16], T.Wl[:, f::16], [[-1, 16], [-16, 8]], A.not_equal, 1.0 if f in (4, 5) else -1.0, 0, 1),
+               ["Wz%d" % r for r in range(8)], ["Wl%d" % f])
 
     def late(n):
         if n == 0:
-            copyV(wf, T.wi[:], ["wi"], ["wf"])
-            for f in range(4):
-                row(f, *piece(f))
-            for f, c, name in ((6, 1152, "Cb6"), (7, 1344, "Cb7"), (10, 1536, "Cb8"), (8, 768, "Clh"), (9, 960, "Cll")):
+            for f, c, name in ((6, 1152, "Cb6"), (7, 1344, "Cb7"), (11, 1536, "Cb8"), (8, 768, "Clh"), (9, 960, "Cll")):
                 row(f, T.Cb[:, c:c + 192], name)
-            remote(T.qp0[:], T.X[:, V0:V0 + K], "q0", ["X1"] + prow, "qp0")
-            bfill(["Wp", "Wj", "B2", "B6"])
+            for r in range(8):
+                dma("Y", T.Wl[r::8, :], T.PA[4::8, 0:2048], arow, ["Wz%d" % r])
+            dma("Y", T.wi[:], T.w[:], [], ["wi"])
+            remote(T.qp0[:], T.X[:, V0:V0 + K], "q0", ["X1", "PT0_6"], "qp0")
+            wfill([W_ID0, W_P, W_J])
+            spread(2, 3, 4)
         if n == 1:
+            actS(pm192, pm, F.Identity, ["pm"], ["pm192"], scale=192.0)
+            actS(pmneg, pm, F.Identity, ["pm"], ["pmneg"], scale=-16384.0)
+            actS(lastm1, lastrow, F.Identity, ["last"], ["lastm1"], bias=-1.0)
+            actS(T.Cb[:, 1152:1344], T.idt[:], F.Identity, ["idt", "pm192"], ["Cb6"], bias=pm192)
             actS(Wk(W_MK), Wk(W_MK), F.Abs, [wn(W_MK), "pmneg"], [wn(W_MK)], bias=pmneg, scale=16384.0)
             actS(T.Cf[:], T.Ct[:], F.Identity, ["Ct", "pm"], ["Cf"], bias=pm)
             actS(T.c15[:], T.col[:], F.Identity, ["col", "last"], ["c15"], scale=lastrow)
-            fillS(T.dn[:], lastm1, ["dn", "lastm1"])
+            actS(T.zs[:], lastrow, F.Identity, ["last"], ["zs"], bias=-1.0, scale=17.0)
+        if n == 2:
             actS(Wk(W_N4K), Wk(W_ONE), F.Identity, [wn(W_ONE)], [wn(W_N4K)], scale=-4096.0)
+            fillS(T.dn[:], lastm1, ["dn", "lastm1"])
         if n == 3:
+            copyV(wf, T.wi[:], ["wi"], ["wf"])
+            fill(T.hb[:], 0.0, ["hb"])
+            fill(T.M[:, 0:Z], 0.0, ["Mz"])
             actS(T.Bm[:, B_W * BW + 15:B_W * BW + 143:16], T.Bm[:, 15:143:16], F.Identity, ["B0", "wf"], ["B%d" % B_W], scale=wf)
         if n == 4:
             fillS(T.Wd[:, WD:WD + CAP], 0.0, ["Wd1"])
@@ -350,7 +356,7 @@ def rank_program(g, core, T, topo):
         last = t == RO - 1
         rX = ["X%d" % k for k in range(t + 1)]
         rM = ["M0"] + ["M%d_%d" % (k, h) for k in range(1, t + 1) for h in range(16)]
-        rP = prow + ["PTa"] + ["PT%d_%d" % (k, h) for k in range(1, t + 1) for h in (0, 1)]
+        rP = prow + ["PT%d_%d" % (k, h) for k in range(1, t + 1) for h in (0, 1)]
         rq = ["X%d" % (t + 1)]
         if t > 0:
             rX = rX + ["X%db" % k for k in range(2, t + 1)]
@@ -379,7 +385,8 @@ def rank_program(g, core, T, topo):
             gather(pg[s % 2][:, 16 * a:16 * b], win, offs[s][:, a:b], r + ["ou%d" % s], quarters("pg%d_" % (s % 2), a, b))
 
         def m_test(s):
-            gT(T.cm[:], wins(s)[1], offs[s][:], ask, A.is_ge, rM + rq + ["ou%d" % s], ["cm"])
+            for a, b in ((0, 48), (48, 64)):
+                gT(T.cm[:, 16 * a:16 * b], wins(s)[1], offs[s][:, a:b], T.X[:, o + 16 * a:o + 16 * b], A.is_ge, rM + rq + ["ou%d" % s], ["cm%d" % a])
 
         def x_vec(s, a, b):
             gT(cx[s % 3][:, 16 * a:16 * b], wins(s)[0], offs[s][:, a:b], T.X[:, o + 16 * a:o + 16 * b], A.is_ge, rX + rq + ["ou%d" % s],
@@ -388,14 +395,14 @@ def rank_program(g, core, T, topo):
         def x_get(s):
             gS(T.gy[:], wins(s)[0], offs[s][:, CV:64], rX + ["ou%d" % s], ["gy"])
 
-        def x_open():
-            mw(T.pw0[:, 0:K - LV], W_NI, T.X[:, o + LV:o + K], True, False, rq, ["pw0a"])
+        def x_open(h=0):
+            mw(T.pw0[:, 512 * h:512 * h + K - LV], W_NI, T.X[:, o + LV:o + K], True, False, rq, ["pw0" + "ab"[h]])
 
-        def x_diff():
-            mw(T.pw0[:, 0:K - LV], W_I, T.gy[:], False, True, ["gy"], ["pw0a"])
+        def x_diff(h=0):
+            mw(T.pw0[:, 512 * h:512 * h + K - LV], W_I, T.gy[:], False, True, ["gy"], ["pw0" + "ab"[h]])
 
-        def x_sign(s):
-            actS(cx[s % 3][:, LV:K], T.pw0[:, 0:K - LV], F.Sign, ["pw0a"], quarters("cx%d_" % (s % 3), CV, 64), bias=0.5)
+        def x_sign(s, h=0):
+            actS(cx[s % 3][:, LV:K], T.pw0[:, 512 * h:512 * h + K - LV], F.Sign, ["pw0" + "ab"[h]], quarters("cx%d_" % (s % 3), CV, 64), bias=0.5)
 
         def votes_x(s, bank, bn, start=True, c=0):
             mw(bank[:, c:c + 64], W_I, T.six[:], start, False, ["sixa", "sixb"], [bn])
@@ -405,32 +412,36 @@ def rank_program(g, core, T, topo):
             actS(T.na[:], bank[:, c:c + 64], F.Relu, [bn], ["na"], bias=-9.0)
             actS(nap(s), T.na[:], F.Relu, ["na"], [nn[s]], bias=1.0, scale=-1.0)
 
-        def differences():
-            for a, (p, m) in enumerate(((2, 1), (1, 0))):
-                mm(T.pw1[:, 513 + a:768:4], Ip, uf(p), True, False, ["If0", "uf%d" % p], ["pw1b"])
-                mm(T.pw1[:, 513 + a:768:4], In, uf(m), False, True, ["If1", "uf%d" % m], ["pw1b"])
-            mm(T.pw1[:, 515:768:4], Ip, uf(0), True, True, ["If0", "uf0"], ["pw1b"])
+        def entry(a):
+            if a < 3:
+                mm(T.pw1[:, 512 + a:768:4], In, uf(2 - a), True, False, ["If1", "uf%d" % (2 - a)], ["pw1b"])
+            mm(T.pw1[:, 512 + a:768:4], Ip, uf(3 - a), a == 3, True, ["If0", "uf%d" % (3 - a)], ["pw1b"])
 
         def turn_back(out, bn):
-            mm(out, T.tu[:, 8:136], T.If[:, 0:128:2], False, False, ["tu", "If0"], [bn])
-            mm(out, T.tu[:, 0:128], T.If[:, 1:128:2], False, True, ["tu", "tuz", "If0"], [bn])
+            mm(out, T.tu[:, 1:17, :], T.If[:, 0:128:2], False, False, ["tu", "If0"], [bn])
+            mm(out, T.tu[:, 0:16, :], T.If[:, 1:128:2], False, True, ["tu", "If0"], [bn])
 
         def choose_p():
             scan(T.sp[:], T.d0g[:], T.pw1[:, 512:768], A.mult, A.add, nn + ["pw1b"], ["sp"])
+            if t == 0:
+                fill(T.d0m[:, 0::32], 0.0, ["d0m"])
             copyV(T.op[:], T.sp[:, 3::4], ["sp"], ["op"])
+            if t == 0:
+                fill(T.cnt[:], 0.0, ["cnt"])
 
         def turns(s):
-            turn(T.pa, Wv, T.cm, ["cm", "Wv"], ["pa"])
-            turn(T.pb, Wh, pg[s % 2], quarters("pg%d_" % (s % 2), 0, 64) + ["Wh"], ["pb"])
+            turn(T.pa, Wv, T.cm, ["cm0", "Wv"], ["pa"], 0, 96)
+            turn(T.pa, Wv, T.cm, ["cm48", "Wv"], ["pa"], 96, 128)
+            turn(T.pb, Wh, pg[s % 2], quarters("pg%d_" % (s % 2), 0, 64) + ["Wh"], ["pb"], 0, 128)
 
         def sign():
-            actS(T.sg[:], T.pa[:, 0:128], F.Sign, ["pa"], ["sg"], bias=-9.5)
+            actS(T.sg[:], T.pa[:, 0:64], F.Sign, ["pa"], ["sg"], bias=-9.5)
 
         def middle(s, k=B_SH, out=T.pc[:, 0:64], bn="pc"):
             extract(out, k, pg[s % 2], quarters("pg%d_" % (s % 2), 0, 64), [bn], stop=False)
 
         def signed():
-            tt(T.tu[:, 8:136], T.pb[:, 0:128], T.sg[:], A.mult, ["pb", "sg"], ["tu"])
+            tt(T.tu[:, 1:17:2, :], T.pb[:, 0:64], T.sg[:], A.mult, ["pb", "sg"], ["tu"])
 
         def advance(s):
             copyV(offs[s + 1][:], T.pc[:, 0:64], ["pc"], ["ou%d" % (s + 1)])
@@ -441,38 +452,44 @@ def rank_program(g, core, T, topo):
         for s in range(3):
             if t == 0 and s == 0:
                 m_test(0)
-                pointers(0, gS, 24, 64)
-                pointers(0, gV, 0, 24)
+                pointers(0, gS, 16, 64)
+                pointers(0, gV, 0, 16)
                 turns(0)
                 sign()
-                split(384, 192, 768, ["Ci2"], "Cl")
+                split(384, 192, 768, ["Ci2"], "Cl", "h")
+                fill(T.tu[:], 0.0, ["tu"])
+                fill(T.one64[:], 1.0, ["one64"])
                 middle(0)
                 signed()
+                split(384, 192, 768, ["Ci2"], "Cl", "l")
+                copyV(uf(0), T.u0i[:], ["u0i"], ["uf0"])
+                fill(T.Sc[:, 0:8], 0.0, ["Scz"])
                 late(1)
-                x_open()
                 turn_back(T.pc[:, 0:64], "pc")
                 late(0)
-                x_get(0)
                 advance(0)
-                x_diff()
             elif t == 0 and s == 1:
                 pointers(1)
                 m_test(1)
-                x_sign(0)
+                x_open()
+                x_open(1)
+                x_get(0)
                 turns(1)
+                x_diff()
                 x_vec(0, 0, 40)
                 sign()
                 x_get(1)
+                x_sign(0)
                 middle(1)
                 signed()
-                x_open()
                 turn_back(T.pc[:, 0:64], "pc")
-                x_diff()
-                x_sign(1)
+                x_diff(1)
+                x_sign(1, 1)
                 x_vec(0, 40, CV)
                 x_vec(1, 0, 16)
                 advance(1)
             elif last and s == 2:
+                dma("Y", T.ge[:], ask, rq, ["ge0", "ge1"])
                 x_get(2)
                 open_choice()
                 pointers(2)
@@ -480,7 +497,8 @@ def rank_program(g, core, T, topo):
                 votes_x(1, T.pd, "pd")
                 x_open()
                 x_diff()
-                differences()
+                for a in (3, 2, 1):
+                    entry(a)
                 turns(2)
                 x_vec(2, 0, CV)
                 x_sign(2)
@@ -496,8 +514,6 @@ def rank_program(g, core, T, topo):
                 if t == 0:
                     gaps = [[(1, 16, CV), (2, 0, 8)], [(2, 8, CV)]]
                     copyV(uf(1), offs[1][:], ["ou1"], ["uf1"])
-                if s == 2:
-                    open_choice()
                 pointers(s)
                 m_test(s)
                 if t == 1 and s == 0:
@@ -508,25 +524,34 @@ def rank_program(g, core, T, topo):
                     out_mm(t - 1, 0)
                     out_mm(t - 1, 1)
                 if s == 2:
-                    differences()
-                    mm(T.pw1[:, 512:768:4], In, uf(2), True, False, ["If1", "uf2"], ["pw1b"])
+                    entry(3)
+                    entry(2)
                 x_open()
                 turns(s)
                 x_get(s)
-                x_diff()
+                if s == 2:
+                    x_diff()
                 for x in gaps[0]:
                     x_vec(*x)
                 sign()
-                if t == 1 and s == 1:
-                    late(4)
-                middle(s)
-                signed()
-                turn_back(T.pc[:, 0:64], "pc")
-                x_sign(s)
                 if s > 0:
                     stays(s - 1 - (t == 0))
                 if s == 0:
                     out_store(t - 1, "Y")
+                    if t == 1:
+                        late(4)
+                middle(s)
+                if s < 2:
+                    x_diff()
+                signed()
+                if s == 2:
+                    copyV(uf(2), offs[2][:], ["ou2"], ["uf2"])
+                turn_back(T.pc[:, 0:64], "pc")
+                if s == 2:
+                    entry(1)
+                x_sign(s)
+                if t == 0:
+                    late(2)
                 if t == 0:
                     votes_x(1, T.pw0, "pw0b", c=512)
                 for x in gaps[1]:
@@ -536,11 +561,9 @@ def rank_program(g, core, T, topo):
                 if s == 1:
                     copyV(uf(1), offs[1][:], ["ou1"], ["uf1"])
                 advance(s)
-                if t == 0:
-                    ts(nap(1), T.pw0[:, 512:576], 9.5, None, (A.is_lt,), ["pw0b"], ["n1"])
 
         wx, wm, wp = wins(2)
-        wz_m, wz_p = T.M[:, 0:Z + o], T.PT[:, 0:Z + o]
+        wz_m = T.M[:, 0:Z + o]
         pf = T.sp[:, 3::4]
 
         def half(h):
@@ -558,28 +581,34 @@ def rank_program(g, core, T, topo):
         if not last:
             x_get(3)
             actS(uf(3), T.pc[:, 0:64], F.Identity, ["pc"], ["uf3"])
-            x_vec(3, 0, CV)
+            if t == 0:
+                x_vec(3, 0, 20)
+                ts(nap(1), T.pw0[:, 512:576], 9.5, None, (A.is_lt,), ["pw0b"], ["n1"])
+            x_vec(3, 20 * (t == 0), CV)
             votes_x(2, T.pd, "pd")
             x_open()
             x_diff()
-            mm(T.pw1[:, 512:768:4], Ip, uf(3), False, True, ["If0", "uf3"], ["pw1b"])
+            entry(0)
             stays(2)
             x_sign(3)
             mm(T.pc[:, 1:128:2], Ip, T.Cf[:], True, True, ["If0", "Cf"], ["pc"])
             mw(T.pb[:, 0:128], W_NI, Wk(W_MK), True, False, [wn(W_MK)], ["pb"])
             mw(T.pb[:, 1:128:2], W_I, T.far[:], False, False, ["far"], ["pb"])
+
+            def query(bn, h):
+                mw(T[bn][:, half(h)], W_I, T.X[:, o + 512 * h:o + 512 * h + 512], True, False, rq, [bn + "ab"[h]])
+            query("pw1", 0)
             for s in range(3):
                 mw(T.pa[:, 0:64], W_N128, nap(s), s == 0, False, [nn[s]], ["pa"])
             choose_p()
             votes_x(3, T.pa, "pa", start=False)
-            for bn in ("pw0", "pw1"):
-                for h in (0, 1):
-                    mw(T[bn][:, half(h)], W_I, T.X[:, o + 512 * h:o + 512 * h + 512], True, False, rq, [bn + "ab"[h]])
-            if t == 0:
-                late(3)
+            query("pw0", 0)
+            query("pw0", 1)
             part(gS, "pgp", wp, T.op, 20, 64, rP + ["op"])
             part(gV, "pgp", wp, T.op, 0, 8, rP + ["op"])
             ts(T.fb[:], T.pa[:, 0:64], 9.5 - 384.0, None, (A.is_lt,), ["pa"], ["fb"])
+            if t == 0:
+                fill(T.Wd[:, 0:CAP], 0.0, ["Wd0"])
             scan(T.Sc[:, 8:72], T.one64[:], T.fb[:], A.mult, A.add, ["one64", "fb"], ["Sc"])
             incl, excl = T.Sc[:, 8:72], T.Sc[:, 7:71]
             mw(T.pa[:, 0:64], W_I, T.c15[:], True, False, ["c15"], ["pa"])
@@ -593,8 +622,11 @@ def rank_program(g, core, T, topo):
             scan(T.sst[:], T.d0m[:], T.pb[:, 0:128], A.mult, A.max, ["d0m", "pb"], ["sst"])
             ts(T.cnt[:, 15:16], T.pc[:, 256:257], float(CAP), 192.0, (A.min, A.subtract), ["pc"], ["cnt"])
             remote(T["got%d" % t][:], T.cnt[:], "h%d" % t, ["cnt"], "got%d" % t)
+            if t == 0:
+                spread(5, 8, 9)
             copyV(T.ost[:], T.sst[:, 31::32], ["sst"], ["ost"])
             mm(T.pd[:, 0:64], Ip, pf, True, True, ["If0", "sp"], ["pd"])
+            query("pw1", 1)
             extract(T.pd[:, 64:128], B_J, T.pgp, whole("pgp"), ["pd"])
             part(gS, "gx", wx, T.op, 0, GX, rX + ["op"])
             op("V", lambda: vec.tensor_copy(T.Wd[:, WD * t:WD * t + WD].indirect(T.ost[:]), T.Rk[:]), ["Rk", "ost"], ["Wd%d" % t])
@@ -620,50 +652,60 @@ def rank_program(g, core, T, topo):
             def born(h):
                 mw(T.pw0[:, half(h)], W_ID0 + t, T.PT[:, Z + 512 * h:Z + 512 * h + 512], True, False, rP, ["pw0" + "ab"[h]])
                 mw(T.pw0[:, half(h)], W_P, T.pgp[:, half(h)], False, False, halfof("pgp", h), ["pw0" + "ab"[h]])
+                mw(T.pw0[:, half(h)], W_J, T.pgj[:, half(h)], False, False, halfof("pgj", h), ["pw0" + "ab"[h]])
+
+                def fn():
+                    for i in range(16):
+                        ins = pe.matmul(T.pw0[:, 512 * h + i:512 * h + 512:16], T.Wl[:, 128 * i:128 * i + 128], T.ad[:, 32 * h:32 * h + 32],
+                                        False, i == 15)
+                    return ins
+                op("P", fn, ["ad"] + ["Wl%d" % f for f in (2, 3, 4, 5, 8, 9)], ["pw0" + "ab"[h]])
 
             def bounds(a, b):
                 gT(T.M[:, Z + o + 16 * a:Z + o + 16 * b], wz_m, T.opj[:, 64 + a:64 + b], T.tm[:, 16 * a:16 * b], A.max,
-                   rM + ["Mz", "opj", "tm"], quarters("M%d_" % (t + 1), a, b))
+                   rM + ["Mz", "opj"] + quarters("tm", a, b), quarters("M%d_" % (t + 1), a, b))
 
             def rows(h):
                 actS(T.PT[:, Z + o + 512 * h:Z + o + 512 * h + 512], T.pw0[:, half(h)], F.Relu, ["pw0" + "ab"[h]], ["PT%d_%d" % (t + 1, h)])
             extract(T.pa[:, 0:64], B_LP, T.pgp, whole("pgp"), ["pa"], stop=False)
             part(gS, "pgj", wp, T.oj, PJ, 64, rP + ["oj"])
-            part(gV, "gx", wx, T.op, GX, 64, rX + ["op"])
             part(gV, "pgj", wp, T.oj, 0, PJ, rP + ["oj"])
+            part(gS, "gx", wx, T.op, GX, 64, rX + ["op"])
             sums("pw0", 0)
-            sums("pw1", 0)
             extract(T.pb[:, 0:24], B_ONE, T.Zc, ["Zc"], ["pb"], n=CAP)
-            sums("pw0", 1)
             copyV(T.inv[:], T.pb[:, 0:24], ["pb"], ["inv"])
             remote(T["who%d" % t][:], T.inv[:], "d%d" % t, ["inv"], "who%d" % t)
             extract(T.pa[:, 0:64], B_LN, T.pgj, whole("pgj"), ["pa"], start=False)
+            sums("pw0", 1)
+            sums("pw1", 0)
             wraps(0)
             wraps(1)
+            if t == 0:
+                late(3)
+                bfill(["Wp", "Wj", "B2", "B6"])
+                wfill([W_ID1])
             kept(0)
             sums("pw1", 1)
             kept(1)
+            ts(T.ad[:], T.pa[:, 0:64], 0.0, BIG, (A.not_equal, A.mult), ["pa"], ["ad"])
             born(0)
             born(1)
-            ts(T.ad[:], T.pa[:, 0:64], 0.0, BIG, (A.not_equal, A.mult), ["pa"], ["ad"])
             ts(T.hb[:, 1::2], T.pc[:, 128:192], 511.0 - 192.0, T["got%d" % t][:, 15:16], (A.add, A.is_lt), ["pc", "got%d" % t], ["hb"])
             for h in (0, 1):
                 tt(T.yy[:, 64 * h:64 * h + 64], T.pd[:, 64 * h:64 * h + 64], T.ad[:], A.subtract, ["pd", "ad"], ["yy" + "ab"[h]])
             scan(T.sidx[:], T.hb[:], T.pc[:, 0:128], A.mult, A.add, ["hb", "pc"], ["sidx"])
             ts(T.opj[:], T.yy[:], float(Z), None, (A.add,), ["yya", "yyb"], ["opj"])
             copyV(T.oidx[:], T.sidx[:, 1::2], ["sidx"], ["oidx"])
-            gT(T.tm[:], wz_m, T.opj[:, 0:64], ask, A.max, rM + rq + ["Mz", "opj"], ["tm"])
-            part(gS, "pgz", wz_p, T.opj, 0, PZ, rP + ["opj"], 64)
+            for h in (0, 1):
+                gT(T.tm[:, half(h)], wz_m, T.opj[:, 32 * h:32 * h + 32], T.X[:, o + 512 * h:o + 512 * h + 512], A.max,
+                   rM + rq + ["Mz", "opj"], halfof("tm", h))
             gS(T.tab[:, 0:CAP], T["qp%d" % t][:], T["who%d" % t][:], ["qp%d" % t, "who%d" % t], ["taba"])
-            bounds(0, 20)
+            bounds(0, 16)
             rt = ["taba", "tabc0", "tabc1", "oidx"]
             gS(T.X[:, o + K + 16 * CF:o + 2 * K], T.tab[:], T.oidx[:, CF:64], rt, ["X%db" % (t + 2)])
             gV(T.X[:, o + K:o + K + 16 * CF], T.tab[:], T.oidx[:, 0:CF], rt, ["X%d" % (t + 2)])
-            bounds(20, 52)
-            part(gS, "pgz", wz_p, T.opj, PZ, 64, rP + ["opj"], 64)
-            mw(T.pw0[:, half(0)], W_J, T.pgz[:, half(0)], False, True, halfof("pgz", 0), ["pw0a"])
+            bounds(16, 52)
             extract(T.pb[:, 0:64], B_W, T.X, ["X%d" % (t + 2), "X%db" % (t + 2)], ["pb"], c0=o + K)
-            mw(T.pw0[:, half(1)], W_J, T.pgz[:, half(1)], False, True, halfof("pgz", 1), ["pw0b"])
             rows(0)
             rows(1)
             copyV(T.h0[:], T.pb[:, 0:64], ["pb"], ["h0"])
@@ -690,16 +732,17 @@ def rank_program(g, core, T, topo):
             part(gS, "pgp", wp, T.op, 32, 64, rP + ["op"])
             part(gV, "pgp", wp, T.op, 0, 32, rP + ["op"])
             extract(T.pd[:, 0:64], B_J, T.pgp, whole("pgp"), ["pd"])
-            with_p(0, 32)
+            part(gS, "tm", wm, T.op, 0, 16, rM + ["op"])
+            part(gS, "tm", wm, T.op, 52, 64, rM + ["op"])
+            with_p(16, 52)
             copyV(T.oj[:], T.pd[:, 0:64], ["pd"], ["oj"])
             across(T.pb[:, 0:64], B_ID, T.pgp, "pgp", "pb", True, True)
             extract(T.pa[:, 0:64], B_LP, T.pgp, whole("pgp"), ["pa"], stop=False)
             across(T.pc[:, 0:64], B_LP, T.pgp, "pgp", "pc", True, False)
-            part(gS, "pgj", wp, T.oj, 0, 64, rP + ["oj"])
-            with_p(32, 64)
+            part(gS, "pgj", wp, T.oj, 16, 64, rP + ["oj"])
+            part(gV, "pgj", wp, T.oj, 0, 16, rP + ["oj"])
             copyV(T.yo[:, 0:64], T.pb[:, 0:64], ["pb"], ["yo"])
-            with_j(0, 32)
-            with_j(32, 64)
+            with_j(0, 64)
             dma("Y", T.ypar[:, K * t:K * t + K], T.yo[:, 0:64], ["yo"], [])
             mm(T.pb[:, 0:64], In, T.yo[:, 0:64], True, False, ["If1", "yo"], ["pb"])
             extract(T.pa[:, 0:64], B_LN, T.pgj, whole("pgj"), ["pa"], start=False)
@@ -711,15 +754,18 @@ def rank_program(g, core, T, topo):
             ts(T.na[:], T.pc[:, 0:64], 0.0, None, (A.is_equal,), ["pc"], ["na"])
             rt = rq + whole("both") + ["oidx"]
 
-            def store(gather, q, a, b):
-                part(gather, "gx", T.X[:, o:o + 2 * K], T.oidx, a, b, rt)
-                dma(q, T.ym[:, K * t + 16 * a:K * t + 16 * b], T.gx[:, 16 * a:16 * b], quarters("gx", a, b), [])
-            store(gS, "Y", CL, 48)
+            def with_q(a, b):
+                gT(T.gx[:, 16 * a:16 * b], T.X[:, o:o + 2 * K], T.oidx[:, a:b], T.ge[:, 16 * a:16 * b], A.max, rt + ["ge0"], quarters("gx", a, b))
+            part(gS, "gx", T.X[:, o:o + 2 * K], T.oidx, 16, 32, rt)
+            with_q(0, 16)
+            dma("Y", T.ym[:, K * t:K * t + 512], T.gx[:, half(0)], halfof("gx", 0), [])
+            part(gS, "gx", T.X[:, o:o + 2 * K], T.oidx, 32, 52, rt)
             tt(T.yy[:, 64:128], T.pb[:, 0:64], T.na[:], A.mult, ["pb", "na"], ["yyb"])
-            store(gV, "Y", 0, CL)
+            with_q(52, 64)
+            dma("S", T.ym[:, K * t + 512:K * t + K], T.gx[:, half(1)], halfof("gx", 1), [])
             tt(T.yo[:, 64:128], T.yy[:, 64:128], T.yo[:, 0:64], A.add, ["yyb", "yo"], ["yoj"])
-            store(gS, "S", 48, 64)
             dma("Y", T.yjump[:, K * t:K * t + K], T.yo[:, 64:128], ["yoj"], [])
 
-    for s in total:
-        g.wait_ge(T.sem[s], total[s])
+    rest = [s for s in total if waited.get(s, 0) < total[s]]
+    for s in sorted(rest, key=lambda s: s in ("sV", "sS", "sP")):
+        Q[ending.get(s, "G")].wait_ge(T.sem[s], total[s])

from concourse.mybir import AluOpType as A, ActivationFunctionType as F

V0, K, CAP, RO = 3072, 1024, 384, 3
Z = 16
CV = 48
C1 = 28
CF = 32
GX = 48
PJ = 32
BIG = 8192.0
BW = 144
WD = 3104
B_ONE, B_SH, B_SI, B_J, B_LP, B_LN, B_ID, B_W = range(8)
W_P, W_J, W_ID0, W_ID1, W_I, W_NI, W_N128, W_ONE, W_NU, W_NF, W_TRI, W_N4K, W_MK = range(13)

bf, f32, i32, u16 = "bfloat16", "float32", "int32", "uint16"
SCRATCH = {
    "X": ("sbuf", [128, V0 + RO * K + K], bf), "M": ("sbuf", [128, Z + V0 + RO * K], bf), "PT": ("sbuf", [128, Z + V0 + RO * K], bf),
    "PA": ("sbuf", [128, V0], bf),
    "Ci": ("sbuf", [128, 576], i32), "Cb": ("sbuf", [128, 1728], bf), "idt": ("sbuf", [128, 192], bf),
    "u0i": ("sbuf", [128, 64], i32), "wi": ("sbuf", [128, 1], i32), "pi": ("sbuf", [128, 1], i32), "pj": ("sbuf", [128, 1], i32),
    "cl": ("sbuf", [128, 8], f32), "zs": ("sbuf", [128, 1], bf),
    "Ct": ("sbuf", [128, 64], f32), "Cf": ("sbuf", [128, 64], f32), "col": ("sbuf", [128, 64], bf), "c15": ("sbuf", [128, 64], bf),
    "six": ("sbuf", [128, 64], bf), "dn": ("sbuf", [128, CAP], bf), "far": ("sbuf", [128, 64], bf),
    "ou0": ("sbuf", [128, 64], u16), "ou1": ("sbuf", [128, 64], u16), "ou2": ("sbuf", [128, 64], u16), "ou3": ("sbuf", [128, 64], u16),
    "op": ("sbuf", [128, 64], u16), "oj": ("sbuf", [128, 64], u16), "opj": ("sbuf", [128, 128], u16), "oidx": ("sbuf", [128, 64], u16),
    "ost": ("sbuf", [128, 4], u16),
    "cm": ("sbuf", [128, K], bf), "cx0": ("sbuf", [128, K], bf), "cx1": ("sbuf", [128, K], bf), "cx2": ("sbuf", [128, K], bf), "gx": ("sbuf", [128, K], bf),
    "gy": ("sbuf", [128, K - 16 * CV], bf),
    "pg0": ("sbuf", [128, K], bf), "pg1": ("sbuf", [128, K], bf), "pgp": ("sbuf", [128, K], bf), "pgj": ("sbuf", [128, K], bf),
    "Wl": ("sbuf", [128, 16 * 128], bf), "ge": ("sbuf", [128, K], bf), "tm": ("sbuf", [128, K], bf),
    "uf": ("sbuf", [128, 256], f32), "sg": ("sbuf", [128, 64], bf), "tu": ("sbuf", [128, 17, 8], f32),
    "sp": ("sbuf", [128, 256], f32), "sst": ("sbuf", [128, 128], f32), "sidx": ("sbuf", [128, 128], f32),
    "d0g": ("sbuf", [128, 256], bf), "d0m": ("sbuf", [128, 128], bf),
    "fb": ("sbuf", [128, 64], bf), "hb": ("sbuf", [128, 128], bf), "Rk": ("sbuf", [128, 64], bf),
    "one64": ("sbuf", [128, 64], bf), "na": ("sbuf", [128, 64], f32), "ad": ("sbuf", [128, 64], bf), "yy": ("sbuf", [128, 128], f32),
    "h0": ("sbuf", [128, 64], i32), "h1": ("sbuf", [128, 64], i32), "Sc": ("sbuf", [128, 72], bf),
    "Wd": ("sbuf", [128, 2 * WD], bf), "Zr": ("sbuf", [128, CAP], bf), "Zc": ("sbuf", [128, CAP], bf),
    "cnt": ("sbuf", [128, 16], bf), "got0": ("sbuf", [128, 16], bf), "got1": ("sbuf", [128, 16], bf),
    "inv": ("sbuf", [128, 24], u16), "who0": ("sbuf", [128, 24], u16), "who1": ("sbuf", [128, 24], u16),
    "qp0": ("sbuf", [128, K], bf), "qp1": ("sbuf", [128, K], bf), "tab": ("sbuf", [128, CAP + K], bf),
    "Bm": ("sbuf", [128, 8 * BW], bf), "Wm": ("sbuf", [128, 13 * 128], bf), "Ws": ("sbuf", [128, 32 + CAP], bf), "Wo": ("sbuf", [128, 136], bf),
    "If": ("sbuf", [128, 256], f32), "yo": ("sbuf", [128, 128], f32),
    "pw0": ("psum", [128, 1024], f32), "pw1": ("psum", [128, 1024], f32),
    "pa": ("psum", [128, 512], f32), "pb": ("psum", [128, 512], f32), "pc": ("psum", [128, 512], f32), "pd": ("psum", [128, 512], f32),
}
NDMA = 46
SEMAPHORES = (["sV", "sS", "sP", "sG"] + [a + b + c for a in ("arr", "sent") for b in "qhd" for c in "01"]
              + ["d%d" % k for k in range(NDMA)])
BANKS = ("pw0a", "pw0b", "pw1a", "pw1b", "pa", "pb", "pc", "pd")


def rank_program(g, core, T, topo):
    rank = T.rank_of(core)
    if rank is None:
        return
    nxt = T.cores[(rank + 1) % len(T.cores)]
    Q = {"V": g.vector, "S": g.scalar, "P": g.tensor, "G": g, "Y": g.sync}
    total = {}
    known = {q: {} for q in Q}
    clock = {}
    lastw, readers = {}, {}
    waited, ending = {}, {}
    ndma = [0]

    def need(q, ev):
        s, c = ev[1], ev[2]
        if known[q].get(s, 0) >= c:
            return
        Q[q].wait_ge(T.sem[s], c)
        waited[s] = max(waited.get(s, 0), c)
        known[q][s] = c
        for s2, c2 in clock.get((s, c), {}).items():
            if known[q].get(s2, 0) < c2:
                known[q][s2] = c2

    def order(q, eng, r, w):
        evs = []
        for x in r:
            if x in lastw:
                evs.append(lastw[x])
            if x in BANKS:
                evs += [e for e in readers.get(x, []) if e[0] != eng]
        for x in w:
            if x in lastw and not (eng == "P" and lastw[x][0] == "P"):
                evs.append(lastw[x])
            evs += readers.get(x, [])
        best = {}
        for e in evs:
            if best.get(e[1], (0, 0, 0))[2] < e[2]:
                best[e[1]] = e
        for e in sorted(best.values(), key=lambda e: -len(clock.get((e[1], e[2]), {}))):
            need(q, e)

    def note(ev, q, r, w):
        clock[(ev[1], ev[2])] = dict(known[q])
        for x in r:
            readers.setdefault(x, []).append(ev)
        for x in w:
            lastw[x] = ev
            readers[x] = []

    def op(q, fn, r, w):
        order(q, q, r, w)
        s = "s" + q
        total[s] = total.get(s, 0) + 1
        fn().then_inc(T.sem[s], 1)
        note((q, s, total[s]), q, r, w)

    def dma(q, out, in_, r, w):
        order(q, "D", r, w)
        s = "d%d" % ndma[0]
        ndma[0] += 1
        total[s] = 16
        ending[s] = q
        Q[q].dma_start(out, in_).then_inc(T.sem[s], 16)
        note(("D", s, 16), q, r, w)

    rid, pid, _ = topo.addr(nxt)
    mask = topo.mask(core, nxt)
    neng = len(topo.engines(core, nxt))

    def remote(out, in_, tag, r, land):
        order("G", "D", r, [])
        g.remote_dma(out, in_, T.sem["arr" + tag], T.sem["sent" + tag], pid, rid, mask)
        total["sent" + tag] = neng
        total["arr" + tag] = neng
        note(("D", "sent" + tag, neng), "G", r, [])
        lastw[land] = ("D", "arr" + tag, neng)

    vec, act, pe = g.vector, g.scalar, g.tensor

    def Bi(k, i):
        return T.Bm[:, k * BW + 15 - i:k * BW + 143 - i]

    def Wk(k):
        return T.Wm[:, k * 128:(k + 1) * 128]

    def wn(k):
        return "W%d" % k

    def extract(out, k, src, r, w, start=True, stop=True, c0=0, n=K):
        def fn():
            for i in range(16):
                ins = pe.matmul(out, Bi(k, i), src[:, c0 + i:c0 + n:16], start and i == 0, stop and i == 15)
            return ins
        op("P", fn, r + ["B%d" % k], w)

    def turn(bank, wts, src, r, w, m0, m1):
        def fn():
            for b in range(8):
                ins = pe.matmul(bank[m0:m1, b:64:8], src[:, 8 * m0 + b:8 * m1:8], wts, True, True)
            return ins
        op("P", fn, r, w)

    def mm(out, lhsT, rhs, start, stop, r, w):
        op("P", lambda: pe.matmul(out, lhsT, rhs, start, stop), r, w)

    def mw(out, k, rhs, start, stop, r, w):
        mm(out, Wk(k), rhs, start, stop, r + [wn(k)], w)

    def gS(out, win, off, r, w):
        op("S", lambda: act.activation(out, win.indirect(off), F.Identity), r, w)

    def gV(out, win, off, r, w):
        op("V", lambda: vec.tensor_copy(out, win.indirect(off)), r, w)

    def gT(out, win, off, in1, alu, r, w):
        op("V", lambda: vec.tensor_tensor(out, win.indirect(off), in1, alu), r, w)

    def sel(ap, pattern, cmp, fill, base, name, src=None, cm=1):
        if src is None:
            op("G", lambda: g.affine_select(ap, ap, pattern, cmp, fill, base, cm), [name], [name])
        else:
            op("G", lambda: g.affine_select(ap, src[0], pattern, cmp, fill, base, cm), [src[1]], [name])

    def iota(ap, pattern, base, name):
        op("G", lambda: g.iota(ap, pattern, base, 0, allow_small_or_imprecise_dtypes=True), [], [name])

    def fill(ap, val, names):
        op("V", lambda: vec.memset(ap, val), [], names)

    def copyV(out, in_, r, w):
        op("V", lambda: vec.tensor_copy(out, in_), r, w)

    def ts(out, in_, s1, s2, ops, r, w):
        op("V", lambda: vec.tensor_scalar(out, in_, s1, s2, *ops), r, w)

    def tt(out, in0, in1, alu, r, w):
        op("V", lambda: vec.tensor_tensor(out, in0, in1, alu), r, w)

    def scan(out, d0, d1, op0, op1, r, w):
        op("V", lambda: vec.tensor_tensor_scan(out, d0, d1, 0.0, op0, op1), r, w)

    def actS(out, in_, func, r, w, bias=0.0, scale=1.0):
        op("S", lambda: act.activation(out, in_, func, bias=bias, scale=scale), r, w)

    def fillS(ap, val, names):
        actS(ap, T.Ws[:, 32:32 + ap.shape[1]], F.Identity, ["zt"] + names[1:], names[:1], bias=val)

    dma("Y", T.Ci[0:64, 0:384], T.par[:], [], ["Ci0"])
    dma("S", T.Ci[64:128, 0:384], T.jump[:], [], ["Ci1"])
    dma("Y", T.u0i[:], T.u0[:], [], ["u0i"])
    dma("S", T.X[:, V0:V0 + K], T.q[:], [], ["X1"])
    dma("Y", T.M[:, Z:Z + V0], T.m[:], [], ["M0"])

    prow = ["PT0_%d" % f for f in range(16)]
    arow = ["PA_%d" % f for f in range(4)]
    Wv, Wh, zt = T.Ws[:, 0:8], T.Ws[:, 16:24], (T.Ws[:, 32:160], "zt")
    Ip, In = T.If[:, 0:128], T.If[:, 128:256]
    pm, lastrow, pm192, pmneg, lastm1, wf = [T.cl[:, k:k + 1] for k in range(6)]
    op("G", lambda: g.iota(T.pi[:], [[0, 1]], 0, 1), [], ["pi"])
    fill(T.Ws[:], 0.0, ["Wv", "Wh", "zt"])
    fill(T.PA[:, 0:2560], 0.0, ["PAa"])

    def split(a, n, o, r, w, parts="hl"):
        if "h" in parts:
            ts(T.Cb[:, o:o + n], T.Ci[:, a:a + n], 16.0, 0.0, (A.subtract, A.max), r, [w + "h"])
        if "l" in parts:
            tt(T.Cb[:, o + n:o + 2 * n], T.Ci[:, a:a + n], T.Cb[:, o:o + n], A.subtract, r + [w + "h"], [w + "l"])

    def piece(f):
        return T.Cb[64 * (f // 2):64 * (f // 2) + 64, 384 * (f % 2):384 * (f % 2) + 384], "Cp" + "hl"[f % 2]
    split(0, 384, 0, ["Ci0", "Ci1"], "Cp", "h")
    fill(T.PA[:, 2560:V0], 0.0, ["PAb"])
    split(0, 384, 0, ["Ci0", "Ci1"], "Cp", "l")
    for f in (0, 2, 1, 3):
        dma("Y", T.PA[f::16, :], piece(f)[0], [piece(f)[1], "PAa", "PAb"], ["PA_%d" % f])
    dma("Y", T.Ci[:, 384:576], T.ln[:], [], ["Ci2"])
    dma("Y", T.X[:, 0:V0], T.x[:], [], ["X0"])
    for f, step in ((0, 16), (1, 16), (2, 8), (3, 16), (4, 8), (5, 8), (14, 16), (15, 16)):
        dma("Y", T.PT[f::step, Z:Z + V0], T.PA[f::step, :], arow, ["PT0_%d" % f])
    ts(T.pj[:], T.pi[:], 15, None, (A.bitwise_and,), ["pi"], ["pj"])
    copyV(T.ou0[:], T.u0i[:], ["u0i"], ["ou0"])
    copyV(pm, T.pj[:], ["pj"], ["pm"])
    ts(lastrow, T.pj[:], 15.0, None, (A.is_equal,), ["pj"], ["last"])

    fills = {"Wv": [(16, 1.0), (0, 0.0)], "Wh": [(6, -0.5), (2, 0.5), (0, 0.0)],
             "B0": [(16, 1.0), (0, 0.0)], "B1": [(6, 0.5), (0, 0.0)], "B2": [(8, -1.0), (6, 0.5), (0, 0.0)], "B3": [(6, 1.0), (2, 0.0)],
             "B4": [(11, 1.0), (8, 0.0)], "B5": [(11, -1.0), (8, 0.0)], "B6": [(8, 1.0), (6, 0.0)],
             "Wp": [(2, 1.0), (0, 0.0)], "Wj": [(6, 1.0), (2, 0.0)]}
    cols = {"Wv": Wv, "Wh": Wh, "Wp": T.Wo[:, 7:71:8], "Wj": T.Wo[:, 71:135:8]}
    for k in range(7):
        cols["B%d" % k] = T.Bm[:, k * BW + 15:k * BW + 143:16]

    def bfill(ks):
        for lvl in range(3):
            for k in ks:
                if lvl < len(fills[k]):
                    top, val = fills[k][lvl]
                    sel(cols[k], [[-16, 8]], A.is_ge, val, -top, k)
    ents = {W_ID0: [(6, 6, 1.0), (7, 7, 1.0), (11, 6, float(V0))],
            W_P: [(6, 0, 1.0), (7, 1, 1.0), (6, 4, 1.0), (7, 5, 1.0), (11, 10, 1.0), (11, 11, 1.0), (11, 4, -BIG), (11, 5, -BIG)],
            W_J: [(2, 2, 1.0), (3, 3, 1.0), (4, 2, 1.0), (5, 3, 1.0), (8, 8, 2.0), (9, 9, 2.0), (10, 9, 2.0)],
            W_ID1: [(6, 6, 1.0), (7, 7, 1.0), (11, 6, float(V0 + K))]}

    def wfill(ks):
        for lvl in range(8):
            for k in ks:
                if lvl < len(ents[k]):
                    f, f2, val = ents[k][lvl]
                    sel(T.Wm[:, k * 128 + f2:(k + 1) * 128:16], [[-16, 8]], A.not_equal, val, -f, wn(k))

    def zeros(buf, a, b, names):
        for c in range(a, b, CAP):
            actS(buf[:, c:min(c + CAP, b)], T.Ws[:, 32:32 + min(CAP, b - c)], F.Identity, ["zt"], names)
    for k in (0, 2, 4, 6):
        zeros(T.Bm, k * BW, (k + 2) * BW, ["B%d" % k, "B%d" % (k + 1)])
    zeros(T.Wm, 0, 384, [wn(k) for k in range(3)])
    zeros(T.Wm, 384, 512, [wn(3)])
    zeros(T.Wo, 0, 136, ["Wp", "Wj"])
    bfill(["Wv", "Wh"])
    sel(Wk(W_I), [[-1, 128]], A.not_equal, 1.0, 0, wn(W_I), zt)
    bfill(["B1", "B0"])
    fillS(T.six[:, 0:CV], 0.0, ["sixa"])
    fillS(T.six[:, CV:64], 6.0, ["sixb"])
    actS(Ip, Wk(W_I), F.Identity, [wn(W_I)], ["If0"])
    actS(Wk(W_NI), Wk(W_I), F.Identity, [wn(W_I)], [wn(W_NI)], scale=-1.0)
    iota(T.idt[:], [[64, 3], [0, 64]], 0, "idt")
    iota(T.Cb[:, 1344:1536], [[0, 3], [1, 64]], 0, "Cb7")
    fillS(T.Cb[:, 1536:1728], 1.0, ["Cb8"])
    actS(In, Wk(W_I), F.Identity, [wn(W_I)], ["If1"], scale=-1.0)
    actS(Wk(W_N128), Wk(W_I), F.Identity, [wn(W_I)], [wn(W_N128)], scale=-128.0)
    fillS(T.d0g[:], 0.0, ["n0"])
    lastw["n1"] = lastw["n2"] = lastw["n0"]
    fillS(T.d0m[:], 1.0, ["d0m"])
    block = [[-16, 8], [0, 16]]
    iota(T.Ct[:], [[16, 64]], CAP, "Ct")
    iota(T.col[:], [[1, 64]], 0, "col")
    iota(Wk(W_MK), [[0, 4], [1, 16], [0, 2]], 0, wn(W_MK))
    sel(Wk(W_ONE), block, A.is_ge, 1.0, -16, wn(W_ONE), zt)
    sel(Wk(W_NU), block, A.is_ge, -1.0, -16, wn(W_NU), zt)
    sel(Wk(W_ONE), block, A.is_ge, 0.0, 0, wn(W_ONE))
    sel(Wk(W_NU), [[-1, 128]], A.is_ge, 0.0, 0, wn(W_NU))
    iota(T.far[:], [[16, 64]], K, "far")
    sel(Wk(W_TRI), [[1, 128]], A.is_ge, 0.0, 0, wn(W_TRI), (Wk(W_ONE), wn(W_ONE)), -1)
    sel(Wk(W_NF), [[-1, 128]], A.not_equal, -512.0, 0, wn(W_NF), (Wk(W_NU), wn(W_NU)))
    sel(T.Wm[:, W_TRI * 128 + 15:(W_TRI + 1) * 128:16], [[0, 8]], A.is_gt, 0.0, 0, wn(W_TRI), None, 0)
    bfill(["B3", "B4", "B5"])

    def row(f, src, name):
        dma("Y", T.PT[f::16, Z:Z + V0], src, [name, "X0"], ["PT0_%d" % f])

    def spread(*fs):
        for f in fs:
            op("G", lambda: g.affine_select(T.Wl[:, f::16], T.Wl[:, f::16], [[-1, 16], [-16, 8]], A.not_equal, 1.0 if f in (4, 5) else -1.0, 0, 1),
               ["Wz%d" % r for r in range(8)], ["Wl%d" % f])

    def late(n):
        if n == 0:
            for f, c, name in ((6, 1152, "Cb6"), (7, 1344, "Cb7"), (11, 1536, "Cb8"), (8, 768, "Clh"), (9, 960, "Cll")):
                row(f, T.Cb[:, c:c + 192], name)
            for r in range(8):
                dma("Y", T.Wl[r::8, :], T.PA[4::8, 0:2048], arow, ["Wz%d" % r])
            dma("Y", T.wi[:], T.w[:], [], ["wi"])
            remote(T.qp0[:], T.X[:, V0:V0 + K], "q0", ["X1", "PT0_6"], "qp0")
            wfill([W_ID0, W_P, W_J])
            spread(2, 3, 4)
        if n == 1:
            actS(pm192, pm, F.Identity, ["pm"], ["pm192"], scale=192.0)
            actS(pmneg, pm, F.Identity, ["pm"], ["pmneg"], scale=-16384.0)
            actS(lastm1, lastrow, F.Identity, ["last"], ["lastm1"], bias=-1.0)
            actS(T.Cb[:, 1152:1344], T.idt[:], F.Identity, ["idt", "pm192"], ["Cb6"], bias=pm192)
            actS(Wk(W_MK), Wk(W_MK), F.Abs, [wn(W_MK), "pmneg"], [wn(W_MK)], bias=pmneg, scale=16384.0)
            actS(T.Cf[:], T.Ct[:], F.Identity, ["Ct", "pm"], ["Cf"], bias=pm)
            actS(T.c15[:], T.col[:], F.Identity, ["col", "last"], ["c15"], scale=lastrow)
            actS(T.zs[:], lastrow, F.Identity, ["last"], ["zs"], bias=-1.0, scale=17.0)
        if n == 2:
            actS(Wk(W_N4K), Wk(W_ONE), F.Identity, [wn(W_ONE)], [wn(W_N4K)], scale=-4096.0)
            fillS(T.dn[:], lastm1, ["dn", "lastm1"])
        if n == 3:
            copyV(wf, T.wi[:], ["wi"], ["wf"])
            fill(T.hb[:], 0.0, ["hb"])
            fill(T.M[:, 0:Z], 0.0, ["Mz"])
            actS(T.Bm[:, B_W * BW + 15:B_W * BW + 143:16], T.Bm[:, 15:143:16], F.Identity, ["B0", "wf"], ["B%d" % B_W], scale=wf)
        if n == 4:
            fillS(T.Wd[:, WD:WD + CAP], 0.0, ["Wd1"])

    def out_mm(t, h):
        def fn():
            for a in range(4 * h, 4 * h + 4):
                c = Z + V0 + K * t + 128 * a
                ins = pe.matmul(T.pw1[:, 0:128], T.Wo[:, 7 - a:135 - a], T.PT[:, c:c + 128], a == 0, a == 7)
            return ins
        op("P", fn, ["Wp", "Wj", "PT%d_%d" % (t + 1, h)], ["pw1a"])

    def out_store(t, q):
        actS(T.yo[:], T.pw1[:, 0:128], F.Identity, ["pw1a"], ["yo"])
        dma(q, T.ypar[:, K * t:K * t + K], T.yo[0:64, :], ["yo"], [])
        dma(q, T.yjump[:, K * t:K * t + K], T.yo[64:128, :], ["yo"], [])

    LV = 16 * CV

    for t in range(RO):
        o = V0 + K * t
        last = t == RO - 1
        rX = ["X%d" % k for k in range(t + 1)]
        rM = ["M0"] + ["M%d_%d" % (k, h) for k in range(1, t + 1) for h in range(16)]
        rP = prow + ["PT%d_%d" % (k, h) for k in range(1, t + 1) for h in (0, 1)]
        rq = ["X%d" % (t + 1)]
        if t > 0:
            rX = rX + ["X%db" % k for k in range(2, t + 1)]
            rq = rq + ["X%db" % (t + 1)]
        ask = T.X[:, o:o + K]
        offs = [T.ou0, T.ou1, T.ou2, T.ou3]
        cx = [T.cx0, T.cx1, T.cx2]
        pg = [T.pg0, T.pg1]
        nn = ["n0", "n1", "n2"]

        def uf(s):
            return T.uf[:, 64 * s:64 * s + 64]

        def nap(s):
            return T.d0g[:, 3 - s::4]

        def quarters(name, a, b):
            return ["%s%d" % (name, k) for k in range(a // 4, b // 4)]

        def wins(s):
            a = o - K if (s == 0 and t > 0) else 0
            return T.X[:, a:o], T.M[:, Z + a:Z + o], T.PT[:, Z + a:Z + o]

        def pointers(s, gather=gS, a=0, b=64):
            win, r = (T.PA[:], arow) if t == 0 else (wins(s)[2], rP)
            gather(pg[s % 2][:, 16 * a:16 * b], win, offs[s][:, a:b], r + ["ou%d" % s], quarters("pg%d_" % (s % 2), a, b))

        def m_test(s):
            for a, b in ((0, 48), (48, 64)):
                gT(T.cm[:, 16 * a:16 * b], wins(s)[1], offs[s][:, a:b], T.X[:, o + 16 * a:o + 16 * b], A.is_ge, rM + rq + ["ou%d" % s], ["cm%d" % a])

        def x_vec(s, a, b):
            gT(cx[s % 3][:, 16 * a:16 * b], wins(s)[0], offs[s][:, a:b], T.X[:, o + 16 * a:o + 16 * b], A.is_ge, rX + rq + ["ou%d" % s],
               quarters("cx%d_" % (s % 3), a, b))

        def x_get(s):
            gS(T.gy[:], wins(s)[0], offs[s][:, CV:64], rX + ["ou%d" % s], ["gy"])

        def x_open(h=0):
            mw(T.pw0[:, 512 * h:512 * h + K - LV], W_NI, T.X[:, o + LV:o + K], True, False, rq, ["pw0" + "ab"[h]])

        def x_diff(h=0):
            mw(T.pw0[:, 512 * h:512 * h + K - LV], W_I, T.gy[:], False, True, ["gy"], ["pw0" + "ab"[h]])

        def x_sign(s, h=0):
            actS(cx[s % 3][:, LV:K], T.pw0[:, 512 * h:512 * h + K - LV], F.Sign, ["pw0" + "ab"[h]], quarters("cx%d_" % (s % 3), CV, 64), bias=0.5)

        def votes_x(s, bank, bn, start=True, c=0):
            mw(bank[:, c:c + 64], W_I, T.six[:], start, False, ["sixa", "sixb"], [bn])
            extract(bank[:, c:c + 64], B_ONE, cx[s % 3], quarters("cx%d_" % (s % 3), 0, 64), [bn], start=False)

        def stays(s, bank=T.pd, bn="pd", c=0):
            actS(T.na[:], bank[:, c:c + 64], F.Relu, [bn], ["na"], bias=-9.0)
            actS(nap(s), T.na[:], F.Relu, ["na"], [nn[s]], bias=1.0, scale=-1.0)

        def entry(a):
            if a < 3:
                mm(T.pw1[:, 512 + a:768:4], In, uf(2 - a), True, False, ["If1", "uf%d" % (2 - a)], ["pw1b"])
            mm(T.pw1[:, 512 + a:768:4], Ip, uf(3 - a), a == 3, True, ["If0", "uf%d" % (3 - a)], ["pw1b"])

        def turn_back(out, bn):
            mm(out, T.tu[:, 1:17, :], T.If[:, 0:128:2], False, False, ["tu", "If0"], [bn])
            mm(out, T.tu[:, 0:16, :], T.If[:, 1:128:2], False, True, ["tu", "If0"], [bn])

        def choose_p():
            scan(T.sp[:], T.d0g[:], T.pw1[:, 512:768], A.mult, A.add, nn + ["pw1b"], ["sp"])
            if t == 0:
                fill(T.d0m[:, 0::32], 0.0, ["d0m"])
            copyV(T.op[:], T.sp[:, 3::4], ["sp"], ["op"])
            if t == 0:
                fill(T.cnt[:], 0.0, ["cnt"])

        def turns(s):
            turn(T.pa, Wv, T.cm, ["cm0", "Wv"], ["pa"], 0, 96)
            turn(T.pa, Wv, T.cm, ["cm48", "Wv"], ["pa"], 96, 128)
            turn(T.pb, Wh, pg[s % 2], quarters("pg%d_" % (s % 2), 0, 64) + ["Wh"], ["pb"], 0, 128)

        def sign():
            actS(T.sg[:], T.pa[:, 0:64], F.Sign, ["pa"], ["sg"], bias=-9.5)

        def middle(s, k=B_SH, out=T.pc[:, 0:64], bn="pc"):
            extract(out, k, pg[s % 2], quarters("pg%d_" % (s % 2), 0, 64), [bn], stop=False)

        def signed():
            tt(T.tu[:, 1:17:2, :], T.pb[:, 0:64], T.sg[:], A.mult, ["pb", "sg"], ["tu"])

        def advance(s):
            copyV(offs[s + 1][:], T.pc[:, 0:64], ["pc"], ["ou%d" % (s + 1)])

        def open_choice():
            actS(uf(2), T.pc[:, 0:64], F.Identity, ["pc"], ["uf2"])

        for s in range(3):
            if t == 0 and s == 0:
                m_test(0)
                pointers(0, gS, 16, 64)
                pointers(0, gV, 0, 16)
                turns(0)
                sign()
                split(384, 192, 768, ["Ci2"], "Cl", "h")
                fill(T.tu[:], 0.0, ["tu"])
                fill(T.one64[:], 1.0, ["one64"])
                middle(0)
                signed()
                split(384, 192, 768, ["Ci2"], "Cl", "l")
                copyV(uf(0), T.u0i[:], ["u0i"], ["uf0"])
                fill(T.Sc[:, 0:8], 0.0, ["Scz"])
                late(1)
                turn_back(T.pc[:, 0:64], "pc")
                late(0)
                advance(0)
            elif t == 0 and s == 1:
                pointers(1)
                m_test(1)
                x_open()
                x_open(1)
                x_get(0)
                turns(1)
                x_diff()
                x_vec(0, 0, 40)
                sign()
                x_get(1)
                x_sign(0)
                middle(1)
                signed()
                turn_back(T.pc[:, 0:64], "pc")
                x_diff(1)
                x_sign(1, 1)
                x_vec(0, 40, CV)
                x_vec(1, 0, 16)
                advance(1)
            elif last and s == 2:
                dma("Y", T.ge[:], ask, rq, ["ge0", "ge1"])
                x_get(2)
                open_choice()
                pointers(2)
                m_test(2)
                votes_x(1, T.pd, "pd")
                x_open()
                x_diff()
                for a in (3, 2, 1):
                    entry(a)
                turns(2)
                x_vec(2, 0, CV)
                x_sign(2)
                sign()
                stays(1)
                middle(2, B_SI, T.pw1[:, 512:768:4], "pw1b")
                signed()
                votes_x(2, T.pw0, "pw0b", c=512)
                turn_back(T.pw1[:, 512:768:4], "pw1b")
                ts(nap(2), T.pw0[:, 512:576], 9.5, None, (A.is_lt,), ["pw0b"], ["n2"])
            else:
                gaps = [[(s, 0, C1)], [(s, C1, CV)]]
                if t == 0:
                    gaps = [[(1, 16, CV), (2, 0, 8)], [(2, 8, CV)]]
                    copyV(uf(1), offs[1][:], ["ou1"], ["uf1"])
                pointers(s)
                m_test(s)
                if t == 1 and s == 0:
                    remote(T.qp1[:], ask, "q1", rq, "qp1")
                if s > 0:
                    votes_x(s - 1 - (t == 0), T.pd, "pd")
                if s == 0:
                    out_mm(t - 1, 0)
                    out_mm(t - 1, 1)
                if s == 2:
                    entry(3)
                    entry(2)
                x_open()
                turns(s)
                x_get(s)
                if s == 2:
                    x_diff()
                for x in gaps[0]:
                    x_vec(*x)
                sign()
                if s > 0:
                    stays(s - 1 - (t == 0))
                if s == 0:
                    out_store(t - 1, "Y")
                    if t == 1:
                        late(4)
                middle(s)
                if s < 2:
                    x_diff()
                signed()
                if s == 2:
                    copyV(uf(2), offs[2][:], ["ou2"], ["uf2"])
                turn_back(T.pc[:, 0:64], "pc")
                if s == 2:
                    entry(1)
                x_sign(s)
                if t == 0:
                    late(2)
                if t == 0:
                    votes_x(1, T.pw0, "pw0b", c=512)
                for x in gaps[1]:
                    x_vec(*x)
                if s == 0:
                    ts(uf(0), T.h1[:], float(o - K), None, (A.add,), ["h1"], ["uf0"])
                if s == 1:
                    copyV(uf(1), offs[1][:], ["ou1"], ["uf1"])
                advance(s)

        wx, wm, wp = wins(2)
        wz_m = T.M[:, 0:Z + o]
        pf = T.sp[:, 3::4]

        def half(h):
            return slice(512 * h, 512 * h + 512)

        def part(gather, name, win, off, a, b, r, c0=0):
            gather(T[name][:, 16 * a:16 * b], win, off[:, c0 + a:c0 + b], r, quarters(name, a, b))

        def whole(name):
            return quarters(name, 0, 64)

        def halfof(name, h):
            return quarters(name, 32 * h, 32 * h + 32)

        if not last:
            x_get(3)
            actS(uf(3), T.pc[:, 0:64], F.Identity, ["pc"], ["uf3"])
            if t == 0:
                x_vec(3, 0, 20)
                ts(nap(1), T.pw0[:, 512:576], 9.5, None, (A.is_lt,), ["pw0b"], ["n1"])
            x_vec(3, 20 * (t == 0), CV)
            votes_x(2, T.pd, "pd")
            x_open()
            x_diff()
            entry(0)
            stays(2)
            x_sign(3)
            mm(T.pc[:, 1:128:2], Ip, T.Cf[:], True, True, ["If0", "Cf"], ["pc"])
            mw(T.pb[:, 0:128], W_NI, Wk(W_MK), True, False, [wn(W_MK)], ["pb"])
            mw(T.pb[:, 1:128:2], W_I, T.far[:], False, False, ["far"], ["pb"])

            def query(bn, h):
                mw(T[bn][:, half(h)], W_I, T.X[:, o + 512 * h:o + 512 * h + 512], True, False, rq, [bn + "ab"[h]])
            query("pw1", 0)
            for s in range(3):
                mw(T.pa[:, 0:64], W_N128, nap(s), s == 0, False, [nn[s]], ["pa"])
            choose_p()
            votes_x(3, T.pa, "pa", start=False)
            query("pw0", 0)
            query("pw0", 1)
            part(gS, "pgp", wp, T.op, 20, 64, rP + ["op"])
            part(gV, "pgp", wp, T.op, 0, 8, rP + ["op"])
            ts(T.fb[:], T.pa[:, 0:64], 9.5 - 384.0, None, (A.is_lt,), ["pa"], ["fb"])
            if t == 0:
                fill(T.Wd[:, 0:CAP], 0.0, ["Wd0"])
            scan(T.Sc[:, 8:72], T.one64[:], T.fb[:], A.mult, A.add, ["one64", "fb"], ["Sc"])
            incl, excl = T.Sc[:, 8:72], T.Sc[:, 7:71]
            mw(T.pa[:, 0:64], W_I, T.c15[:], True, False, ["c15"], ["pa"])
            mw(T.pa[:, 0:64], W_TRI, T.fb[:], False, True, ["fb"], ["pa"])
            mw(T.pb[:, 1:128:2], W_N4K, T.fb[:], False, False, ["fb"], ["pb"])
            mw(T.pb[:, 0:128:2], W_ONE, excl, False, False, ["Sc", "Scz"], ["pb"])
            mw(T.pb[:, 1:128:2], W_ONE, excl, False, True, ["Sc", "Scz"], ["pb"])
            mw(T.pc[:, 256:257], W_ONE, T.Sc[:, 71:72], True, True, ["Sc"], ["pc"])
            part(gV, "pgp", wp, T.op, 8, 20, rP + ["op"])
            copyV(T.Rk[:], T.pa[:, 0:64], ["pa"], ["Rk"])
            scan(T.sst[:], T.d0m[:], T.pb[:, 0:128], A.mult, A.max, ["d0m", "pb"], ["sst"])
            ts(T.cnt[:, 15:16], T.pc[:, 256:257], float(CAP), 192.0, (A.min, A.subtract), ["pc"], ["cnt"])
            remote(T["got%d" % t][:], T.cnt[:], "h%d" % t, ["cnt"], "got%d" % t)
            if t == 0:
                spread(5, 8, 9)
            copyV(T.ost[:], T.sst[:, 31::32], ["sst"], ["ost"])
            mm(T.pd[:, 0:64], Ip, pf, True, True, ["If0", "sp"], ["pd"])
            query("pw1", 1)
            extract(T.pd[:, 64:128], B_J, T.pgp, whole("pgp"), ["pd"])
            part(gS, "gx", wx, T.op, 0, GX, rX + ["op"])
            op("V", lambda: vec.tensor_copy(T.Wd[:, WD * t:WD * t + WD].indirect(T.ost[:]), T.Rk[:]), ["Rk", "ost"], ["Wd%d" % t])
            copyV(T.oj[:], T.pd[:, 64:128], ["pd"], ["oj"])
            scan(T.Zr[:], T.Wd[:, WD * t:WD * t + CAP], T.dn[:], A.max, A.add, ["Wd%d" % t, "dn"], ["Zr"])
            ts(T.Zc[:], T.Zr[:], T.zs[:], 0.0, (A.mult, A.max), ["Zr", "zs"], ["Zc"])
            mm(T.pc[:, 0:128:2], In, T.Cf[:], True, False, ["If1", "Cf"], ["pc"])
            mw(T.pc[:, 0:128:2], W_NU, T.fb[:], False, False, ["fb"], ["pc"])
            mw(T.pc[:, 0:128:2], W_ONE, incl, False, True, ["Sc"], ["pc"])
            mw(T.pc[:, 128:192], W_NF, T.fb[:], True, False, ["fb"], ["pc"])
            mw(T.pc[:, 128:192], W_ONE, incl, False, True, ["Sc"], ["pc"])

            def sums(bn, h):
                mw(T[bn][:, half(h)], W_I, T.gx[:, half(h)], False, bn == "pw0", halfof("gx", h), [bn + "ab"[h]])

            def wraps(h):
                actS(T.ge[:, half(h)], T.pw0[:, half(h)], F.Sign, ["pw0" + "ab"[h]], ["ge%d" % h], bias=t - 255.5)

            def kept(h):
                mw(T.pw1[:, half(h)], W_N128, T.ge[:, half(h)], False, True, ["ge%d" % h], ["pw1" + "ab"[h]])
                actS(T.tab[:, CAP + 512 * h:CAP + 512 * h + 512], T.pw1[:, half(h)], F.Identity, ["pw1" + "ab"[h]], ["tabc%d" % h], bias=t - 128.0)

            def born(h):
                mw(T.pw0[:, half(h)], W_ID0 + t, T.PT[:, Z + 512 * h:Z + 512 * h + 512], True, False, rP, ["pw0" + "ab"[h]])
                mw(T.pw0[:, half(h)], W_P, T.pgp[:, half(h)], False, False, halfof("pgp", h), ["pw0" + "ab"[h]])
                mw(T.pw0[:, half(h)], W_J, T.pgj[:, half(h)], False, False, halfof("pgj", h), ["pw0" + "ab"[h]])

                def fn():
                    for i in range(16):
                        ins = pe.matmul(T.pw0[:, 512 * h + i:512 * h + 512:16], T.Wl[:, 128 * i:128 * i + 128], T.ad[:, 32 * h:32 * h + 32],
                                        False, i == 15)
                    return ins
                op("P", fn, ["ad"] + ["Wl%d" % f for f in (2, 3, 4, 5, 8, 9)], ["pw0" + "ab"[h]])

            def bounds(a, b):
                gT(T.M[:, Z + o + 16 * a:Z + o + 16 * b], wz_m, T.opj[:, 64 + a:64 + b], T.tm[:, 16 * a:16 * b], A.max,
                   rM + ["Mz", "opj"] + quarters("tm", a, b), quarters("M%d_" % (t + 1), a, b))

            def rows(h):
                actS(T.PT[:, Z + o + 512 * h:Z + o + 512 * h + 512], T.pw0[:, half(h)], F.Relu, ["pw0" + "ab"[h]], ["PT%d_%d" % (t + 1, h)])
            extract(T.pa[:, 0:64], B_LP, T.pgp, whole("pgp"), ["pa"], stop=False)
            part(gS, "pgj", wp, T.oj, PJ, 64, rP + ["oj"])
            part(gV, "pgj", wp, T.oj, 0, PJ, rP + ["oj"])
            part(gS, "gx", wx, T.op, GX, 64, rX + ["op"])
            sums("pw0", 0)
            extract(T.pb[:, 0:24], B_ONE, T.Zc, ["Zc"], ["pb"], n=CAP)
            copyV(T.inv[:], T.pb[:, 0:24], ["pb"], ["inv"])
            remote(T["who%d" % t][:], T.inv[:], "d%d" % t, ["inv"], "who%d" % t)
            extract(T.pa[:, 0:64], B_LN, T.pgj, whole("pgj"), ["pa"], start=False)
            sums("pw0", 1)
            sums("pw1", 0)
            wraps(0)
            wraps(1)
            if t == 0:
                late(3)
                bfill(["Wp", "Wj", "B2", "B6"])
                wfill([W_ID1])
            kept(0)
            sums("pw1", 1)
            kept(1)
            ts(T.ad[:], T.pa[:, 0:64], 0.0, BIG, (A.not_equal, A.mult), ["pa"], ["ad"])
            born(0)
            born(1)
            ts(T.hb[:, 1::2], T.pc[:, 128:192], 511.0 - 192.0, T["got%d" % t][:, 15:16], (A.add, A.is_lt), ["pc", "got%d" % t], ["hb"])
            for h in (0, 1):
                tt(T.yy[:, 64 * h:64 * h + 64], T.pd[:, 64 * h:64 * h + 64], T.ad[:], A.subtract, ["pd", "ad"], ["yy" + "ab"[h]])
            scan(T.sidx[:], T.hb[:], T.pc[:, 0:128], A.mult, A.add, ["hb", "pc"], ["sidx"])
            ts(T.opj[:], T.yy[:], float(Z), None, (A.add,), ["yya", "yyb"], ["opj"])
            copyV(T.oidx[:], T.sidx[:, 1::2], ["sidx"], ["oidx"])
            for h in (0, 1):
                gT(T.tm[:, half(h)], wz_m, T.opj[:, 32 * h:32 * h + 32], T.X[:, o + 512 * h:o + 512 * h + 512], A.max,
                   rM + rq + ["Mz", "opj"], halfof("tm", h))
            gS(T.tab[:, 0:CAP], T["qp%d" % t][:], T["who%d" % t][:], ["qp%d" % t, "who%d" % t], ["taba"])
            bounds(0, 16)
            rt = ["taba", "tabc0", "tabc1", "oidx"]
            gS(T.X[:, o + K + 16 * CF:o + 2 * K], T.tab[:], T.oidx[:, CF:64], rt, ["X%db" % (t + 2)])
            gV(T.X[:, o + K:o + K + 16 * CF], T.tab[:], T.oidx[:, 0:CF], rt, ["X%d" % (t + 2)])
            bounds(16, 52)
            extract(T.pb[:, 0:64], B_W, T.X, ["X%d" % (t + 2), "X%db" % (t + 2)], ["pb"], c0=o + K)
            rows(0)
            rows(1)
            copyV(T.h0[:], T.pb[:, 0:64], ["pb"], ["h0"])
            bounds(52, 60)
            ts(T.h1[:], T.h0[:], K - 1, None, (A.bitwise_and,), ["h0"], ["h1"])
            bounds(60, 64)
            copyV(T.ou0[:], T.h1[:], ["h1"], ["ou0"])
            dma("Y", T.ym[:, K * t:K * t + K], T.M[:, Z + o:Z + o + K], whole("M%d_" % (t + 1)), [])
        else:
            def across(out, k, src, name, bn, start, stop):
                def fn():
                    for a in range(16):
                        ins = pe.matmul(out, Bi(k, a), src[:, 64 * a:64 * a + 64], start and a == 0, stop and a == 15)
                    return ins
                op("P", fn, whole(name) + ["B%d" % k], [bn])

            def with_p(a, b):
                gT(T.tm[:, 16 * a:16 * b], wm, T.op[:, a:b], T.X[:, o + 16 * a:o + 16 * b], A.max, rM + rq + ["op"], quarters("tm", a, b))

            def with_j(a, b):
                gT(T.X[:, o + K + 16 * a:o + K + 16 * b], wm, T.oj[:, a:b], T.tm[:, 16 * a:16 * b], A.max, rM + ["oj"] + quarters("tm", a, b),
                   quarters("both", a, b))
            choose_p()
            part(gS, "pgp", wp, T.op, 32, 64, rP + ["op"])
            part(gV, "pgp", wp, T.op, 0, 32, rP + ["op"])
            extract(T.pd[:, 0:64], B_J, T.pgp, whole("pgp"), ["pd"])
            part(gS, "tm", wm, T.op, 0, 16, rM + ["op"])
            part(gS, "tm", wm, T.op, 52, 64, rM + ["op"])
            with_p(16, 52)
            copyV(T.oj[:], T.pd[:, 0:64], ["pd"], ["oj"])
            across(T.pb[:, 0:64], B_ID, T.pgp, "pgp", "pb", True, True)
            extract(T.pa[:, 0:64], B_LP, T.pgp, whole("pgp"), ["pa"], stop=False)
            across(T.pc[:, 0:64], B_LP, T.pgp, "pgp", "pc", True, False)
            part(gS, "pgj", wp, T.oj, 16, 64, rP + ["oj"])
            part(gV, "pgj", wp, T.oj, 0, 16, rP + ["oj"])
            copyV(T.yo[:, 0:64], T.pb[:, 0:64], ["pb"], ["yo"])
            with_j(0, 64)
            dma("Y", T.ypar[:, K * t:K * t + K], T.yo[:, 0:64], ["yo"], [])
            mm(T.pb[:, 0:64], In, T.yo[:, 0:64], True, False, ["If1", "yo"], ["pb"])
            extract(T.pa[:, 0:64], B_LN, T.pgj, whole("pgj"), ["pa"], start=False)
            across(T.pc[:, 0:64], B_LN, T.pgj, "pgj", "pc", False, True)
            across(T.pb[:, 0:64], B_J, T.pgj, "pgj", "pb", False, True)
            ts(T.ad[:], T.pa[:, 0:64], 0.0, float(K), (A.is_equal, A.mult), ["pa"], ["ad"])
            tt(T.yy[:, 0:64], T.ad[:], T.Cf[:], A.add, ["ad", "Cf"], ["yya"])
            ts(T.oidx[:], T.yy[:, 0:64], float(CAP), None, (A.subtract,), ["yya"], ["oidx"])
            ts(T.na[:], T.pc[:, 0:64], 0.0, None, (A.is_equal,), ["pc"], ["na"])
            rt = rq + whole("both") + ["oidx"]

            def with_q(a, b):
                gT(T.gx[:, 16 * a:16 * b], T.X[:, o:o + 2 * K], T.oidx[:, a:b], T.ge[:, 16 * a:16 * b], A.max, rt + ["ge0"], quarters("gx", a, b))
            part(gS, "gx", T.X[:, o:o + 2 * K], T.oidx, 16, 32, rt)
            with_q(0, 16)
            dma("Y", T.ym[:, K * t:K * t + 512], T.gx[:, half(0)], halfof("gx", 0), [])
            part(gS, "gx", T.X[:, o:o + 2 * K], T.oidx, 32, 52, rt)
            tt(T.yy[:, 64:128], T.pb[:, 0:64], T.na[:], A.mult, ["pb", "na"], ["yyb"])
            with_q(52, 64)
            dma("S", T.ym[:, K * t + 512:K * t + K], T.gx[:, half(1)], halfof("gx", 1), [])
            tt(T.yo[:, 64:128], T.yy[:, 64:128], T.yo[:, 0:64], A.add, ["yyb", "yo"], ["yoj"])
            dma("Y", T.yjump[:, K * t:K * t + K], T.yo[:, 64:128], ["yoj"], [])

    rest = [s for s in total if waited.get(s, 0) < total[s]]
    for s in sorted(rest, key=lambda s: s in ("sV", "sS", "sP")):
        Q[ending.get(s, "G")].wait_ge(T.sem[s], total[s])
